import numpy as np
import ml_dtypes


def mxq(x, axis, fmt="e4m3"):
    dtype, down = {"e4m3": (ml_dtypes.float8_e4m3fn, 7), "e5m2": (ml_dtypes.float8_e5m2, 14)}[fmt]
    v = np.moveaxis(np.asarray(x, np.float32).astype(ml_dtypes.bfloat16).astype(np.float64), axis, -1)
    blocks = v.reshape(v.shape[:-1] + (-1, 32))
    amax = np.abs(blocks).max(-1, keepdims=True)
    byte = np.maximum(np.where(amax > 0, np.frexp(amax)[1] - 1 + 127, 0) - down, 1)
    scale = np.exp2(byte - 127.0)
    codes = (blocks / scale).astype(np.float32).astype(dtype).astype(np.float64)
    return np.moveaxis((codes * scale).reshape(v.shape), -1, axis)


WIDE = False


def mx_kscale(k):
    if not WIDE:
        return np.ones(k)
    levels = np.array([10, -10, 5, -5, 0])
    if k % 512:
        return np.exp2(np.random.permutation(np.resize(levels, k // 32))).repeat(32)
    a = np.empty((k // 512, 16))
    for p in range(k // 512):
        a[p, :8] = np.random.permutation(np.resize(levels, 8))
        for g in range(8):
            far = levels[np.abs(levels - a[p, g]) >= 10]
            a[p, g + 8] = far[np.random.randint(len(far))]
    return np.exp2(a.ravel()).repeat(32)


def f64(x):
    return np.asarray(x).astype(np.float64)


def striped(idx):
    return np.tile(idx.reshape(-1, 16).T, (8, 1)).astype(np.uint16)


def unstriped(offs):
    return offs[:16].T.reshape(-1).astype(np.int64)


E2M1 = np.array([0.0, 0.5, 1.0, 1.5, 2.0, 3.0, 4.0, 6.0, -0.0, -0.5, -1.0, -1.5, -2.0, -3.0, -4.0, -6.0])


def pack_weight(w, fmt):
    k, n = w.shape
    w = f64(np.asarray(w, np.float32).astype(ml_dtypes.bfloat16)).reshape(k // 32, 32, n)
    amax = np.abs(w).max(1)
    if fmt == "e4m3":
        byte = np.frexp(amax)[1] - 1 + 127 - 7
    else:
        mant, ex = np.frexp(amax / 6.0)
        byte = np.where(mant > 0.5, ex, ex - 1) + 127
    byte = np.clip(np.where(amax > 0, byte, 1), 1, 254)
    scaled = (w * np.exp2(127.0 - byte)[:, None, :]).reshape(k, n).astype(np.float32)
    by_word = np.ascontiguousarray(scaled.reshape(k // 512, 128, 4, n).transpose(0, 1, 3, 2))
    if fmt == "e4m3":
        words = by_word.astype(ml_dtypes.float8_e4m3fn).view(np.uint8)
    else:
        c = by_word.astype(ml_dtypes.float4_e2m1fn).view(np.uint8) & 0xF
        words = (c[..., 0::2] | (c[..., 1::2] << 4)).reshape(k // 512, 128, 2 * n)
    return np.ascontiguousarray(words), np.ascontiguousarray(byte.astype(np.uint8).reshape(k // 512, 16, n))


def unpack_weight(words, scales, fmt):
    g, _, n = scales.shape
    words = np.ascontiguousarray(words).reshape(g, 128, n, -1)
    if fmt == "e4m3":
        vals = words.view(ml_dtypes.float8_e4m3fn).astype(np.float64)
    else:
        nib = np.empty((g, 128, n, 4), np.uint8)
        nib[..., 0::2] = words & 0xF
        nib[..., 1::2] = words >> 4
        vals = E2M1[nib]
    vals = vals * np.repeat(np.exp2(scales.astype(np.float64) - 127.0), 8, axis=1)[..., None]
    return vals.transpose(0, 1, 3, 2).reshape(g * 512, n)


def gelu(v):
    return 0.5 * v * (1.0 + np.tanh(np.sqrt(2.0 / np.pi) * (v + 0.044715 * v**3)))


K, H, N, T, S, P = 1024, 1024, 768, 4096, 1024, 512

def setup_inputs():
    n = np.random.standard_normal
    s = mx_kscale(K)[:, None]
    u = mx_kscale(H)[:, None]
    tab_words, tab_scales = pack_weight(n((K, T)) * s, "e4m3")
    wm_words, wm_scales = pack_weight(n((H, N)) / np.sqrt(H) / u, "e2m1")
    return {
        "tab_words": tab_words, "tab_scales": tab_scales,
        "offs": striped(np.random.permutation(T)[:S]),
        "w1": (n((K, H)) / np.sqrt(K) / s * u.T).astype(np.float32),
        "b1": (0.4 * n(H) * u[:, 0]).astype(np.float32),
        "pos1": striped(np.random.permutation(S)[:P]),
        "pos2": striped(np.random.permutation(S)[:P]),
        "wm_words": wm_words, "wm_scales": wm_scales,
        "ws": (n((H, N)) / np.sqrt(H) / u).astype(np.float32),
        "bs": (0.5 * n(N)).astype(np.float32),
    }

def reference(tab_words, tab_scales, offs, w1, b1, pos1, pos2, wm_words, wm_scales, ws, bs):
    v = unpack_weight(tab_words, tab_scales, "e4m3")[:, unstriped(offs)]
    w1q = mxq(f64(w1), 0, "e4m3")
    h = (w1q.T @ v) + f64(b1)[:, None]
    a = h[:, unstriped(pos1)]
    b = h[:, unstriped(pos2)]
    zq = mxq(np.maximum(a, b), 0, "e4m3")
    wm = unpack_weight(wm_words, wm_scales, "e2m1")
    wsq = mxq(f64(ws), 0, "e4m3")
    m = wm.T @ zq
    g = (wsq.T @ zq) + f64(bs)[:, None]
    return m * (1.0 / (1.0 + np.exp(-g)))

@@ -1,0 +1,308 @@
+from contextlib import ExitStack
+
+import concourse.mybir as mybir
+
+K, H, N, T, S, PAIRS = 1024, 1024, 768, 4096, 1024, 512
+FLOPS = 2 * K * H * S + 2 * 2 * H * N * PAIRS
+
+F32 = mybir.dt.float32
+BF16 = mybir.dt.bfloat16
+I32 = mybir.dt.int32
+U32 = mybir.dt.uint32
+U16 = mybir.dt.uint16
+U8 = mybir.dt.uint8
+FP8X4 = mybir.dt.float8_e4m3fn_x4
+FP4X4 = mybir.dt.float4_e2m1fn_x4
+ALU = mybir.AluOpType
+ACT = mybir.ActivationFunctionType
+
+P = 128
+PACK = 4
+K_PASS = P * PACK
+BANK = 512
+HALF = PAIRS // 2
+
+
+def tile_list_grasp_pair_wrench_kernel(
+    tc, tab_words, tab_scales, offs, w1, b1, pos1, pos2, wm_words, wm_scales, ws, bs, out
+):
+    nc = tc.nc
+    with ExitStack() as ctx:
+        lists = ctx.enter_context(tc.tile_pool(name="lists", bufs=1))
+        keep = ctx.enter_context(tc.tile_pool(name="keep", bufs=1))
+        psum = ctx.enter_context(tc.psum_pool(name="psum", bufs=1))
+
+        def sbuf(name, shape, dtype, tag="", bufs=1):
+            return keep.tile(shape, dtype, name=name, tag=tag or name, bufs=bufs, align_bytes=64)
+
+        def bank(k, shape, name):
+            return psum.tile(shape, F32, name=name, tag="bank%d" % k)
+
+        offs_sb = lists.tile([P, S // 16], U16, name="offs_sb")
+        pos1_sb = lists.tile([P, PAIRS // 16], U16, name="pos1_sb")
+        pos2_sb = lists.tile([P, PAIRS // 16], U16, name="pos2_sb")
+
+        scale_window = sbuf("scale_window", [P, T // 4], I32)
+        wm_scale = sbuf("wm_scale", [P, 2, N // 4], I32)
+        nc.vector.memset(scale_window[:], 0)
+        nc.vector.memset(wm_scale[:], 0)
+        warm = sbuf("warm", [P, 2], F32)
+        nc.vector.memset(warm[:, 0:1], 0.0)
+        nc.scalar.activation(warm[:, 1:2], warm[:, 0:1], ACT.Sigmoid)
+        nc.sync.dma_start(offs_sb[:], offs)
+        word_window = []
+        for a in range(2):
+            win = sbuf("word_window%d" % a, [P, T], I32)
+            nc.sync.dma_start(out=win[:], in_=tab_words[a].rearrange("p t i -> p (t i)").bitcast(I32))
+            word_window.append(win)
+            if a == 0:
+                for q in range(2):
+                    nc.sync.dma_start(
+                        out=scale_window[32 * q : 32 * q + 8, :],
+                        in_=tab_scales[:, 4 * q : 4 * q + 4, :].bitcast(I32),
+                    )
+                for q in range(2, 4):
+                    for c in range(2):
+                        nc.sync.dma_start(
+                            out=scale_window[32 * q + 4 * c : 32 * q + 4 * c + 4, :],
+                            in_=tab_scales[c, 4 * q : 4 * q + 4, :].bitcast(I32),
+                        )
+
+        w1_raw = {}
+
+        def load_w1(a, b):
+            raw = sbuf("w1_raw%d%d" % (a, b), [P, PACK, K_PASS], F32)
+            nc.sync.dma_start(
+                out=raw[:],
+                in_=w1[K_PASS * a : K_PASS * (a + 1), K_PASS * b : K_PASS * (b + 1)].rearrange(
+                    "(p j) c -> p j c", j=PACK
+                ),
+            )
+            w1_raw[a, b] = raw
+
+        load_w1(0, 0)
+        load_w1(1, 0)
+        nc.sync.dma_start(pos1_sb[:], pos1)
+        nc.sync.dma_start(pos2_sb[:], pos2)
+        b1_sb = sbuf("b1_sb", [P, 2, PACK], F32)
+        nc.sync.dma_start(out=b1_sb[:], in_=b1.rearrange("(b p t) -> p b t", b=2, t=PACK))
+        load_w1(0, 1)
+        load_w1(1, 1)
+        ws_raw = []
+        for a in range(2):
+            raw = sbuf("ws_raw%d" % a, [P, PACK, N], F32)
+            nc.sync.dma_start(
+                out=raw[:], in_=ws[K_PASS * a : K_PASS * (a + 1), :].rearrange("(p j) n -> p j n", j=PACK)
+            )
+            ws_raw.append(raw)
+        wm_sb = sbuf("wm_sb", [P, 2, 2 * N], U8)
+        nc.sync.dma_start(out=wm_sb[:].bitcast(I32), in_=wm_words.bitcast(I32).rearrange("a p w -> p a w"))
+        for q in range(4):
+            nc.sync.dma_start(
+                out=wm_scale[32 * q : 32 * q + 4, :, :],
+                in_=wm_scales[:, 4 * q : 4 * q + 4, :].bitcast(I32).rearrange("a r w -> r a w"),
+            )
+        bs_sb = sbuf("bs_sb", [P, N // P], F32)
+        with nc.allow_non_contiguous_dma(reason="one bias value for each partition and output tile"):
+            nc.sync.dma_start(out=bs_sb[:], in_=bs.rearrange("(c p) -> p c", p=P))
+
+        v_scale = sbuf("v_scale", [P, S], U8)
+        v_words = []
+        for a in range(2):
+            g = sbuf("v_words%d" % a, [P, S], U32)
+            nc.vector.tensor_copy(g[:], word_window[a][:].bitcast(U32).indirect(offs_sb[:]))
+            v_words.append(g)
+            if a == 0:
+                nc.vector.tensor_copy(v_scale[:], scale_window[:].bitcast(U8).indirect(offs_sb[:]))
+
+        w1_bf, w1_code, w1_scale = {}, {}, {}
+
+        def round_w1(a, b, u, on_vector):
+            if (a, b) not in w1_bf:
+                w1_bf[a, b] = sbuf("w1_bf%d%d" % (a, b), [P, PACK, P, PACK], BF16)
+            dst = w1_bf[a, b][:, 2 * u : 2 * u + 2, :, :].rearrange("p t m j -> p m j t")
+            src = w1_raw[a, b][:].rearrange("p j (m t) -> p m j t", t=PACK)[:, :, :, 2 * u : 2 * u + 2]
+            if on_vector:
+                nc.vector.tensor_copy(dst, src)
+            else:
+                nc.scalar.copy(dst, src)
+
+        def quantize_w1(a, b, t0, t1):
+            if (a, b) not in w1_code:
+                w1_code[a, b] = sbuf("w1_code%d%d" % (a, b), [P, K_PASS], U32)
+                w1_scale[a, b] = sbuf("w1_scale%d%d" % (a, b), [P, K_PASS], U8)
+            cols = slice(P * t0, P * t1)
+            nc.vector.quantize_mx(
+                out=w1_code[a, b][:, cols].bitcast(FP8X4),
+                scales=w1_scale[a, b][:, cols],
+                in_=w1_bf[a, b][:, t0:t1, :, :].rearrange("p t m j -> p (t m j)"),
+            )
+
+        h = {}
+
+        def features(b, t):
+            h[b, t] = sbuf("h%d%d" % (b, t), [P, S], F32)
+            accs = [bank(2 * (t % 2) + i, [P, BANK], "h_acc%d%d%d" % (b, t, i)) for i in range(2)]
+            rows = slice(P * t, P * (t + 1))
+            for a in range(2):
+                for i in range(2):
+                    cols = slice(BANK * i, BANK * (i + 1))
+                    nc.tensor.matmul_mx(
+                        out=accs[i][:],
+                        lhsT=w1_code[a, b][:, rows].bitcast(FP8X4),
+                        lhsT_scale=w1_scale[a, b][:, rows],
+                        rhs=v_words[a][:, cols].bitcast(FP8X4),
+                        rhs_scale=v_scale[4 * a : P, cols],
+                        start=(a == 0),
+                        stop=(a == 1),
+                    )
+            bias = b1_sb[:, b, t : t + 1]
+            for i in range(2):
+                cols = slice(BANK * i, BANK * (i + 1))
+                if (b, t, i) == (0, 0, 1):
+                    nc.vector.tensor_scalar(h[b, t][:, cols], accs[i][:], bias, None, ALU.add)
+                else:
+                    nc.scalar.activation(h[b, t][:, cols], accs[i][:], ACT.Identity, bias=bias)
+
+        z_code = sbuf("z_code", [P, 2, PAIRS], U32)
+        z_scale = sbuf("z_scale", [P, 2, PAIRS], U8)
+
+        def finger_tiles(name, width, tag):
+            first = sbuf("first" + name, [P, PACK, width], F32, tag="first" + tag)
+            second = sbuf("second" + name, [P, PACK, width], F32, tag="second" + tag)
+            return first, second
+
+        def gather_fingers(tiles, b, t, j0, j1):
+            entries = slice(j0 // 16, j1 // 16)
+            nc.vector.tensor_copy(tiles[0][:, t, :], h[b, t][:].indirect(pos1_sb[:, entries]))
+            nc.vector.tensor_copy(tiles[1][:, t, :], h[b, t][:].indirect(pos2_sb[:, entries]))
+
+        def pair_max(tiles, name, width):
+            z_bf = sbuf("z_bf" + name, [P, width, PACK], BF16)
+            nc.vector.tensor_tensor(
+                z_bf[:].rearrange("p (c i) t -> p c t i", i=2),
+                tiles[0][:].rearrange("p t (c i) -> p c t i", i=2),
+                tiles[1][:].rearrange("p t (c i) -> p c t i", i=2),
+                ALU.max,
+            )
+            return z_bf
+
+        def quantize_z(z_bf, b, j0, j1):
+            nc.vector.quantize_mx(
+                out=z_code[:, b, j0:j1].bitcast(FP8X4),
+                scales=z_scale[:, b, j0:j1],
+                in_=z_bf[:].rearrange("p j t -> p (j t)"),
+            )
+
+        ws_bf = sbuf("ws_bf", [P, 3, 2, 2 * P, PACK], BF16)
+        ws_code = sbuf("ws_code", [P, 3, 2, 2 * P], U32)
+        ws_scale = sbuf("ws_scale", [P, 3, 2, 2 * P], U8)
+
+        def round_ws(q):
+            for a in range(2):
+                nc.scalar.copy(
+                    ws_bf[:, q, a, :, :].rearrange("p (c i) j -> p c j i", i=4),
+                    ws_raw[a][:, :, 2 * P * q : 2 * P * (q + 1)].rearrange("p j (c i) -> p c j i", i=4),
+                )
+
+        def quantize_ws(q):
+            nc.vector.quantize_mx(
+                out=ws_code[:, q, :, :].rearrange("p a n -> p (a n)").bitcast(FP8X4),
+                scales=ws_scale[:, q, :, :].rearrange("p a n -> p (a n)"),
+                in_=ws_bf[:, q, :, :, :].rearrange("p a n j -> p (a n j)"),
+            )
+
+        def products(half, q, first_bank):
+            m_acc = bank(first_bank, [P, 2, HALF], "m_acc%d%d" % (half, q))
+            g_acc = bank(first_bank + 1, [P, 2, HALF], "g_acc%d%d" % (half, q))
+            gate = sbuf("gate%d%d" % (half, q), [P, 2, HALF], F32, tag="gate", bufs=3)
+            j0 = HALF * half
+            for e in range(2):
+                c = 2 * q + e
+                for a in range(2):
+                    nc.tensor.matmul_mx(
+                        out=g_acc[:, e, :],
+                        lhsT=ws_code[:, q, a, P * e : P * (e + 1)].bitcast(FP8X4),
+                        lhsT_scale=ws_scale[:, q, a, P * e : P * (e + 1)],
+                        rhs=z_code[:, a, j0 : j0 + HALF].bitcast(FP8X4),
+                        rhs_scale=z_scale[:, a, j0 : j0 + HALF],
+                        start=(a == 0),
+                        stop=(a == 1),
+                    )
+            for e in range(2):
+                c = 2 * q + e
+                for s in range(HALF // P):
+                    cols = slice(j0 + P * s, j0 + P * (s + 1))
+                    for a in range(2):
+                        nc.tensor.matmul_mx(
+                            out=m_acc[:, e, P * s : P * (s + 1)],
+                            lhsT=wm_sb[:, a, 2 * P * c : 2 * P * (c + 1)].bitcast(FP4X4),
+                            lhsT_scale=wm_scale[:, a, P // 4 * c : P // 4 * (c + 1)].bitcast(U8),
+                            rhs=z_code[:, a, cols].bitcast(FP8X4),
+                            rhs_scale=z_scale[:, a, cols],
+                            start=(a == 0),
+                            stop=(a == 1),
+                        )
+            for e in range(2):
+                c = 2 * q + e
+                nc.scalar.activation(gate[:, e, :], g_acc[:, e, :], ACT.Sigmoid, bias=bs_sb[:, c : c + 1])
+            return m_acc, gate
+
+        def finish(half, q, m_acc, gate):
+            res = sbuf("res%d%d" % (half, q), [P, 2, HALF], F32, tag="res", bufs=3)
+            nc.vector.tensor_tensor(res[:], m_acc[:], gate[:], ALU.mult)
+            nc.sync.dma_start(
+                out=out[2 * P * q : 2 * P * (q + 1), HALF * half : HALF * (half + 1)].rearrange(
+                    "(e p) j -> p e j", p=P
+                ),
+                in_=res[:],
+            )
+
+        for a in range(2):
+            round_w1(a, 0, 0, True)
+            round_w1(a, 0, 1, False)
+            quantize_w1(a, 0, 0, 2)
+            quantize_w1(a, 0, 2, 4)
+        for t in range(PACK):
+            features(0, t)
+        for a in range(2):
+            round_w1(a, 1, 0, False)
+            round_w1(a, 1, 1, False)
+
+        fingers = finger_tiles("0", PAIRS, "x")
+        for t in range(PACK):
+            gather_fingers(fingers, 0, t, 0, PAIRS)
+        for a in range(2):
+            quantize_w1(a, 1, 0, 4)
+        for t in range(PACK):
+            features(1, t)
+        for q in range(3):
+            round_ws(q)
+        z_bf = pair_max(fingers, "0", PAIRS)
+
+        fingers = finger_tiles("10", HALF, "y")
+        gather_fingers(fingers, 1, 0, 0, HALF)
+        quantize_z(z_bf, 0, 0, PAIRS)
+        for t in range(1, PACK):
+            gather_fingers(fingers, 1, t, 0, HALF)
+        z_bf = pair_max(fingers, "10", HALF)
+        quantize_ws(0)
+        quantize_z(z_bf, 1, 0, HALF)
+        early = [products(0, 0, 4)]
+
+        fingers = finger_tiles("11", HALF, "x")
+        for t in range(PACK):
+            gather_fingers(fingers, 1, t, HALF, PAIRS)
+            if t < 2:
+                quantize_ws(t + 1)
+                early.append(products(0, t + 1, (6 + 2 * t) % 8))
+        z_bf = pair_max(fingers, "11", HALF)
+        finish(0, 0, *early[0])
+        quantize_z(z_bf, 1, HALF, PAIRS)
+        late = [products(1, 0, 2)]
+        finish(0, 1, *early[1])
+        late.append(products(1, 1, 4))
+        finish(0, 2, *early[2])
+        late.append(products(1, 2, 6))
+        for q in range(3):
+            finish(1, q, *late[q])

@@ -49,24 +49,18 @@ def tile_list_grasp_pair_wrench_kernel(
         warm = sbuf("warm", [P, 2], F32)
         nc.vector.memset(warm[:, 0:1], 0.0)
         nc.scalar.activation(warm[:, 1:2], warm[:, 0:1], ACT.Sigmoid)
+        for q in range(4):
+            nc.gpsimd.dma_start(
+                out=scale_window[32 * q : 32 * q + 8, :],
+                in_=tab_scales[:, 4 * q : 4 * q + 4, :].bitcast(I32),
+            )
+
         nc.sync.dma_start(offs_sb[:], offs)
         word_window = []
         for a in range(2):
             win = sbuf("word_window%d" % a, [P, T], I32)
             nc.sync.dma_start(out=win[:], in_=tab_words[a].rearrange("p t i -> p (t i)").bitcast(I32))
             word_window.append(win)
-            if a == 0:
-                for q in range(2):
-                    nc.sync.dma_start(
-                        out=scale_window[32 * q : 32 * q + 8, :],
-                        in_=tab_scales[:, 4 * q : 4 * q + 4, :].bitcast(I32),
-                    )
-                for q in range(2, 4):
-                    for c in range(2):
-                        nc.sync.dma_start(
-                            out=scale_window[32 * q + 4 * c : 32 * q + 4 * c + 4, :],
-                            in_=tab_scales[c, 4 * q : 4 * q + 4, :].bitcast(I32),
-                        )
 
         w1_raw = {}
 
@@ -82,10 +76,10 @@ def tile_list_grasp_pair_wrench_kernel(
 
         load_w1(0, 0)
         load_w1(1, 0)
-        nc.sync.dma_start(pos1_sb[:], pos1)
-        nc.sync.dma_start(pos2_sb[:], pos2)
         b1_sb = sbuf("b1_sb", [P, 2, PACK], F32)
         nc.sync.dma_start(out=b1_sb[:], in_=b1.rearrange("(b p t) -> p b t", b=2, t=PACK))
+        nc.sync.dma_start(pos1_sb[:], pos1)
+        nc.sync.dma_start(pos2_sb[:], pos2)
         load_w1(0, 1)
         load_w1(1, 1)
         ws_raw = []
@@ -119,7 +113,7 @@ def tile_list_grasp_pair_wrench_kernel(
 
         def round_w1(a, b, u, on_vector):
             if (a, b) not in w1_bf:
-                w1_bf[a, b] = sbuf("w1_bf%d%d" % (a, b), [P, PACK, P, PACK], BF16)
+                w1_bf[a, b] = sbuf("w1_bf%d%d" % (a, b), [P, PACK, P, PACK], BF16, tag="w1_bf", bufs=2)
             dst = w1_bf[a, b][:, 2 * u : 2 * u + 2, :, :].rearrange("p t m j -> p m j t")
             src = w1_raw[a, b][:].rearrange("p j (m t) -> p m j t", t=PACK)[:, :, :, 2 * u : 2 * u + 2]
             if on_vector:
@@ -142,7 +136,8 @@ def tile_list_grasp_pair_wrench_kernel(
 
         def features(b, t):
             h[b, t] = sbuf("h%d%d" % (b, t), [P, S], F32)
-            accs = [bank(2 * (t % 2) + i, [P, BANK], "h_acc%d%d%d" % (b, t, i)) for i in range(2)]
+            first_bank = 2 * (t % 2) if b == 0 else (4 + 2 * t) % 8
+            accs = [bank(first_bank + i, [P, BANK], "h_acc%d%d%d" % (b, t, i)) for i in range(2)]
             rows = slice(P * t, P * (t + 1))
             for a in range(2):
                 for i in range(2):
@@ -167,22 +162,22 @@ def tile_list_grasp_pair_wrench_kernel(
         z_code = sbuf("z_code", [P, 2, PAIRS], U32)
         z_scale = sbuf("z_scale", [P, 2, PAIRS], U8)
 
-        def finger_tiles(name, width, tag):
-            first = sbuf("first" + name, [P, PACK, width], F32, tag="first" + tag)
-            second = sbuf("second" + name, [P, PACK, width], F32, tag="second" + tag)
-            return first, second
+        fingers = {}
+        for b in range(2):
+            for f in range(2):
+                fingers[b, f] = sbuf("finger%d%d" % (b, f), [P, PACK, PAIRS], F32)
 
-        def gather_fingers(tiles, b, t, j0, j1):
+        def gather_fingers(b, t, j0, j1):
             entries = slice(j0 // 16, j1 // 16)
-            nc.vector.tensor_copy(tiles[0][:, t, :], h[b, t][:].indirect(pos1_sb[:, entries]))
-            nc.vector.tensor_copy(tiles[1][:, t, :], h[b, t][:].indirect(pos2_sb[:, entries]))
+            for f, pos_sb in enumerate((pos1_sb, pos2_sb)):
+                nc.vector.tensor_copy(fingers[b, f][:, t, j0:j1], h[b, t][:].indirect(pos_sb[:, entries]))
 
-        def pair_max(tiles, name, width):
-            z_bf = sbuf("z_bf" + name, [P, width, PACK], BF16)
+        def pair_max(b, j0, j1):
+            z_bf = sbuf("z_bf%d_%d" % (b, j0), [P, j1 - j0, PACK], BF16)
             nc.vector.tensor_tensor(
                 z_bf[:].rearrange("p (c i) t -> p c t i", i=2),
-                tiles[0][:].rearrange("p t (c i) -> p c t i", i=2),
-                tiles[1][:].rearrange("p t (c i) -> p c t i", i=2),
+                fingers[b, 0][:, :, j0:j1].rearrange("p t (c i) -> p c t i", i=2),
+                fingers[b, 1][:, :, j0:j1].rearrange("p t (c i) -> p c t i", i=2),
                 ALU.max,
             )
             return z_bf
@@ -212,45 +207,53 @@ def tile_list_grasp_pair_wrench_kernel(
                 in_=ws_bf[:, q, :, :, :].rearrange("p a n j -> p (a n j)"),
             )
 
-        def products(half, q, first_bank):
-            m_acc = bank(first_bank, [P, 2, HALF], "m_acc%d%d" % (half, q))
-            g_acc = bank(first_bank + 1, [P, 2, HALF], "g_acc%d%d" % (half, q))
-            gate = sbuf("gate%d%d" % (half, q), [P, 2, HALF], F32, tag="gate", bufs=3)
+        acc = {}
+
+        def products(half, q, a, first_bank=None):
+            if a == 0:
+                acc[half, q] = (
+                    bank(first_bank, [P, 2, HALF], "m_acc%d%d" % (half, q)),
+                    bank(first_bank + 1, [P, 2, HALF], "g_acc%d%d" % (half, q)),
+                )
+            m_acc, g_acc = acc[half, q]
             j0 = HALF * half
             for e in range(2):
-                c = 2 * q + e
-                for a in range(2):
-                    nc.tensor.matmul_mx(
-                        out=g_acc[:, e, :],
-                        lhsT=ws_code[:, q, a, P * e : P * (e + 1)].bitcast(FP8X4),
-                        lhsT_scale=ws_scale[:, q, a, P * e : P * (e + 1)],
-                        rhs=z_code[:, a, j0 : j0 + HALF].bitcast(FP8X4),
-                        rhs_scale=z_scale[:, a, j0 : j0 + HALF],
-                        start=(a == 0),
-                        stop=(a == 1),
-                    )
+                nc.tensor.matmul_mx(
+                    out=g_acc[:, e, :],
+                    lhsT=ws_code[:, q, a, P * e : P * (e + 1)].bitcast(FP8X4),
+                    lhsT_scale=ws_scale[:, q, a, P * e : P * (e + 1)],
+                    rhs=z_code[:, a, j0 : j0 + HALF].bitcast(FP8X4),
+                    rhs_scale=z_scale[:, a, j0 : j0 + HALF],
+                    start=(a == 0 and e == 0),
+                    stop=(a == 1 and e == 1),
+                )
             for e in range(2):
                 c = 2 * q + e
-                for s in range(HALF // P):
+                for s in range(2):
                     cols = slice(j0 + P * s, j0 + P * (s + 1))
-                    for a in range(2):
-                        nc.tensor.matmul_mx(
-                            out=m_acc[:, e, P * s : P * (s + 1)],
-                            lhsT=wm_sb[:, a, 2 * P * c : 2 * P * (c + 1)].bitcast(FP4X4),
-                            lhsT_scale=wm_scale[:, a, P // 4 * c : P // 4 * (c + 1)].bitcast(U8),
-                            rhs=z_code[:, a, cols].bitcast(FP8X4),
-                            rhs_scale=z_scale[:, a, cols],
-                            start=(a == 0),
-                            stop=(a == 1),
-                        )
+                    nc.tensor.matmul_mx(
+                        out=m_acc[:, e, P * s : P * (s + 1)],
+                        lhsT=wm_sb[:, a, 2 * P * c : 2 * P * (c + 1)].bitcast(FP4X4),
+                        lhsT_scale=wm_scale[:, a, P // 4 * c : P // 4 * (c + 1)].bitcast(U8),
+                        rhs=z_code[:, a, cols].bitcast(FP8X4),
+                        rhs_scale=z_scale[:, a, cols],
+                        start=(a == 0 and e == 0 and s == 0),
+                        stop=(a == 1 and e == 1 and s == 1),
+                    )
+
+        gates = {}
+
+        def gate(half, q):
+            gates[half, q] = sbuf("gate%d%d" % (half, q), [P, 2, HALF], F32, tag="gate", bufs=3)
             for e in range(2):
                 c = 2 * q + e
-                nc.scalar.activation(gate[:, e, :], g_acc[:, e, :], ACT.Sigmoid, bias=bs_sb[:, c : c + 1])
-            return m_acc, gate
+                nc.scalar.activation(
+                    gates[half, q][:, e, :], acc[half, q][1][:, e, :], ACT.Sigmoid, bias=bs_sb[:, c : c + 1]
+                )
 
-        def finish(half, q, m_acc, gate):
+        def finish(half, q):
             res = sbuf("res%d%d" % (half, q), [P, 2, HALF], F32, tag="res", bufs=3)
-            nc.vector.tensor_tensor(res[:], m_acc[:], gate[:], ALU.mult)
+            nc.vector.tensor_tensor(res[:], acc[half, q][0][:], gates[half, q][:], ALU.mult)
             nc.sync.dma_start(
                 out=out[2 * P * q : 2 * P * (q + 1), HALF * half : HALF * (half + 1)].rearrange(
                     "(e p) j -> p e j", p=P
@@ -264,45 +267,44 @@ def tile_list_grasp_pair_wrench_kernel(
             quantize_w1(a, 0, 0, 2)
             quantize_w1(a, 0, 2, 4)
         for t in range(PACK):
+            if t >= 2:
+                round_w1(t - 2, 1, 0, False)
+                round_w1(t - 2, 1, 1, False)
+                quantize_w1(t - 2, 1, 0, 4)
             features(0, t)
-        for a in range(2):
-            round_w1(a, 1, 0, False)
-            round_w1(a, 1, 1, False)
-
-        fingers = finger_tiles("0", PAIRS, "x")
-        for t in range(PACK):
-            gather_fingers(fingers, 0, t, 0, PAIRS)
-        for a in range(2):
-            quantize_w1(a, 1, 0, 4)
-        for t in range(PACK):
-            features(1, t)
-        for q in range(3):
-            round_ws(q)
-        z_bf = pair_max(fingers, "0", PAIRS)
-
-        fingers = finger_tiles("10", HALF, "y")
-        gather_fingers(fingers, 1, 0, 0, HALF)
+            gather_fingers(0, t, 0, PAIRS)
+        z_bf = pair_max(0, 0, PAIRS)
         quantize_z(z_bf, 0, 0, PAIRS)
-        for t in range(1, PACK):
-            gather_fingers(fingers, 1, t, 0, HALF)
-        z_bf = pair_max(fingers, "10", HALF)
-        quantize_ws(0)
-        quantize_z(z_bf, 1, 0, HALF)
-        early = [products(0, 0, 4)]
 
-        fingers = finger_tiles("11", HALF, "x")
-        for t in range(PACK):
-            gather_fingers(fingers, 1, t, HALF, PAIRS)
-            if t < 2:
-                quantize_ws(t + 1)
-                early.append(products(0, t + 1, (6 + 2 * t) % 8))
-        z_bf = pair_max(fingers, "11", HALF)
-        finish(0, 0, *early[0])
-        quantize_z(z_bf, 1, HALF, PAIRS)
-        late = [products(1, 0, 2)]
-        finish(0, 1, *early[1])
-        late.append(products(1, 1, 4))
-        finish(0, 2, *early[2])
-        late.append(products(1, 2, 6))
+        for t in range(3):
+            round_ws(t)
+            quantize_ws(t)
+            features(1, t)
+            gather_fingers(1, t, 0, PAIRS)
+        features(1, 3)
         for q in range(3):
-            finish(1, q, *late[q])
+            products(0, q, 0, (4 + 2 * q) % 8)
+        gather_fingers(1, 3, 0, HALF)
+        z_bf = pair_max(1, 0, HALF)
+        quantize_z(z_bf, 1, 0, HALF)
+        for q in range(3):
+            products(0, q, 1)
+            gate(0, q)
+        products(1, 0, 0, 2)
+
+        gather_fingers(1, 3, HALF, PAIRS)
+        z_bf = pair_max(1, HALF, PAIRS)
+        finish(0, 0)
+        quantize_z(z_bf, 1, HALF, PAIRS)
+        products(1, 0, 1)
+        gate(1, 0)
+        products(1, 1, 0, 4)
+        products(1, 1, 1)
+        gate(1, 1)
+        finish(0, 1)
+        products(1, 2, 0, 6)
+        products(1, 2, 1)
+        gate(1, 2)
+        finish(0, 2)
+        for q in range(3):
+            finish(1, q)

@@ -21,6 +21,7 @@ PACK = 4
 K_PASS = P * PACK
 BANK = 512
 HALF = PAIRS // 2
+FIRST_WORDS = 1536
 
 
 def tile_list_grasp_pair_wrench_kernel(
@@ -49,18 +50,29 @@ def tile_list_grasp_pair_wrench_kernel(
         warm = sbuf("warm", [P, 2], F32)
         nc.vector.memset(warm[:, 0:1], 0.0)
         nc.scalar.activation(warm[:, 1:2], warm[:, 0:1], ACT.Sigmoid)
-        for q in range(4):
-            nc.gpsimd.dma_start(
-                out=scale_window[32 * q : 32 * q + 8, :],
-                in_=tab_scales[:, 4 * q : 4 * q + 4, :].bitcast(I32),
+        word_window = [sbuf("word_window%d" % a, [P, T], I32) for a in range(2)]
+
+        def load_words(a, c0, c1):
+            nc.sync.dma_start(
+                out=word_window[a][:, c0:c1],
+                in_=tab_words[a].rearrange("p t i -> p (t i)").bitcast(I32)[:, c0:c1],
             )
 
+        def load_scale_rows(r):
+            for a in range(2):
+                nc.sync.dma_start(
+                    out=scale_window[4 * a + r : P : 32, :],
+                    in_=tab_scales[a, r:16:4, :].bitcast(I32),
+                )
+
         nc.sync.dma_start(offs_sb[:], offs)
-        word_window = []
-        for a in range(2):
-            win = sbuf("word_window%d" % a, [P, T], I32)
-            nc.sync.dma_start(out=win[:], in_=tab_words[a].rearrange("p t i -> p (t i)").bitcast(I32))
-            word_window.append(win)
+        load_words(0, 0, FIRST_WORDS)
+        load_scale_rows(0)
+        load_scale_rows(1)
+        load_words(0, FIRST_WORDS, T)
+        load_scale_rows(2)
+        load_scale_rows(3)
+        load_words(1, 0, T)
 
         w1_raw = {}
 
@@ -251,11 +263,11 @@ def tile_list_grasp_pair_wrench_kernel(
                     gates[half, q][:, e, :], acc[half, q][1][:, e, :], ACT.Sigmoid, bias=bs_sb[:, c : c + 1]
                 )
 
-        def finish(half, q):
-            res = sbuf("res%d%d" % (half, q), [P, 2, HALF], F32, tag="res", bufs=3)
-            nc.vector.tensor_tensor(res[:], acc[half, q][0][:], gates[half, q][:], ALU.mult)
+        def finish(half, q, e0=0, e1=2):
+            res = sbuf("res%d%d%d" % (half, q, e0), [P, e1 - e0, HALF], F32, tag="res", bufs=4)
+            nc.vector.tensor_tensor(res[:], acc[half, q][0][:, e0:e1, :], gates[half, q][:, e0:e1, :], ALU.mult)
             nc.sync.dma_start(
-                out=out[2 * P * q : 2 * P * (q + 1), HALF * half : HALF * (half + 1)].rearrange(
+                out=out[P * (2 * q + e0) : P * (2 * q + e1), HALF * half : HALF * (half + 1)].rearrange(
                     "(e p) j -> p e j", p=P
                 ),
                 in_=res[:],
@@ -306,5 +318,7 @@ def tile_list_grasp_pair_wrench_kernel(
         products(1, 2, 1)
         gate(1, 2)
         finish(0, 2)
-        for q in range(3):
-            finish(1, q)
+        finish(1, 0)
+        finish(1, 1)
+        finish(1, 2, 0, 1)
+        finish(1, 2, 1, 2)

@@ -18,9 +18,14 @@ ACT = mybir.ActivationFunctionType
 
 P = 128
 PACK = 4
-K_PASS = P * PACK
+PASS = P * PACK
+PASSES = 2
 BANK = 512
+BANKS = 8
+QUADS = 4
+PER_COLUMN = 16
 HALF = PAIRS // 2
+COUPLES = N // (2 * P)
 FIRST_WORDS = 1536
 
 
@@ -36,37 +41,34 @@ def tile_list_grasp_pair_wrench_kernel(
         def sbuf(name, shape, dtype, tag="", bufs=1):
             return keep.tile(shape, dtype, name=name, tag=tag or name, bufs=bufs, align_bytes=64)
 
-        def bank(k, shape, name):
-            return psum.tile(shape, F32, name=name, tag="bank%d" % k)
+        def bank(number, shape, name):
+            return psum.tile(shape, F32, name=name, tag="bank%d" % number)
 
-        offs_sb = lists.tile([P, S // 16], U16, name="offs_sb")
-        pos1_sb = lists.tile([P, PAIRS // 16], U16, name="pos1_sb")
-        pos2_sb = lists.tile([P, PAIRS // 16], U16, name="pos2_sb")
+        offs_sb = lists.tile([P, S // PER_COLUMN], U16, name="offs_sb")
+        pos1_sb = lists.tile([P, PAIRS // PER_COLUMN], U16, name="pos1_sb")
+        pos2_sb = lists.tile([P, PAIRS // PER_COLUMN], U16, name="pos2_sb")
 
         scale_window = sbuf("scale_window", [P, T // 4], I32)
-        wm_scale = sbuf("wm_scale", [P, 2, N // 4], I32)
+        wm_scale = sbuf("wm_scale", [P, PASSES, N // 4], I32)
         nc.vector.memset(scale_window[:], 0)
         nc.vector.memset(wm_scale[:], 0)
-        warm = sbuf("warm", [P, 2], F32)
-        nc.vector.memset(warm[:, 0:1], 0.0)
-        nc.scalar.activation(warm[:, 1:2], warm[:, 0:1], ACT.Sigmoid)
-        word_window = [sbuf("word_window%d" % a, [P, T], I32) for a in range(2)]
+        word_window = [sbuf("word_window%d" % a, [P, T], I32) for a in range(PASSES)]
 
-        def load_words(a, c0, c1):
+        def load_words(a, t0, t1):
             nc.sync.dma_start(
-                out=word_window[a][:, c0:c1],
-                in_=tab_words[a].rearrange("p t i -> p (t i)").bitcast(I32)[:, c0:c1],
+                out=word_window[a][:, t0:t1],
+                in_=tab_words[a].rearrange("p t x -> p (t x)").bitcast(I32)[:, t0:t1],
             )
 
-        def load_scale_rows(r):
-            for a in range(2):
+        def load_scale_rows(row):
+            for a in range(PASSES):
                 nc.sync.dma_start(
-                    out=scale_window[4 * a + r : P : 32, :],
-                    in_=tab_scales[a, r:16:4, :].bitcast(I32),
+                    out=scale_window[4 * a + row : P : 32, :],
+                    in_=tab_scales[a, row:16:4, :].bitcast(I32),
                 )
 
-        nc.sync.dma_start(offs_sb[:], offs)
         load_words(0, 0, FIRST_WORDS)
+        nc.sync.dma_start(offs_sb[:], offs)
         load_scale_rows(0)
         load_scale_rows(1)
         load_words(0, FIRST_WORDS, T)
@@ -77,246 +79,240 @@ def tile_list_grasp_pair_wrench_kernel(
         w1_raw = {}
 
         def load_w1(a, b):
-            raw = sbuf("w1_raw%d%d" % (a, b), [P, PACK, K_PASS], F32)
+            w1_raw[a, b] = sbuf("w1_raw%d%d" % (a, b), [P, PACK, PASS], F32)
             nc.sync.dma_start(
-                out=raw[:],
-                in_=w1[K_PASS * a : K_PASS * (a + 1), K_PASS * b : K_PASS * (b + 1)].rearrange(
-                    "(p j) c -> p j c", j=PACK
-                ),
+                out=w1_raw[a, b][:],
+                in_=w1[PASS * a : PASS * (a + 1), PASS * b : PASS * (b + 1)].rearrange("(p x) c -> p x c", x=PACK),
             )
-            w1_raw[a, b] = raw
 
         load_w1(0, 0)
         load_w1(1, 0)
-        b1_sb = sbuf("b1_sb", [P, 2, PACK], F32)
-        nc.sync.dma_start(out=b1_sb[:], in_=b1.rearrange("(b p t) -> p b t", b=2, t=PACK))
+        b1_sb = sbuf("b1_sb", [P, PASSES, PACK], F32)
+        nc.sync.dma_start(out=b1_sb[:], in_=b1.rearrange("(b p t) -> p b t", b=PASSES, t=PACK))
         nc.sync.dma_start(pos1_sb[:], pos1)
         nc.sync.dma_start(pos2_sb[:], pos2)
         load_w1(0, 1)
         load_w1(1, 1)
         ws_raw = []
-        for a in range(2):
-            raw = sbuf("ws_raw%d" % a, [P, PACK, N], F32)
+        for b in range(PASSES):
+            ws_raw.append(sbuf("ws_raw%d" % b, [P, PACK, N], F32))
             nc.sync.dma_start(
-                out=raw[:], in_=ws[K_PASS * a : K_PASS * (a + 1), :].rearrange("(p j) n -> p j n", j=PACK)
+                out=ws_raw[b][:], in_=ws[PASS * b : PASS * (b + 1), :].rearrange("(p x) n -> p x n", x=PACK)
             )
-            ws_raw.append(raw)
-        wm_sb = sbuf("wm_sb", [P, 2, 2 * N], U8)
-        nc.sync.dma_start(out=wm_sb[:].bitcast(I32), in_=wm_words.bitcast(I32).rearrange("a p w -> p a w"))
-        for q in range(4):
+        wm_sb = sbuf("wm_sb", [P, PASSES, 2 * N], U8)
+        nc.sync.dma_start(out=wm_sb[:].bitcast(I32), in_=wm_words.bitcast(I32).rearrange("b p w -> p b w"))
+        for quad in range(QUADS):
             nc.sync.dma_start(
-                out=wm_scale[32 * q : 32 * q + 4, :, :],
-                in_=wm_scales[:, 4 * q : 4 * q + 4, :].bitcast(I32).rearrange("a r w -> r a w"),
+                out=wm_scale[32 * quad : 32 * quad + 4, :, :],
+                in_=wm_scales[:, 4 * quad : 4 * quad + 4, :].bitcast(I32).rearrange("b row w -> row b w"),
             )
         bs_sb = sbuf("bs_sb", [P, N // P], F32)
         with nc.allow_non_contiguous_dma(reason="one bias value for each partition and output tile"):
             nc.sync.dma_start(out=bs_sb[:], in_=bs.rearrange("(c p) -> p c", p=P))
 
         v_scale = sbuf("v_scale", [P, S], U8)
-        v_words = []
-        for a in range(2):
-            g = sbuf("v_words%d" % a, [P, S], U32)
-            nc.vector.tensor_copy(g[:], word_window[a][:].bitcast(U32).indirect(offs_sb[:]))
-            v_words.append(g)
-            if a == 0:
-                nc.vector.tensor_copy(v_scale[:], scale_window[:].bitcast(U8).indirect(offs_sb[:]))
+        v_words = [sbuf("v_words%d" % a, [P, S], U32) for a in range(PASSES)]
+        nc.vector.tensor_copy(v_words[0][:], word_window[0][:].bitcast(U32).indirect(offs_sb[:]))
+        nc.vector.tensor_copy(v_scale[:], scale_window[:].bitcast(U8).indirect(offs_sb[:]))
+        nc.vector.tensor_copy(v_words[1][:], word_window[1][:].bitcast(U32).indirect(offs_sb[:]))
 
         w1_bf, w1_code, w1_scale = {}, {}, {}
 
-        def round_w1(a, b, u, on_vector):
+        def round_w1(a, b, t0, copy):
             if (a, b) not in w1_bf:
                 w1_bf[a, b] = sbuf("w1_bf%d%d" % (a, b), [P, PACK, P, PACK], BF16, tag="w1_bf", bufs=2)
-            dst = w1_bf[a, b][:, 2 * u : 2 * u + 2, :, :].rearrange("p t m j -> p m j t")
-            src = w1_raw[a, b][:].rearrange("p j (m t) -> p m j t", t=PACK)[:, :, :, 2 * u : 2 * u + 2]
-            if on_vector:
-                nc.vector.tensor_copy(dst, src)
-            else:
-                nc.scalar.copy(dst, src)
+            copy(
+                w1_bf[a, b][:, t0 : t0 + 2, :, :].rearrange("p t m x -> p m x t"),
+                w1_raw[a, b][:].rearrange("p x (m t) -> p m x t", t=PACK)[:, :, :, t0 : t0 + 2],
+            )
 
         def quantize_w1(a, b, t0, t1):
             if (a, b) not in w1_code:
-                w1_code[a, b] = sbuf("w1_code%d%d" % (a, b), [P, K_PASS], U32)
-                w1_scale[a, b] = sbuf("w1_scale%d%d" % (a, b), [P, K_PASS], U8)
+                w1_code[a, b] = sbuf("w1_code%d%d" % (a, b), [P, PASS], U32)
+                w1_scale[a, b] = sbuf("w1_scale%d%d" % (a, b), [P, PASS], U8)
             cols = slice(P * t0, P * t1)
             nc.vector.quantize_mx(
                 out=w1_code[a, b][:, cols].bitcast(FP8X4),
                 scales=w1_scale[a, b][:, cols],
-                in_=w1_bf[a, b][:, t0:t1, :, :].rearrange("p t m j -> p (t m j)"),
+                in_=w1_bf[a, b][:, t0:t1, :, :].rearrange("p t m x -> p (t m x)"),
             )
 
-        h = {}
+        h, h_acc = {}, {}
 
-        def features(b, t):
+        def multiply_h(b, t, first_bank):
             h[b, t] = sbuf("h%d%d" % (b, t), [P, S], F32)
-            first_bank = 2 * (t % 2) if b == 0 else (4 + 2 * t) % 8
-            accs = [bank(first_bank + i, [P, BANK], "h_acc%d%d%d" % (b, t, i)) for i in range(2)]
+            h_acc[b, t] = [bank(first_bank + side, [P, BANK], "h_acc%d%d%d" % (b, t, side)) for side in range(2)]
             rows = slice(P * t, P * (t + 1))
-            for a in range(2):
-                for i in range(2):
-                    cols = slice(BANK * i, BANK * (i + 1))
+            for a in range(PASSES):
+                for side in range(2):
+                    cols = slice(BANK * side, BANK * (side + 1))
                     nc.tensor.matmul_mx(
-                        out=accs[i][:],
+                        out=h_acc[b, t][side][:],
                         lhsT=w1_code[a, b][:, rows].bitcast(FP8X4),
                         lhsT_scale=w1_scale[a, b][:, rows],
                         rhs=v_words[a][:, cols].bitcast(FP8X4),
                         rhs_scale=v_scale[4 * a : P, cols],
                         start=(a == 0),
-                        stop=(a == 1),
+                        stop=(a == PASSES - 1),
                     )
-            bias = b1_sb[:, b, t : t + 1]
-            for i in range(2):
-                cols = slice(BANK * i, BANK * (i + 1))
-                if (b, t, i) == (0, 0, 1):
-                    nc.vector.tensor_scalar(h[b, t][:, cols], accs[i][:], bias, None, ALU.add)
-                else:
-                    nc.scalar.activation(h[b, t][:, cols], accs[i][:], ACT.Identity, bias=bias)
 
-        z_code = sbuf("z_code", [P, 2, PAIRS], U32)
-        z_scale = sbuf("z_scale", [P, 2, PAIRS], U8)
+        def add_bias(b, t, side):
+            bias = b1_sb[:, b, t : t + 1]
+            cols = slice(BANK * side, BANK * (side + 1))
+            if (b, t, side) == (0, 0, 1):
+                nc.vector.tensor_scalar(h[b, t][:, cols], h_acc[b, t][side][:], bias, None, ALU.add)
+            else:
+                nc.scalar.activation(h[b, t][:, cols], h_acc[b, t][side][:], ACT.Identity, bias=bias)
+
+        z_code = {1: sbuf("z_code1", [P, PAIRS], U32)}
+        z_scale = sbuf("z_scale", [P, PASSES, PAIRS], U8)
 
         fingers = {}
-        for b in range(2):
+        for b in range(PASSES):
             for f in range(2):
                 fingers[b, f] = sbuf("finger%d%d" % (b, f), [P, PACK, PAIRS], F32)
 
         def gather_fingers(b, t, j0, j1):
-            entries = slice(j0 // 16, j1 // 16)
+            entries = slice(j0 // PER_COLUMN, j1 // PER_COLUMN)
             for f, pos_sb in enumerate((pos1_sb, pos2_sb)):
                 nc.vector.tensor_copy(fingers[b, f][:, t, j0:j1], h[b, t][:].indirect(pos_sb[:, entries]))
 
         def pair_max(b, j0, j1):
             z_bf = sbuf("z_bf%d_%d" % (b, j0), [P, j1 - j0, PACK], BF16)
             nc.vector.tensor_tensor(
-                z_bf[:].rearrange("p (c i) t -> p c t i", i=2),
-                fingers[b, 0][:, :, j0:j1].rearrange("p t (c i) -> p c t i", i=2),
-                fingers[b, 1][:, :, j0:j1].rearrange("p t (c i) -> p c t i", i=2),
+                z_bf[:].rearrange("p (c u) t -> p c t u", u=2),
+                fingers[b, 0][:, :, j0:j1].rearrange("p t (c u) -> p c t u", u=2),
+                fingers[b, 1][:, :, j0:j1].rearrange("p t (c u) -> p c t u", u=2),
                 ALU.max,
             )
             return z_bf
 
         def quantize_z(z_bf, b, j0, j1):
             nc.vector.quantize_mx(
-                out=z_code[:, b, j0:j1].bitcast(FP8X4),
+                out=z_code[b][:, j0:j1].bitcast(FP8X4),
                 scales=z_scale[:, b, j0:j1],
                 in_=z_bf[:].rearrange("p j t -> p (j t)"),
             )
 
-        ws_bf = sbuf("ws_bf", [P, 3, 2, 2 * P, PACK], BF16)
-        ws_code = sbuf("ws_code", [P, 3, 2, 2 * P], U32)
-        ws_scale = sbuf("ws_scale", [P, 3, 2, 2 * P], U8)
+        ws_bf = [sbuf("ws_bf%d" % q, [P, PASSES, 2 * P, PACK], BF16) for q in range(COUPLES)]
+        ws_code = sbuf("ws_code", [P, COUPLES, PASSES, 2 * P], U32)
+        ws_scale = sbuf("ws_scale", [P, COUPLES, PASSES, 2 * P], U8)
 
         def round_ws(q):
-            for a in range(2):
+            for b in range(PASSES):
                 nc.scalar.copy(
-                    ws_bf[:, q, a, :, :].rearrange("p (c i) j -> p c j i", i=4),
-                    ws_raw[a][:, :, 2 * P * q : 2 * P * (q + 1)].rearrange("p j (c i) -> p c j i", i=4),
+                    ws_bf[q][:, b, :, :].rearrange("p (c u) x -> p c x u", u=4),
+                    ws_raw[b][:, :, 2 * P * q : 2 * P * (q + 1)].rearrange("p x (c u) -> p c x u", u=4),
                 )
 
         def quantize_ws(q):
             nc.vector.quantize_mx(
-                out=ws_code[:, q, :, :].rearrange("p a n -> p (a n)").bitcast(FP8X4),
-                scales=ws_scale[:, q, :, :].rearrange("p a n -> p (a n)"),
-                in_=ws_bf[:, q, :, :, :].rearrange("p a n j -> p (a n j)"),
+                out=ws_code[:, q, :, :].rearrange("p b n -> p (b n)").bitcast(FP8X4),
+                scales=ws_scale[:, q, :, :].rearrange("p b n -> p (b n)"),
+                in_=ws_bf[q][:].rearrange("p b n x -> p (b n x)"),
             )
 
-        acc = {}
+        m_acc, g_acc, gates = {}, {}, {}
 
-        def products(half, q, a, first_bank=None):
-            if a == 0:
-                acc[half, q] = (
-                    bank(first_bank, [P, 2, HALF], "m_acc%d%d" % (half, q)),
-                    bank(first_bank + 1, [P, 2, HALF], "g_acc%d%d" % (half, q)),
-                )
-            m_acc, g_acc = acc[half, q]
+        def multiply_z(half, q, b, first_bank=None):
+            if b == 0:
+                m_acc[half, q] = bank(first_bank, [P, 2, HALF], "m_acc%d%d" % (half, q))
+                g_acc[half, q] = bank(first_bank + 1, [P, 2, HALF], "g_acc%d%d" % (half, q))
             j0 = HALF * half
             for e in range(2):
                 nc.tensor.matmul_mx(
-                    out=g_acc[:, e, :],
-                    lhsT=ws_code[:, q, a, P * e : P * (e + 1)].bitcast(FP8X4),
-                    lhsT_scale=ws_scale[:, q, a, P * e : P * (e + 1)],
-                    rhs=z_code[:, a, j0 : j0 + HALF].bitcast(FP8X4),
-                    rhs_scale=z_scale[:, a, j0 : j0 + HALF],
-                    start=(a == 0 and e == 0),
-                    stop=(a == 1 and e == 1),
+                    out=g_acc[half, q][:, e, :],
+                    lhsT=ws_code[:, q, b, P * e : P * (e + 1)].bitcast(FP8X4),
+                    lhsT_scale=ws_scale[:, q, b, P * e : P * (e + 1)],
+                    rhs=z_code[b][:, j0 : j0 + HALF].bitcast(FP8X4),
+                    rhs_scale=z_scale[:, b, j0 : j0 + HALF],
+                    start=(b, e) == (0, 0),
+                    stop=(b, e) == (1, 1),
                 )
             for e in range(2):
                 c = 2 * q + e
-                for s in range(2):
-                    cols = slice(j0 + P * s, j0 + P * (s + 1))
+                for piece in range(HALF // P):
+                    cols = slice(j0 + P * piece, j0 + P * (piece + 1))
                     nc.tensor.matmul_mx(
-                        out=m_acc[:, e, P * s : P * (s + 1)],
-                        lhsT=wm_sb[:, a, 2 * P * c : 2 * P * (c + 1)].bitcast(FP4X4),
-                        lhsT_scale=wm_scale[:, a, P // 4 * c : P // 4 * (c + 1)].bitcast(U8),
-                        rhs=z_code[:, a, cols].bitcast(FP8X4),
-                        rhs_scale=z_scale[:, a, cols],
-                        start=(a == 0 and e == 0 and s == 0),
-                        stop=(a == 1 and e == 1 and s == 1),
+                        out=m_acc[half, q][:, e, P * piece : P * (piece + 1)],
+                        lhsT=wm_sb[:, b, 2 * P * c : 2 * P * (c + 1)].bitcast(FP4X4),
+                        lhsT_scale=wm_scale[:, b, P // 4 * c : P // 4 * (c + 1)].bitcast(U8),
+                        rhs=z_code[b][:, cols].bitcast(FP8X4),
+                        rhs_scale=z_scale[:, b, cols],
+                        start=(b, e, piece) == (0, 0, 0),
+                        stop=(b, e, piece) == (1, 1, 1),
                     )
 
-        gates = {}
-
         def gate(half, q):
-            gates[half, q] = sbuf("gate%d%d" % (half, q), [P, 2, HALF], F32, tag="gate", bufs=3)
+            gates[half, q] = sbuf("gate%d%d" % (half, q), [P, 2, HALF], F32)
             for e in range(2):
                 c = 2 * q + e
                 nc.scalar.activation(
-                    gates[half, q][:, e, :], acc[half, q][1][:, e, :], ACT.Sigmoid, bias=bs_sb[:, c : c + 1]
+                    gates[half, q][:, e, :], g_acc[half, q][:, e, :], ACT.Sigmoid, bias=bs_sb[:, c : c + 1]
                 )
 
         def finish(half, q, e0=0, e1=2):
-            res = sbuf("res%d%d%d" % (half, q, e0), [P, e1 - e0, HALF], F32, tag="res", bufs=4)
-            nc.vector.tensor_tensor(res[:], acc[half, q][0][:, e0:e1, :], gates[half, q][:, e0:e1, :], ALU.mult)
+            result = gates[half, q][:, e0:e1, :]
+            nc.vector.tensor_tensor(result, m_acc[half, q][:, e0:e1, :], result, ALU.mult)
+            rows = slice(P * (2 * q + e0), P * (2 * q + e1))
             nc.sync.dma_start(
-                out=out[P * (2 * q + e0) : P * (2 * q + e1), HALF * half : HALF * (half + 1)].rearrange(
-                    "(e p) j -> p e j", p=P
-                ),
-                in_=res[:],
+                out=out[rows, HALF * half : HALF * (half + 1)].rearrange("(e p) j -> p e j", p=P), in_=result
             )
 
-        for a in range(2):
-            round_w1(a, 0, 0, True)
-            round_w1(a, 0, 1, False)
+        for a in range(PASSES):
+            round_w1(a, 0, 0, nc.vector.tensor_copy)
+            round_w1(a, 0, 2, nc.scalar.copy)
             quantize_w1(a, 0, 0, 2)
-            quantize_w1(a, 0, 2, 4)
+            quantize_w1(a, 0, 2, PACK)
         for t in range(PACK):
             if t >= 2:
-                round_w1(t - 2, 1, 0, False)
-                round_w1(t - 2, 1, 1, False)
-                quantize_w1(t - 2, 1, 0, 4)
-            features(0, t)
+                round_w1(t - 2, 1, 0, nc.scalar.copy)
+                round_w1(t - 2, 1, 2, nc.scalar.copy)
+                quantize_w1(t - 2, 1, 0, PACK)
+            multiply_h(0, t, 2 * (t % 2))
+            add_bias(0, t, 0)
+            add_bias(0, t, 1)
             gather_fingers(0, t, 0, PAIRS)
         z_bf = pair_max(0, 0, PAIRS)
-        quantize_z(z_bf, 0, 0, PAIRS)
 
-        for t in range(3):
+        for t in range(2):
             round_ws(t)
             quantize_ws(t)
-            features(1, t)
+            multiply_h(1, t, 4 + 2 * t)
+            add_bias(1, t, 0)
+            add_bias(1, t, 1)
             gather_fingers(1, t, 0, PAIRS)
-        features(1, 3)
-        for q in range(3):
-            products(0, q, 0, (4 + 2 * q) % 8)
+        round_ws(2)
+        quantize_ws(2)
+        z_code[0] = sbuf("z_code0", [P, PAIRS], U32, tag="ws_bf2")
+        quantize_z(z_bf, 0, 0, PAIRS)
+        multiply_h(1, 2, 0)
+        multiply_h(1, 3, 2)
+        for t, side in ((2, 0), (3, 0), (3, 1), (2, 1)):
+            add_bias(1, t, side)
+
+        for q in range(COUPLES):
+            multiply_z(0, q, 0, (4 + 2 * q) % BANKS)
         gather_fingers(1, 3, 0, HALF)
+        gather_fingers(1, 2, 0, HALF)
         z_bf = pair_max(1, 0, HALF)
         quantize_z(z_bf, 1, 0, HALF)
-        for q in range(3):
-            products(0, q, 1)
+        for q in range(COUPLES):
+            multiply_z(0, q, 1)
             gate(0, q)
-        products(1, 0, 0, 2)
+        multiply_z(1, 0, 0, 2)
 
         gather_fingers(1, 3, HALF, PAIRS)
-        z_bf = pair_max(1, HALF, PAIRS)
+        gather_fingers(1, 2, HALF, PAIRS)
         finish(0, 0)
-        quantize_z(z_bf, 1, HALF, PAIRS)
-        products(1, 0, 1)
-        gate(1, 0)
-        products(1, 1, 0, 4)
-        products(1, 1, 1)
-        gate(1, 1)
+        multiply_z(1, 1, 0, 4)
+        z_bf = pair_max(1, HALF, PAIRS)
         finish(0, 1)
-        products(1, 2, 0, 6)
-        products(1, 2, 1)
-        gate(1, 2)
+        multiply_z(1, 2, 0, 6)
+        quantize_z(z_bf, 1, HALF, PAIRS)
+        for q in range(COUPLES):
+            multiply_z(1, q, 1)
+            gate(1, q)
         finish(0, 2)
         finish(1, 0)
         finish(1, 1)

@@ -21,12 +21,12 @@ PACK = 4
 PASS = P * PACK
 PASSES = 2
 BANK = 512
-BANKS = 8
 QUADS = 4
 PER_COLUMN = 16
 HALF = PAIRS // 2
 COUPLES = N // (2 * P)
 FIRST_WORDS = 1536
+PIECES = ((0, 128), (128, 256), (256, 512))
 
 
 def tile_list_grasp_pair_wrench_kernel(
@@ -74,31 +74,64 @@ def tile_list_grasp_pair_wrench_kernel(
         load_words(0, FIRST_WORDS, T)
         load_scale_rows(2)
         load_scale_rows(3)
-        load_words(1, 0, T)
 
-        w1_raw = {}
+        piece_raw = {}
 
-        def load_w1(a, b):
-            w1_raw[a, b] = sbuf("w1_raw%d%d" % (a, b), [P, PACK, PASS], F32)
+        def load_piece(n):
+            c0, c1 = PIECES[n]
+            for a in range(PASSES):
+                piece_raw[n, a] = sbuf("piece_raw%d%d" % (n, a), [P, PACK, c1 - c0], F32)
+                nc.sync.dma_start(
+                    out=piece_raw[n, a][:],
+                    in_=w1[PASS * a : PASS * (a + 1), c0:c1].rearrange("(p x) c -> p x c", x=PACK),
+                )
+
+        bias_of = {}
+
+        def load_bias(b, t0, t1):
+            rows = b1[PASS * b : PASS * (b + 1)].rearrange("(p t) -> p t" if b else "(t p) -> p t", t=PACK)
+            column = sbuf("b1_%d%d" % (b, t0), [P, t1 - t0], F32)
+            with nc.allow_non_contiguous_dma(reason="one bias value for each partition and tile of h"):
+                nc.sync.dma_start(out=column[:], in_=rows[:, t0:t1])
+            for t in range(t0, t1):
+                bias_of[b, t] = column[:, t - t0 : t - t0 + 1]
+
+        w1_raw = []
+
+        def load_dealt(a):
+            w1_raw.append(sbuf("w1_raw%d" % a, [P, PACK, PASS], F32))
             nc.sync.dma_start(
-                out=w1_raw[a, b][:],
-                in_=w1[PASS * a : PASS * (a + 1), PASS * b : PASS * (b + 1)].rearrange("(p x) c -> p x c", x=PACK),
+                out=w1_raw[a][:],
+                in_=w1[PASS * a : PASS * (a + 1), PASS:H].rearrange("(p x) c -> p x c", x=PACK),
             )
 
-        load_w1(0, 0)
-        load_w1(1, 0)
-        b1_sb = sbuf("b1_sb", [P, PASSES, PACK], F32)
-        nc.sync.dma_start(out=b1_sb[:], in_=b1.rearrange("(b p t) -> p b t", b=PASSES, t=PACK))
+        ws_raw = []
+
+        def load_ws(q):
+            ws_raw.append(sbuf("ws_raw%d" % q, [P, PASSES, PACK, 2 * P], F32))
+            for b in range(PASSES):
+                nc.sync.dma_start(
+                    out=ws_raw[q][:, b, :, :],
+                    in_=ws[PASS * b : PASS * (b + 1), 2 * P * q : 2 * P * (q + 1)].rearrange("(p x) n -> p x n", x=PACK),
+                )
+
+        load_piece(0)
+        load_words(1, 0, T)
+        load_piece(1)
+        load_bias(0, 0, 1)
         nc.sync.dma_start(pos1_sb[:], pos1)
         nc.sync.dma_start(pos2_sb[:], pos2)
-        load_w1(0, 1)
-        load_w1(1, 1)
-        ws_raw = []
-        for b in range(PASSES):
-            ws_raw.append(sbuf("ws_raw%d" % b, [P, PACK, N], F32))
-            nc.sync.dma_start(
-                out=ws_raw[b][:], in_=ws[PASS * b : PASS * (b + 1), :].rearrange("(p x) n -> p x n", x=PACK)
-            )
+        load_piece(2)
+        load_bias(0, 1, 2)
+        load_dealt(0)
+        load_bias(0, 2, 3)
+        load_dealt(1)
+        load_bias(0, 3, 4)
+        load_ws(0)
+        load_bias(1, 0, 2)
+        load_ws(1)
+        load_bias(1, 2, 3)
+        load_ws(2)
         wm_sb = sbuf("wm_sb", [P, PASSES, 2 * N], U8)
         nc.sync.dma_start(out=wm_sb[:].bitcast(I32), in_=wm_words.bitcast(I32).rearrange("b p w -> p b w"))
         for quad in range(QUADS):
@@ -114,34 +147,51 @@ def tile_list_grasp_pair_wrench_kernel(
         v_words = [sbuf("v_words%d" % a, [P, S], U32) for a in range(PASSES)]
         nc.vector.tensor_copy(v_words[0][:], word_window[0][:].bitcast(U32).indirect(offs_sb[:]))
         nc.vector.tensor_copy(v_scale[:], scale_window[:].bitcast(U8).indirect(offs_sb[:]))
-        nc.vector.tensor_copy(v_words[1][:], word_window[1][:].bitcast(U32).indirect(offs_sb[:]))
 
-        w1_bf, w1_code, w1_scale = {}, {}, {}
-
-        def round_w1(a, b, t0, copy):
-            if (a, b) not in w1_bf:
-                w1_bf[a, b] = sbuf("w1_bf%d%d" % (a, b), [P, PACK, P, PACK], BF16, tag="w1_bf", bufs=2)
-            copy(
-                w1_bf[a, b][:, t0 : t0 + 2, :, :].rearrange("p t m x -> p m x t"),
-                w1_raw[a, b][:].rearrange("p x (m t) -> p m x t", t=PACK)[:, :, :, t0 : t0 + 2],
+        def gather_words(side):
+            entries = slice(side * BANK // PER_COLUMN, (side + 1) * BANK // PER_COLUMN)
+            nc.vector.tensor_copy(
+                v_words[1][:, BANK * side : BANK * (side + 1)],
+                word_window[1][:].bitcast(U32).indirect(offs_sb[:, entries]),
             )
 
-        def quantize_w1(a, b, t0, t1):
-            if (a, b) not in w1_code:
+        w1_code, w1_scale = {}, {}
+        for a in range(PASSES):
+            for b in range(PASSES):
                 w1_code[a, b] = sbuf("w1_code%d%d" % (a, b), [P, PASS], U32)
                 w1_scale[a, b] = sbuf("w1_scale%d%d" % (a, b), [P, PASS], U8)
-            cols = slice(P * t0, P * t1)
+
+        def quantize_piece(n, a):
+            c0, c1 = PIECES[n]
+            rounded = sbuf("piece_bf%d%d" % (n, a), [P, c1 - c0, PACK], BF16)
+            nc.scalar.copy(
+                rounded[:].rearrange("p (c u) x -> p c x u", u=4),
+                piece_raw[n, a][:].rearrange("p x (c u) -> p c x u", u=4),
+            )
             nc.vector.quantize_mx(
-                out=w1_code[a, b][:, cols].bitcast(FP8X4),
-                scales=w1_scale[a, b][:, cols],
-                in_=w1_bf[a, b][:, t0:t1, :, :].rearrange("p t m x -> p (t m x)"),
+                out=w1_code[a, 0][:, c0:c1].bitcast(FP8X4),
+                scales=w1_scale[a, 0][:, c0:c1],
+                in_=rounded[:].rearrange("p c x -> p (c x)"),
+            )
+
+        def quantize_dealt(a):
+            rounded = sbuf("w1_bf%d" % a, [P, PACK, P, PACK], BF16)
+            for t0 in range(0, PACK, 2):
+                nc.scalar.copy(
+                    rounded[:, t0 : t0 + 2, :, :].rearrange("p t m x -> p m x t"),
+                    w1_raw[a][:].rearrange("p x (m t) -> p m x t", t=PACK)[:, :, :, t0 : t0 + 2],
+                )
+            nc.vector.quantize_mx(
+                out=w1_code[a, 1][:].bitcast(FP8X4),
+                scales=w1_scale[a, 1][:],
+                in_=rounded[:].rearrange("p t m x -> p (t m x)"),
             )
 
         h, h_acc = {}, {}
 
-        def multiply_h(b, t, first_bank):
+        def multiply_h(b, t):
             h[b, t] = sbuf("h%d%d" % (b, t), [P, S], F32)
-            h_acc[b, t] = [bank(first_bank + side, [P, BANK], "h_acc%d%d%d" % (b, t, side)) for side in range(2)]
+            h_acc[b, t] = [bank(2 * t + side, [P, BANK], "h_acc%d%d%d" % (b, t, side)) for side in range(2)]
             rows = slice(P * t, P * (t + 1))
             for a in range(PASSES):
                 for side in range(2):
@@ -157,14 +207,14 @@ def tile_list_grasp_pair_wrench_kernel(
                     )
 
         def add_bias(b, t, side):
-            bias = b1_sb[:, b, t : t + 1]
+            bias = bias_of[b, t]
             cols = slice(BANK * side, BANK * (side + 1))
             if (b, t, side) == (0, 0, 1):
                 nc.vector.tensor_scalar(h[b, t][:, cols], h_acc[b, t][side][:], bias, None, ALU.add)
             else:
                 nc.scalar.activation(h[b, t][:, cols], h_acc[b, t][side][:], ACT.Identity, bias=bias)
 
-        z_code = {1: sbuf("z_code1", [P, PAIRS], U32)}
+        z_code = [sbuf("z_code%d" % b, [P, PAIRS], U32) for b in range(PASSES)]
         z_scale = sbuf("z_scale", [P, PASSES, PAIRS], U8)
 
         fingers = {}
@@ -187,6 +237,26 @@ def tile_list_grasp_pair_wrench_kernel(
             )
             return z_bf
 
+        z_planes = sbuf("z_planes", [P, PACK, PAIRS], BF16)
+
+        def plain_max(q0, tag):
+            z_plain = sbuf("z_plain%d" % q0, [P, 2, PAIRS], BF16, tag=tag)
+            nc.vector.tensor_tensor(
+                z_plain[:], fingers[0, 0][:, q0 : q0 + 2, :], fingers[0, 1][:, q0 : q0 + 2, :], ALU.max
+            )
+            for e in range(2):
+                q = q0 + e
+                for t in range(PACK):
+                    nc.sync.dma_start(out=z_planes[32 * q : 32 * (q + 1), t, :], in_=z_plain[t:P:PACK, e, :])
+
+        def weave_planes():
+            z_bf = sbuf("z_bf0", [P, PAIRS, PACK], BF16)
+            nc.scalar.copy(
+                z_bf[:].rearrange("p (c u) t -> p c t u", u=4),
+                z_planes[:].rearrange("p t (c u) -> p c t u", u=4),
+            )
+            return z_bf
+
         def quantize_z(z_bf, b, j0, j1):
             nc.vector.quantize_mx(
                 out=z_code[b][:, j0:j1].bitcast(FP8X4),
@@ -199,11 +269,10 @@ def tile_list_grasp_pair_wrench_kernel(
         ws_scale = sbuf("ws_scale", [P, COUPLES, PASSES, 2 * P], U8)
 
         def round_ws(q):
-            for b in range(PASSES):
-                nc.scalar.copy(
-                    ws_bf[q][:, b, :, :].rearrange("p (c u) x -> p c x u", u=4),
-                    ws_raw[b][:, :, 2 * P * q : 2 * P * (q + 1)].rearrange("p x (c u) -> p c x u", u=4),
-                )
+            nc.scalar.copy(
+                ws_bf[q][:].rearrange("p b (c u) x -> p b c x u", u=4),
+                ws_raw[q][:].rearrange("p b x (c u) -> p b c x u", u=4),
+            )
 
         def quantize_ws(q):
             nc.vector.quantize_mx(
@@ -214,10 +283,10 @@ def tile_list_grasp_pair_wrench_kernel(
 
         m_acc, g_acc, gates = {}, {}, {}
 
-        def multiply_z(half, q, b, first_bank=None):
+        def multiply_z(half, q, b, banks=None):
             if b == 0:
-                m_acc[half, q] = bank(first_bank, [P, 2, HALF], "m_acc%d%d" % (half, q))
-                g_acc[half, q] = bank(first_bank + 1, [P, 2, HALF], "g_acc%d%d" % (half, q))
+                m_acc[half, q] = bank(banks[0], [P, 2, HALF], "m_acc%d%d" % (half, q))
+                g_acc[half, q] = bank(banks[1], [P, 2, HALF], "g_acc%d%d" % (half, q))
             j0 = HALF * half
             for e in range(2):
                 nc.tensor.matmul_mx(
@@ -244,7 +313,7 @@ def tile_list_grasp_pair_wrench_kernel(
                     )
 
         def gate(half, q):
-            gates[half, q] = sbuf("gate%d%d" % (half, q), [P, 2, HALF], F32)
+            gates[half, q] = sbuf("gate%d%d" % (half, q), [P, 2, HALF], F32, tag="h%d%d" % (half, q))
             for e in range(2):
                 c = 2 * q + e
                 nc.scalar.activation(
@@ -259,61 +328,61 @@ def tile_list_grasp_pair_wrench_kernel(
                 out=out[rows, HALF * half : HALF * (half + 1)].rearrange("(e p) j -> p e j", p=P), in_=result
             )
 
-        for a in range(PASSES):
-            round_w1(a, 0, 0, nc.vector.tensor_copy)
-            round_w1(a, 0, 2, nc.scalar.copy)
-            quantize_w1(a, 0, 0, 2)
-            quantize_w1(a, 0, 2, PACK)
-        for t in range(PACK):
-            if t >= 2:
-                round_w1(t - 2, 1, 0, nc.scalar.copy)
-                round_w1(t - 2, 1, 2, nc.scalar.copy)
-                quantize_w1(t - 2, 1, 0, PACK)
-            multiply_h(0, t, 2 * (t % 2))
-            add_bias(0, t, 0)
-            add_bias(0, t, 1)
-            gather_fingers(0, t, 0, PAIRS)
-        z_bf = pair_max(0, 0, PAIRS)
+        def tile_of_h(b, t, j1=PAIRS):
+            multiply_h(b, t)
+            add_bias(b, t, 0)
+            add_bias(b, t, 1)
+            gather_fingers(b, t, 0, j1)
 
-        for t in range(2):
-            round_ws(t)
-            quantize_ws(t)
-            multiply_h(1, t, 4 + 2 * t)
-            add_bias(1, t, 0)
-            add_bias(1, t, 1)
-            gather_fingers(1, t, 0, PAIRS)
+        for a in range(PASSES):
+            quantize_piece(0, a)
+        gather_words(0)
+        gather_words(1)
+        for a in range(PASSES):
+            quantize_piece(1, a)
+        tile_of_h(0, 0)
+        for a in range(PASSES):
+            quantize_piece(2, a)
+        tile_of_h(0, 1)
+        quantize_dealt(0)
+        plain_max(0, "w1_raw0")
+        tile_of_h(0, 2)
+        quantize_dealt(1)
+        tile_of_h(0, 3)
+        round_ws(0)
+        quantize_ws(0)
+        plain_max(2, "ws_raw0")
+        load_bias(1, 3, 4)
+        tile_of_h(1, 0)
+        tile_of_h(1, 1)
+        round_ws(1)
+        quantize_ws(1)
+        tile_of_h(1, 2)
         round_ws(2)
         quantize_ws(2)
-        z_code[0] = sbuf("z_code0", [P, PAIRS], U32, tag="ws_bf2")
-        quantize_z(z_bf, 0, 0, PAIRS)
-        multiply_h(1, 2, 0)
-        multiply_h(1, 3, 2)
-        for t, side in ((2, 0), (3, 0), (3, 1), (2, 1)):
-            add_bias(1, t, side)
+        quantize_z(weave_planes(), 0, 0, PAIRS)
+        tile_of_h(1, 3, HALF)
 
         for q in range(COUPLES):
-            multiply_z(0, q, 0, (4 + 2 * q) % BANKS)
-        gather_fingers(1, 3, 0, HALF)
-        gather_fingers(1, 2, 0, HALF)
+            multiply_z(0, q, 0, (2 * q, 2 * q + 1))
         z_bf = pair_max(1, 0, HALF)
         quantize_z(z_bf, 1, 0, HALF)
         for q in range(COUPLES):
             multiply_z(0, q, 1)
             gate(0, q)
-        multiply_z(1, 0, 0, 2)
+        multiply_z(1, 0, 0, (6, 7))
 
         gather_fingers(1, 3, HALF, PAIRS)
-        gather_fingers(1, 2, HALF, PAIRS)
-        finish(0, 0)
-        multiply_z(1, 1, 0, 4)
+        multiply_z(1, 1, 0, (1, 3))
         z_bf = pair_max(1, HALF, PAIRS)
-        finish(0, 1)
-        multiply_z(1, 2, 0, 6)
+        finish(0, 0)
+        multiply_z(1, 2, 0, (5, 0))
         quantize_z(z_bf, 1, HALF, PAIRS)
+        finish(0, 1)
+        finish(0, 2)
         for q in range(COUPLES):
             multiply_z(1, q, 1)
             gate(1, q)
-        finish(0, 2)
         finish(1, 0)
         finish(1, 1)
         finish(1, 2, 0, 1)

@@ -77,9 +77,9 @@ def tile_list_grasp_pair_wrench_kernel(
 
         piece_raw = {}
 
-        def load_piece(n):
+        def load_piece(n, passes=range(PASSES)):
             c0, c1 = PIECES[n]
-            for a in range(PASSES):
+            for a in passes:
                 piece_raw[n, a] = sbuf("piece_raw%d%d" % (n, a), [P, PACK, c1 - c0], F32)
                 nc.sync.dma_start(
                     out=piece_raw[n, a][:],
@@ -105,18 +105,17 @@ def tile_list_grasp_pair_wrench_kernel(
                 in_=w1[PASS * a : PASS * (a + 1), PASS:H].rearrange("(p x) c -> p x c", x=PACK),
             )
 
-        ws_raw = []
+        ws_raw = [sbuf("ws_raw%d" % q, [P, PASSES, PACK, 2 * P], F32) for q in range(COUPLES)]
 
-        def load_ws(q):
-            ws_raw.append(sbuf("ws_raw%d" % q, [P, PASSES, PACK, 2 * P], F32))
-            for b in range(PASSES):
-                nc.sync.dma_start(
-                    out=ws_raw[q][:, b, :, :],
-                    in_=ws[PASS * b : PASS * (b + 1), 2 * P * q : 2 * P * (q + 1)].rearrange("(p x) n -> p x n", x=PACK),
-                )
+        def load_ws(q, b):
+            nc.sync.dma_start(
+                out=ws_raw[q][:, b, :, :],
+                in_=ws[PASS * b : PASS * (b + 1), 2 * P * q : 2 * P * (q + 1)].rearrange("(p x) n -> p x n", x=PACK),
+            )
 
-        load_piece(0)
+        load_piece(0, (0,))
         load_words(1, 0, T)
+        load_piece(0, (1,))
         load_piece(1)
         load_bias(0, 0, 1)
         nc.sync.dma_start(pos1_sb[:], pos1)
@@ -127,11 +126,12 @@ def tile_list_grasp_pair_wrench_kernel(
         load_bias(0, 2, 3)
         load_dealt(1)
         load_bias(0, 3, 4)
-        load_ws(0)
+        load_ws(0, 0)
+        load_ws(0, 1)
         load_bias(1, 0, 2)
-        load_ws(1)
-        load_bias(1, 2, 3)
-        load_ws(2)
+        load_ws(1, 0)
+        load_ws(1, 1)
+        load_ws(2, 0)
         wm_sb = sbuf("wm_sb", [P, PASSES, 2 * N], U8)
         nc.sync.dma_start(out=wm_sb[:].bitcast(I32), in_=wm_words.bitcast(I32).rearrange("b p w -> p b w"))
         for quad in range(QUADS):
@@ -144,16 +144,18 @@ def tile_list_grasp_pair_wrench_kernel(
             nc.sync.dma_start(out=bs_sb[:], in_=bs.rearrange("(c p) -> p c", p=P))
 
         v_scale = sbuf("v_scale", [P, S], U8)
-        v_words = [sbuf("v_words%d" % a, [P, S], U32) for a in range(PASSES)]
-        nc.vector.tensor_copy(v_words[0][:], word_window[0][:].bitcast(U32).indirect(offs_sb[:]))
+        v_words = {}
+        words_0 = sbuf("v_words0", [P, S], U32)
+        nc.vector.tensor_copy(words_0[:], word_window[0][:].bitcast(U32).indirect(offs_sb[:]))
         nc.vector.tensor_copy(v_scale[:], scale_window[:].bitcast(U8).indirect(offs_sb[:]))
+        for side in range(2):
+            v_words[0, side] = words_0[:, BANK * side : BANK * (side + 1)]
 
-        def gather_words(side):
+        def gather_words(side, tag=""):
             entries = slice(side * BANK // PER_COLUMN, (side + 1) * BANK // PER_COLUMN)
-            nc.vector.tensor_copy(
-                v_words[1][:, BANK * side : BANK * (side + 1)],
-                word_window[1][:].bitcast(U32).indirect(offs_sb[:, entries]),
-            )
+            words = sbuf("v_words1%d" % side, [P, BANK], U32, tag=tag)
+            nc.vector.tensor_copy(words[:], word_window[1][:].bitcast(U32).indirect(offs_sb[:, entries]))
+            v_words[1, side] = words[:]
 
         w1_code, w1_scale = {}, {}
         for a in range(PASSES):
@@ -200,7 +202,7 @@ def tile_list_grasp_pair_wrench_kernel(
                         out=h_acc[b, t][side][:],
                         lhsT=w1_code[a, b][:, rows].bitcast(FP8X4),
                         lhsT_scale=w1_scale[a, b][:, rows],
-                        rhs=v_words[a][:, cols].bitcast(FP8X4),
+                        rhs=v_words[a, side].bitcast(FP8X4),
                         rhs_scale=v_scale[4 * a : P, cols],
                         start=(a == 0),
                         stop=(a == PASSES - 1),
@@ -239,15 +241,12 @@ def tile_list_grasp_pair_wrench_kernel(
 
         z_planes = sbuf("z_planes", [P, PACK, PAIRS], BF16)
 
-        def plain_max(q0, tag):
-            z_plain = sbuf("z_plain%d" % q0, [P, 2, PAIRS], BF16, tag=tag)
-            nc.vector.tensor_tensor(
-                z_plain[:], fingers[0, 0][:, q0 : q0 + 2, :], fingers[0, 1][:, q0 : q0 + 2, :], ALU.max
-            )
-            for e in range(2):
-                q = q0 + e
+        def plain_max(q0, q1, tag):
+            z_plain = sbuf("z_plain%d" % q0, [P, q1 - q0, PAIRS], BF16, tag=tag)
+            nc.vector.tensor_tensor(z_plain[:], fingers[0, 0][:, q0:q1, :], fingers[0, 1][:, q0:q1, :], ALU.max)
+            for q in range(q0, q1):
                 for t in range(PACK):
-                    nc.sync.dma_start(out=z_planes[32 * q : 32 * (q + 1), t, :], in_=z_plain[t:P:PACK, e, :])
+                    nc.sync.dma_start(out=z_planes[32 * q : 32 * (q + 1), t, :], in_=z_plain[t:P:PACK, q - q0, :])
 
         def weave_planes():
             z_bf = sbuf("z_bf0", [P, PAIRS, PACK], BF16)
@@ -268,10 +267,10 @@ def tile_list_grasp_pair_wrench_kernel(
         ws_code = sbuf("ws_code", [P, COUPLES, PASSES, 2 * P], U32)
         ws_scale = sbuf("ws_scale", [P, COUPLES, PASSES, 2 * P], U8)
 
-        def round_ws(q):
+        def round_ws(q, b0=0, b_end=PASSES):
             nc.scalar.copy(
-                ws_bf[q][:].rearrange("p b (c u) x -> p b c x u", u=4),
-                ws_raw[q][:].rearrange("p b x (c u) -> p b c x u", u=4),
+                ws_bf[q][:, b0:b_end, :, :].rearrange("p b (c u) x -> p b c x u", u=4),
+                ws_raw[q][:, b0:b_end, :, :].rearrange("p b x (c u) -> p b c x u", u=4),
             )
 
         def quantize_ws(q):
@@ -283,25 +282,28 @@ def tile_list_grasp_pair_wrench_kernel(
 
         m_acc, g_acc, gates = {}, {}, {}
 
-        def multiply_z(half, q, b, banks=None):
+        def multiply_g(half, q, b, number=None):
             if b == 0:
-                m_acc[half, q] = bank(banks[0], [P, 2, HALF], "m_acc%d%d" % (half, q))
-                g_acc[half, q] = bank(banks[1], [P, 2, HALF], "g_acc%d%d" % (half, q))
-            j0 = HALF * half
+                g_acc[half, q] = bank(number, [P, 2, HALF], "g_acc%d%d" % (half, q))
+            cols = slice(HALF * half, HALF * (half + 1))
             for e in range(2):
                 nc.tensor.matmul_mx(
                     out=g_acc[half, q][:, e, :],
                     lhsT=ws_code[:, q, b, P * e : P * (e + 1)].bitcast(FP8X4),
                     lhsT_scale=ws_scale[:, q, b, P * e : P * (e + 1)],
-                    rhs=z_code[b][:, j0 : j0 + HALF].bitcast(FP8X4),
-                    rhs_scale=z_scale[:, b, j0 : j0 + HALF],
+                    rhs=z_code[b][:, cols].bitcast(FP8X4),
+                    rhs_scale=z_scale[:, b, cols],
                     start=(b, e) == (0, 0),
                     stop=(b, e) == (1, 1),
                 )
+
+        def multiply_m(half, q, b, number=None):
+            if b == 0:
+                m_acc[half, q] = bank(number, [P, 2, HALF], "m_acc%d%d" % (half, q))
             for e in range(2):
                 c = 2 * q + e
                 for piece in range(HALF // P):
-                    cols = slice(j0 + P * piece, j0 + P * (piece + 1))
+                    cols = slice(HALF * half + P * piece, HALF * half + P * (piece + 1))
                     nc.tensor.matmul_mx(
                         out=m_acc[half, q][:, e, P * piece : P * (piece + 1)],
                         lhsT=wm_sb[:, b, 2 * P * c : 2 * P * (c + 1)].bitcast(FP4X4),
@@ -311,6 +313,18 @@ def tile_list_grasp_pair_wrench_kernel(
                         start=(b, e, piece) == (0, 0, 0),
                         stop=(b, e, piece) == (1, 1, 1),
                     )
+
+        def first_pass(half, q, m_bank, g_bank):
+            multiply_g(half, q, 0, g_bank)
+            multiply_m(half, q, 0, m_bank)
+
+        def second_pass(half):
+            multiply_g(half, 0, 1)
+            for q in range(COUPLES):
+                gate(half, q)
+                if q + 1 < COUPLES:
+                    multiply_g(half, q + 1, 1)
+                multiply_m(half, q, 1)
 
         def gate(half, q):
             gates[half, q] = sbuf("gate%d%d" % (half, q), [P, 2, HALF], F32, tag="h%d%d" % (half, q))
@@ -334,10 +348,10 @@ def tile_list_grasp_pair_wrench_kernel(
             add_bias(b, t, 1)
             gather_fingers(b, t, 0, j1)
 
-        for a in range(PASSES):
-            quantize_piece(0, a)
+        quantize_piece(0, 0)
         gather_words(0)
-        gather_words(1)
+        quantize_piece(0, 1)
+        gather_words(1, "piece_raw01")
         for a in range(PASSES):
             quantize_piece(1, a)
         tile_of_h(0, 0)
@@ -345,44 +359,45 @@ def tile_list_grasp_pair_wrench_kernel(
             quantize_piece(2, a)
         tile_of_h(0, 1)
         quantize_dealt(0)
-        plain_max(0, "w1_raw0")
+        plain_max(0, 2, "w1_raw0")
         tile_of_h(0, 2)
         quantize_dealt(1)
+        plain_max(2, 3, "w1_raw1")
         tile_of_h(0, 3)
         round_ws(0)
         quantize_ws(0)
-        plain_max(2, "ws_raw0")
-        load_bias(1, 3, 4)
+        plain_max(3, 4, "ws_raw0")
+        load_bias(1, 2, 4)
+        load_ws(2, 1)
         tile_of_h(1, 0)
         tile_of_h(1, 1)
         round_ws(1)
         quantize_ws(1)
-        tile_of_h(1, 2)
-        round_ws(2)
-        quantize_ws(2)
+        round_ws(2, 0, 1)
         quantize_z(weave_planes(), 0, 0, PAIRS)
         tile_of_h(1, 3, HALF)
+        tile_of_h(1, 2, HALF)
+        round_ws(2, 1, 2)
+        quantize_ws(2)
 
-        for q in range(COUPLES):
-            multiply_z(0, q, 0, (2 * q, 2 * q + 1))
+        first_pass(0, 0, 0, 1)
+        first_pass(0, 1, 2, 3)
+        first_pass(1, 0, 6, 7)
+        first_pass(0, 2, 4, 5)
         z_bf = pair_max(1, 0, HALF)
         quantize_z(z_bf, 1, 0, HALF)
-        for q in range(COUPLES):
-            multiply_z(0, q, 1)
-            gate(0, q)
-        multiply_z(1, 0, 0, (6, 7))
+        second_pass(0)
 
         gather_fingers(1, 3, HALF, PAIRS)
-        multiply_z(1, 1, 0, (1, 3))
+        gather_fingers(1, 2, HALF, PAIRS)
+        first_pass(1, 1, 1, 3)
         z_bf = pair_max(1, HALF, PAIRS)
         finish(0, 0)
-        multiply_z(1, 2, 0, (5, 0))
+        first_pass(1, 2, 0, 5)
         quantize_z(z_bf, 1, HALF, PAIRS)
         finish(0, 1)
         finish(0, 2)
-        for q in range(COUPLES):
-            multiply_z(1, q, 1)
-            gate(1, q)
+        second_pass(1)
         finish(1, 0)
         finish(1, 1)
         finish(1, 2, 0, 1)

@@ -105,12 +105,12 @@ def tile_list_grasp_pair_wrench_kernel(
                 in_=w1[PASS * a : PASS * (a + 1), PASS:H].rearrange("(p x) c -> p x c", x=PACK),
             )
 
-        ws_raw = [sbuf("ws_raw%d" % q, [P, PASSES, PACK, 2 * P], F32) for q in range(COUPLES)]
+        ws_raw = []
 
-        def load_ws(q, b):
+        def load_ws(b):
+            ws_raw.append(sbuf("ws_raw%d" % b, [P, PACK, N], F32))
             nc.sync.dma_start(
-                out=ws_raw[q][:, b, :, :],
-                in_=ws[PASS * b : PASS * (b + 1), 2 * P * q : 2 * P * (q + 1)].rearrange("(p x) n -> p x n", x=PACK),
+                out=ws_raw[b][:], in_=ws[PASS * b : PASS * (b + 1), :].rearrange("(p x) n -> p x n", x=PACK)
             )
 
         load_piece(0, (0,))
@@ -126,22 +126,21 @@ def tile_list_grasp_pair_wrench_kernel(
         load_bias(0, 2, 3)
         load_dealt(1)
         load_bias(0, 3, 4)
-        load_ws(0, 0)
-        load_ws(0, 1)
+        load_ws(0)
         load_bias(1, 0, 2)
-        load_ws(1, 0)
-        load_ws(1, 1)
-        load_ws(2, 0)
+        load_ws(1)
         wm_sb = sbuf("wm_sb", [P, PASSES, 2 * N], U8)
-        nc.sync.dma_start(out=wm_sb[:].bitcast(I32), in_=wm_words.bitcast(I32).rearrange("b p w -> p b w"))
-        for quad in range(QUADS):
-            nc.sync.dma_start(
-                out=wm_scale[32 * quad : 32 * quad + 4, :, :],
-                in_=wm_scales[:, 4 * quad : 4 * quad + 4, :].bitcast(I32).rearrange("b row w -> row b w"),
-            )
         bs_sb = sbuf("bs_sb", [P, N // P], F32)
-        with nc.allow_non_contiguous_dma(reason="one bias value for each partition and output tile"):
-            nc.sync.dma_start(out=bs_sb[:], in_=bs.rearrange("(c p) -> p c", p=P))
+
+        def load_wm_and_bs():
+            nc.sync.dma_start(out=wm_sb[:].bitcast(I32), in_=wm_words.bitcast(I32).rearrange("b p w -> p b w"))
+            for quad in range(QUADS):
+                nc.sync.dma_start(
+                    out=wm_scale[32 * quad : 32 * quad + 4, :, :],
+                    in_=wm_scales[:, 4 * quad : 4 * quad + 4, :].bitcast(I32).rearrange("b row w -> row b w"),
+                )
+            with nc.allow_non_contiguous_dma(reason="one bias value for each partition and output tile"):
+                nc.sync.dma_start(out=bs_sb[:], in_=bs.rearrange("(c p) -> p c", p=P))
 
         v_scale = sbuf("v_scale", [P, S], U8)
         v_words = {}
@@ -263,21 +262,19 @@ def tile_list_grasp_pair_wrench_kernel(
                 in_=z_bf[:].rearrange("p j t -> p (j t)"),
             )
 
-        ws_bf = [sbuf("ws_bf%d" % q, [P, PASSES, 2 * P, PACK], BF16) for q in range(COUPLES)]
-        ws_code = sbuf("ws_code", [P, COUPLES, PASSES, 2 * P], U32)
-        ws_scale = sbuf("ws_scale", [P, COUPLES, PASSES, 2 * P], U8)
+        ws_code = sbuf("ws_code", [P, PASSES, N], U32)
+        ws_scale = sbuf("ws_scale", [P, PASSES, N], U8)
 
-        def round_ws(q, b0=0, b_end=PASSES):
+        def quantize_ws(b, n0, n1, tag=""):
+            rounded = sbuf("ws_bf%d_%d" % (b, n0), [P, n1 - n0, PACK], BF16, tag=tag)
             nc.scalar.copy(
-                ws_bf[q][:, b0:b_end, :, :].rearrange("p b (c u) x -> p b c x u", u=4),
-                ws_raw[q][:, b0:b_end, :, :].rearrange("p b x (c u) -> p b c x u", u=4),
+                rounded[:].rearrange("p (c u) x -> p c x u", u=4),
+                ws_raw[b][:, :, n0:n1].rearrange("p x (c u) -> p c x u", u=4),
             )
-
-        def quantize_ws(q):
             nc.vector.quantize_mx(
-                out=ws_code[:, q, :, :].rearrange("p b n -> p (b n)").bitcast(FP8X4),
-                scales=ws_scale[:, q, :, :].rearrange("p b n -> p (b n)"),
-                in_=ws_bf[q][:].rearrange("p b n x -> p (b n x)"),
+                out=ws_code[:, b, n0:n1].bitcast(FP8X4),
+                scales=ws_scale[:, b, n0:n1],
+                in_=rounded[:].rearrange("p n x -> p (n x)"),
             )
 
         m_acc, g_acc, gates = {}, {}, {}
@@ -287,10 +284,11 @@ def tile_list_grasp_pair_wrench_kernel(
                 g_acc[half, q] = bank(number, [P, 2, HALF], "g_acc%d%d" % (half, q))
             cols = slice(HALF * half, HALF * (half + 1))
             for e in range(2):
+                rows = slice(P * (2 * q + e), P * (2 * q + e + 1))
                 nc.tensor.matmul_mx(
                     out=g_acc[half, q][:, e, :],
-                    lhsT=ws_code[:, q, b, P * e : P * (e + 1)].bitcast(FP8X4),
-                    lhsT_scale=ws_scale[:, q, b, P * e : P * (e + 1)],
+                    lhsT=ws_code[:, b, rows].bitcast(FP8X4),
+                    lhsT_scale=ws_scale[:, b, rows],
                     rhs=z_code[b][:, cols].bitcast(FP8X4),
                     rhs_scale=z_scale[:, b, cols],
                     start=(b, e) == (0, 0),
@@ -363,22 +361,19 @@ def tile_list_grasp_pair_wrench_kernel(
         tile_of_h(0, 2)
         quantize_dealt(1)
         plain_max(2, 3, "w1_raw1")
+        load_wm_and_bs()
         tile_of_h(0, 3)
-        round_ws(0)
-        quantize_ws(0)
-        plain_max(3, 4, "ws_raw0")
+        plain_max(3, 4, "")
         load_bias(1, 2, 4)
-        load_ws(2, 1)
+        quantize_ws(0, 0, 4 * P)
         tile_of_h(1, 0)
         tile_of_h(1, 1)
-        round_ws(1)
-        quantize_ws(1)
-        round_ws(2, 0, 1)
+        quantize_ws(1, 0, 4 * P)
+        quantize_ws(0, 4 * P, N)
         quantize_z(weave_planes(), 0, 0, PAIRS)
         tile_of_h(1, 3, HALF)
         tile_of_h(1, 2, HALF)
-        round_ws(2, 1, 2)
-        quantize_ws(2)
+        quantize_ws(1, 4 * P, N, "z_planes")
 
         first_pass(0, 0, 0, 1)
         first_pass(0, 1, 2, 3)

@@ -120,15 +120,15 @@ def tile_list_grasp_pair_wrench_kernel(
         load_bias(0, 0, 1)
         nc.sync.dma_start(pos1_sb[:], pos1)
         nc.sync.dma_start(pos2_sb[:], pos2)
-        load_piece(2)
+        load_piece(2, (0,))
         load_bias(0, 1, 2)
+        load_piece(2, (1,))
         load_dealt(0)
         load_bias(0, 2, 3)
         load_dealt(1)
         load_bias(0, 3, 4)
         load_ws(0)
         load_bias(1, 0, 2)
-        load_ws(1)
         wm_sb = sbuf("wm_sb", [P, PASSES, 2 * N], U8)
         bs_sb = sbuf("bs_sb", [P, N // P], F32)
 
@@ -175,17 +175,19 @@ def tile_list_grasp_pair_wrench_kernel(
                 in_=rounded[:].rearrange("p c x -> p (c x)"),
             )
 
+        dealt_bf = [sbuf("w1_bf%d" % a, [P, PACK, P, PACK], BF16) for a in range(PASSES)]
+
+        def round_dealt(a, t0):
+            nc.scalar.copy(
+                dealt_bf[a][:, t0 : t0 + 2, :, :].rearrange("p t m x -> p m x t"),
+                w1_raw[a][:].rearrange("p x (m t) -> p m x t", t=PACK)[:, :, :, t0 : t0 + 2],
+            )
+
         def quantize_dealt(a):
-            rounded = sbuf("w1_bf%d" % a, [P, PACK, P, PACK], BF16)
-            for t0 in range(0, PACK, 2):
-                nc.scalar.copy(
-                    rounded[:, t0 : t0 + 2, :, :].rearrange("p t m x -> p m x t"),
-                    w1_raw[a][:].rearrange("p x (m t) -> p m x t", t=PACK)[:, :, :, t0 : t0 + 2],
-                )
             nc.vector.quantize_mx(
                 out=w1_code[a, 1][:].bitcast(FP8X4),
                 scales=w1_scale[a, 1][:],
-                in_=rounded[:].rearrange("p t m x -> p (t m x)"),
+                in_=dealt_bf[a][:].rearrange("p t m x -> p (t m x)"),
             )
 
         h, h_acc = {}, {}
@@ -195,6 +197,18 @@ def tile_list_grasp_pair_wrench_kernel(
             h_acc[b, t] = [bank(2 * t + side, [P, BANK], "h_acc%d%d%d" % (b, t, side)) for side in range(2)]
             rows = slice(P * t, P * (t + 1))
             for a in range(PASSES):
+                if (b, t, a) == (0, 0, 1):
+                    warm = bank(7, [P, BANK], "warm")
+                    for repeat in range(2):
+                        nc.tensor.matmul_mx(
+                            out=warm[:],
+                            lhsT=w1_code[0, 0][:, rows].bitcast(FP8X4),
+                            lhsT_scale=w1_scale[0, 0][:, rows],
+                            rhs=v_words[1, 0].bitcast(FP8X4),
+                            rhs_scale=v_scale[4:P, 0:BANK],
+                            start=True,
+                            stop=True,
+                        )
                 for side in range(2):
                     cols = slice(BANK * side, BANK * (side + 1))
                     nc.tensor.matmul_mx(
@@ -218,34 +232,44 @@ def tile_list_grasp_pair_wrench_kernel(
         z_code = [sbuf("z_code%d" % b, [P, PAIRS], U32) for b in range(PASSES)]
         z_scale = sbuf("z_scale", [P, PASSES, PAIRS], U8)
 
-        fingers = {}
-        for b in range(PASSES):
-            for f in range(2):
-                fingers[b, f] = sbuf("finger%d%d" % (b, f), [P, PACK, PAIRS], F32)
+        fingers = [sbuf("finger%d" % f, [P, PACK, PAIRS], F32) for f in range(2)]
+        plain_fingers = {}
 
-        def gather_fingers(b, t, j0, j1):
+        def gather(picked, b, t, f, j0, j1):
             entries = slice(j0 // PER_COLUMN, j1 // PER_COLUMN)
-            for f, pos_sb in enumerate((pos1_sb, pos2_sb)):
-                nc.vector.tensor_copy(fingers[b, f][:, t, j0:j1], h[b, t][:].indirect(pos_sb[:, entries]))
+            nc.vector.tensor_copy(picked, h[b, t][:].indirect((pos1_sb, pos2_sb)[f][:, entries]))
+
+        def gather_plain(q, f, tag=""):
+            plain_fingers[q, f] = sbuf("plain_finger%d%d" % (q, f), [P, PAIRS], F32, tag=tag)
+            gather(plain_fingers[q, f][:], 0, q, f, 0, PAIRS)
+
+        def gather_fingers(t, j0, j1):
+            for f in range(2):
+                gather(fingers[f][:, t, j0:j1], 1, t, f, j0, j1)
 
         def pair_max(b, j0, j1):
             z_bf = sbuf("z_bf%d_%d" % (b, j0), [P, j1 - j0, PACK], BF16)
             nc.vector.tensor_tensor(
                 z_bf[:].rearrange("p (c u) t -> p c t u", u=2),
-                fingers[b, 0][:, :, j0:j1].rearrange("p t (c u) -> p c t u", u=2),
-                fingers[b, 1][:, :, j0:j1].rearrange("p t (c u) -> p c t u", u=2),
+                fingers[0][:, :, j0:j1].rearrange("p t (c u) -> p c t u", u=2),
+                fingers[1][:, :, j0:j1].rearrange("p t (c u) -> p c t u", u=2),
                 ALU.max,
             )
             return z_bf
 
         z_planes = sbuf("z_planes", [P, PACK, PAIRS], BF16)
 
-        def plain_max(q0, q1, tag):
-            z_plain = sbuf("z_plain%d" % q0, [P, q1 - q0, PAIRS], BF16, tag=tag)
-            nc.vector.tensor_tensor(z_plain[:], fingers[0, 0][:, q0:q1, :], fingers[0, 1][:, q0:q1, :], ALU.max)
-            for q in range(q0, q1):
-                for t in range(PACK):
-                    nc.sync.dma_start(out=z_planes[32 * q : 32 * (q + 1), t, :], in_=z_plain[t:P:PACK, q - q0, :])
+        def plain_max(q, tag=""):
+            z_plain = sbuf("z_plain%d" % q, [P, PAIRS], BF16, tag=tag)
+            nc.vector.tensor_tensor(z_plain[:], plain_fingers[q, 0][:], plain_fingers[q, 1][:], ALU.max)
+            z_moves.append((q, z_plain))
+
+        z_moves = []
+
+        def move_z(q):
+            z_plain = dict(z_moves)[q]
+            for t in range(PACK):
+                nc.sync.dma_start(out=z_planes[32 * q : 32 * (q + 1), t, :], in_=z_plain[t:P:PACK, :])
 
         def weave_planes():
             z_bf = sbuf("z_bf0", [P, PAIRS, PACK], BF16)
@@ -265,25 +289,24 @@ def tile_list_grasp_pair_wrench_kernel(
         ws_code = sbuf("ws_code", [P, PASSES, N], U32)
         ws_scale = sbuf("ws_scale", [P, PASSES, N], U8)
 
-        def quantize_ws(b, n0, n1, tag=""):
-            rounded = sbuf("ws_bf%d_%d" % (b, n0), [P, n1 - n0, PACK], BF16, tag=tag)
+        def quantize_ws(b, n0, n1, rounded):
             nc.scalar.copy(
-                rounded[:].rearrange("p (c u) x -> p c x u", u=4),
+                rounded.rearrange("p (c u) x -> p c x u", u=4),
                 ws_raw[b][:, :, n0:n1].rearrange("p x (c u) -> p c x u", u=4),
             )
             nc.vector.quantize_mx(
                 out=ws_code[:, b, n0:n1].bitcast(FP8X4),
                 scales=ws_scale[:, b, n0:n1],
-                in_=rounded[:].rearrange("p n x -> p (n x)"),
+                in_=rounded.rearrange("p n x -> p (n x)"),
             )
 
         m_acc, g_acc, gates = {}, {}, {}
 
-        def multiply_g(half, q, b, number=None):
+        def multiply_g(half, q, b, number=None, tiles=range(2)):
             if b == 0:
                 g_acc[half, q] = bank(number, [P, 2, HALF], "g_acc%d%d" % (half, q))
             cols = slice(HALF * half, HALF * (half + 1))
-            for e in range(2):
+            for e in tiles:
                 rows = slice(P * (2 * q + e), P * (2 * q + e + 1))
                 nc.tensor.matmul_mx(
                     out=g_acc[half, q][:, e, :],
@@ -295,10 +318,10 @@ def tile_list_grasp_pair_wrench_kernel(
                     stop=(b, e) == (1, 1),
                 )
 
-        def multiply_m(half, q, b, number=None):
+        def multiply_m(half, q, b, number=None, tiles=range(2)):
             if b == 0:
                 m_acc[half, q] = bank(number, [P, 2, HALF], "m_acc%d%d" % (half, q))
-            for e in range(2):
+            for e in tiles:
                 c = 2 * q + e
                 for piece in range(HALF // P):
                     cols = slice(HALF * half + P * piece, HALF * half + P * (piece + 1))
@@ -320,9 +343,10 @@ def tile_list_grasp_pair_wrench_kernel(
             multiply_g(half, 0, 1)
             for q in range(COUPLES):
                 gate(half, q)
+                multiply_m(half, q, 1, tiles=(0,))
                 if q + 1 < COUPLES:
                     multiply_g(half, q + 1, 1)
-                multiply_m(half, q, 1)
+                multiply_m(half, q, 1, tiles=(1,))
 
         def gate(half, q):
             gates[half, q] = sbuf("gate%d%d" % (half, q), [P, 2, HALF], F32, tag="h%d%d" % (half, q))
@@ -340,51 +364,73 @@ def tile_list_grasp_pair_wrench_kernel(
                 out=out[rows, HALF * half : HALF * (half + 1)].rearrange("(e p) j -> p e j", p=P), in_=result
             )
 
-        def tile_of_h(b, t, j1=PAIRS):
+        def tile_of_h(b, t):
             multiply_h(b, t)
             add_bias(b, t, 0)
             add_bias(b, t, 1)
-            gather_fingers(b, t, 0, j1)
+
+        def dealt_tile(t, j1=PAIRS):
+            tile_of_h(1, t)
+            gather_fingers(t, 0, j1)
 
         quantize_piece(0, 0)
         gather_words(0)
+        gather_words(1)
         quantize_piece(0, 1)
-        gather_words(1, "piece_raw01")
         for a in range(PASSES):
             quantize_piece(1, a)
         tile_of_h(0, 0)
-        for a in range(PASSES):
-            quantize_piece(2, a)
+        gather_plain(0, 0)
+        gather_plain(0, 1)
+        quantize_piece(2, 0)
+        plain_max(0, "piece_raw20")
         tile_of_h(0, 1)
-        quantize_dealt(0)
-        plain_max(0, 2, "w1_raw0")
+        gather_plain(1, 0)
+        quantize_piece(2, 1)
+        gather_plain(1, 1, "piece_raw21")
+        plain_max(1)
+        move_z(0)
+        move_z(1)
+        load_ws(1)
+        load_bias(1, 2, 3)
+        round_dealt(0, 0)
         tile_of_h(0, 2)
+        gather_plain(2, 0)
+        gather_plain(2, 1)
+        round_dealt(0, 2)
+        quantize_dealt(0)
+        plain_max(2, "w1_raw0")
+        move_z(2)
+        round_dealt(1, 0)
+        round_dealt(1, 2)
         quantize_dealt(1)
-        plain_max(2, 3, "w1_raw1")
-        load_wm_and_bs()
         tile_of_h(0, 3)
-        plain_max(3, 4, "")
-        load_bias(1, 2, 4)
-        quantize_ws(0, 0, 4 * P)
-        tile_of_h(1, 0)
-        tile_of_h(1, 1)
-        quantize_ws(1, 0, 4 * P)
-        quantize_ws(0, 4 * P, N)
+        gather_plain(3, 0)
+        gather_plain(3, 1)
+        plain_max(3)
+        move_z(3)
+        load_bias(1, 3, 4)
+        load_wm_and_bs()
+        ws_bf = sbuf("ws_bf", [P, PASSES, 4 * P, PACK], BF16)
+        quantize_ws(0, 0, 4 * P, ws_bf[:, 0, :, :])
+        dealt_tile(0)
+        dealt_tile(1)
+        quantize_ws(1, 0, 4 * P, ws_bf[:, 1, :, :])
+        dealt_tile(2)
         quantize_z(weave_planes(), 0, 0, PAIRS)
-        tile_of_h(1, 3, HALF)
-        tile_of_h(1, 2, HALF)
-        quantize_ws(1, 4 * P, N, "z_planes")
-
+        dealt_tile(3, HALF)
+        ws_last = sbuf("ws_last", [P, PASSES, 2 * P, PACK], BF16, tag="z_planes")
+        quantize_ws(0, 4 * P, N, ws_last[:, 0, :, :])
         first_pass(0, 0, 0, 1)
         first_pass(0, 1, 2, 3)
         first_pass(1, 0, 6, 7)
         first_pass(0, 2, 4, 5)
         z_bf = pair_max(1, 0, HALF)
+        quantize_ws(1, 4 * P, N, ws_last[:, 1, :, :])
         quantize_z(z_bf, 1, 0, HALF)
         second_pass(0)
 
-        gather_fingers(1, 3, HALF, PAIRS)
-        gather_fingers(1, 2, HALF, PAIRS)
+        gather_fingers(3, HALF, PAIRS)
         first_pass(1, 1, 1, 3)
         z_bf = pair_max(1, HALF, PAIRS)
         finish(0, 0)
@@ -393,7 +439,6 @@ def tile_list_grasp_pair_wrench_kernel(
         finish(0, 1)
         finish(0, 2)
         second_pass(1)
-        finish(1, 0)
-        finish(1, 1)
-        finish(1, 2, 0, 1)
-        finish(1, 2, 1, 2)
+        for q in range(COUPLES):
+            for e in range(2):
+                finish(1, q, e, e + 1)

@@ -52,6 +52,9 @@ def tile_list_grasp_pair_wrench_kernel(
         wm_scale = sbuf("wm_scale", [P, PASSES, N // 4], I32)
         nc.vector.memset(scale_window[:], 0)
         nc.vector.memset(wm_scale[:], 0)
+        table_warm = sbuf("table_warm", [P, 2], F32)
+        nc.vector.memset(table_warm[:, 0:1], 0.0)
+        nc.scalar.activation(table_warm[:, 1:2], table_warm[:, 0:1], ACT.Sigmoid)
         word_window = [sbuf("word_window%d" % a, [P, T], I32) for a in range(PASSES)]
 
         def load_words(a, t0, t1):

@@ -51,6 +51,8 @@ def tile_list_grasp_pair_wrench_kernel(
         scale_window = sbuf("scale_window", [P, T // 4], I32)
         wm_scale = sbuf("wm_scale", [P, PASSES, N // 4], I32)
         nc.vector.memset(scale_window[:], 0)
+        v_scale = sbuf("v_scale", [P, S], U8)
+        nc.vector.memset(v_scale[:].bitcast(I32), 0)
         nc.vector.memset(wm_scale[:], 0)
         table_warm = sbuf("table_warm", [P, 2], F32)
         nc.vector.memset(table_warm[:, 0:1], 0.0)
@@ -63,20 +65,10 @@ def tile_list_grasp_pair_wrench_kernel(
                 in_=tab_words[a].rearrange("p t x -> p (t x)").bitcast(I32)[:, t0:t1],
             )
 
-        def load_scale_rows(row):
-            for a in range(PASSES):
-                nc.sync.dma_start(
-                    out=scale_window[4 * a + row : P : 32, :],
-                    in_=tab_scales[a, row:16:4, :].bitcast(I32),
-                )
-
         load_words(0, 0, FIRST_WORDS)
         nc.sync.dma_start(offs_sb[:], offs)
-        load_scale_rows(0)
-        load_scale_rows(1)
+        nc.sync.dma_start(out=scale_window[0:P:4, :], in_=tab_scales.rearrange("a g t -> (a g) t").bitcast(I32))
         load_words(0, FIRST_WORDS, T)
-        load_scale_rows(2)
-        load_scale_rows(3)
 
         piece_raw = {}
 
@@ -145,11 +137,17 @@ def tile_list_grasp_pair_wrench_kernel(
             with nc.allow_non_contiguous_dma(reason="one bias value for each partition and output tile"):
                 nc.sync.dma_start(out=bs_sb[:], in_=bs.rearrange("(c p) -> p c", p=P))
 
-        v_scale = sbuf("v_scale", [P, S], U8)
+        picked_scale = sbuf("picked_scale", [P, S], U8)
+        nc.vector.tensor_copy(picked_scale[:], scale_window[:].bitcast(U8).indirect(offs_sb[:]))
+        for a in range(PASSES):
+            for row in range(4):
+                nc.scalar.dma_start(
+                    out=v_scale[4 * a + row : P : 32, :].bitcast(I32),
+                    in_=picked_scale[64 * a + 4 * row : 64 * (a + 1) : 16, :].bitcast(I32),
+                )
         v_words = {}
         words_0 = sbuf("v_words0", [P, S], U32)
         nc.vector.tensor_copy(words_0[:], word_window[0][:].bitcast(U32).indirect(offs_sb[:]))
-        nc.vector.tensor_copy(v_scale[:], scale_window[:].bitcast(U8).indirect(offs_sb[:]))
         for side in range(2):
             v_words[0, side] = words_0[:, BANK * side : BANK * (side + 1)]
 

@@ -163,10 +163,10 @@ def tile_list_grasp_pair_wrench_kernel(
                 w1_code[a, b] = sbuf("w1_code%d%d" % (a, b), [P, PASS], U32)
                 w1_scale[a, b] = sbuf("w1_scale%d%d" % (a, b), [P, PASS], U8)
 
-        def quantize_piece(n, a):
+        def quantize_piece(n, a, copy=nc.scalar.copy):
             c0, c1 = PIECES[n]
             rounded = sbuf("piece_bf%d%d" % (n, a), [P, c1 - c0, PACK], BF16)
-            nc.scalar.copy(
+            copy(
                 rounded[:].rearrange("p (c u) x -> p c x u", u=4),
                 piece_raw[n, a][:].rearrange("p x (c u) -> p c x u", u=4),
             )
@@ -374,7 +374,7 @@ def tile_list_grasp_pair_wrench_kernel(
             tile_of_h(1, t)
             gather_fingers(t, 0, j1)
 
-        quantize_piece(0, 0)
+        quantize_piece(0, 0, nc.vector.tensor_copy)
         gather_words(0)
         gather_words(1)
         quantize_piece(0, 1)

@@ -290,11 +290,17 @@ def tile_list_grasp_pair_wrench_kernel(
         ws_code = sbuf("ws_code", [P, PASSES, N], U32)
         ws_scale = sbuf("ws_scale", [P, PASSES, N], U8)
 
-        def quantize_ws(b, n0, n1, rounded):
-            nc.scalar.copy(
-                rounded.rearrange("p (c u) x -> p c x u", u=4),
-                ws_raw[b][:, :, n0:n1].rearrange("p x (c u) -> p c x u", u=4),
+        def round_ws_gpsimd(b, n0, n1, rounded):
+            nc.gpsimd.tensor_scalar(
+                rounded, ws_raw[b][:, :, n0:n1].rearrange("p x n -> p n x"), 1.0, 0.0, ALU.mult, ALU.add
             )
+
+        def quantize_ws(b, n0, n1, rounded, on_scalar=True):
+            if on_scalar:
+                nc.scalar.copy(
+                    rounded.rearrange("p (c u) x -> p c x u", u=4),
+                    ws_raw[b][:, :, n0:n1].rearrange("p x (c u) -> p c x u", u=4),
+                )
             nc.vector.quantize_mx(
                 out=ws_code[:, b, n0:n1].bitcast(FP8X4),
                 scales=ws_scale[:, b, n0:n1],
@@ -412,14 +418,17 @@ def tile_list_grasp_pair_wrench_kernel(
         move_z(3)
         load_bias(1, 3, 4)
         load_wm_and_bs()
-        ws_bf = sbuf("ws_bf", [P, PASSES, 4 * P, PACK], BF16)
-        quantize_ws(0, 0, 4 * P, ws_bf[:, 0, :, :])
+        ws_bf = sbuf("ws_bf0", [P, 4 * P, PACK], BF16, tag="plain_finger31")
+        round_ws_gpsimd(0, 0, 4 * P, ws_bf[:])
         dealt_tile(0)
         dealt_tile(1)
-        quantize_ws(1, 0, 4 * P, ws_bf[:, 1, :, :])
+        quantize_ws(0, 0, 4 * P, ws_bf[:], False)
+        ws_bf = sbuf("ws_bf1", [P, 4 * P, PACK], BF16, tag="plain_finger31")
+        round_ws_gpsimd(1, 0, 4 * P, ws_bf[:])
         dealt_tile(2)
         quantize_z(weave_planes(), 0, 0, PAIRS)
         dealt_tile(3, HALF)
+        quantize_ws(1, 0, 4 * P, ws_bf[:], False)
         ws_last = sbuf("ws_last", [P, PASSES, 2 * P, PACK], BF16, tag="z_planes")
         quantize_ws(0, 4 * P, N, ws_last[:, 0, :, :])
         first_pass(0, 0, 0, 1)

@@ -112,12 +112,12 @@ def tile_list_grasp_pair_wrench_kernel(
         load_words(1, 0, T)
         load_piece(0, (1,))
         load_piece(1)
-        load_bias(0, 0, 1)
         nc.sync.dma_start(pos1_sb[:], pos1)
+        load_bias(0, 0, 1)
         nc.sync.dma_start(pos2_sb[:], pos2)
         load_piece(2, (0,))
-        load_bias(0, 1, 2)
         load_piece(2, (1,))
+        load_bias(0, 1, 2)
         load_dealt(0)
         load_bias(0, 2, 3)
         load_dealt(1)
@@ -159,9 +159,8 @@ def tile_list_grasp_pair_wrench_kernel(
 
         w1_code, w1_scale = {}, {}
         for a in range(PASSES):
-            for b in range(PASSES):
-                w1_code[a, b] = sbuf("w1_code%d%d" % (a, b), [P, PASS], U32)
-                w1_scale[a, b] = sbuf("w1_scale%d%d" % (a, b), [P, PASS], U8)
+            w1_code[a, 0] = sbuf("w1_code%d" % a, [P, PASS], U32)
+            w1_scale[a, 0] = sbuf("w1_scale%d" % a, [P, PASS], U8)
 
         def quantize_piece(n, a, copy=nc.scalar.copy):
             c0, c1 = PIECES[n]
@@ -176,59 +175,69 @@ def tile_list_grasp_pair_wrench_kernel(
                 in_=rounded[:].rearrange("p c x -> p (c x)"),
             )
 
-        dealt_bf = [sbuf("w1_bf%d" % a, [P, PACK, P, PACK], BF16) for a in range(PASSES)]
+        dealt_bf = {}
+        dealt_code = [sbuf("dealt_code%d" % pair, [P, PASSES, 2 * P], U32) for pair in range(2)]
+        dealt_scale = [sbuf("dealt_scale%d" % pair, [P, PASSES, 2 * P], U8) for pair in range(2)]
 
-        def round_dealt(a, t0):
+        def round_dealt(a, pair):
             nc.scalar.copy(
-                dealt_bf[a][:, t0 : t0 + 2, :, :].rearrange("p t m x -> p m x t"),
-                w1_raw[a][:].rearrange("p x (m t) -> p m x t", t=PACK)[:, :, :, t0 : t0 + 2],
+                dealt_bf[pair][:, a, :, :, :].rearrange("p t m x -> p m x t"),
+                w1_raw[a][:].rearrange("p x (m t) -> p m x t", t=PACK)[:, :, :, 2 * pair : 2 * pair + 2],
             )
 
-        def quantize_dealt(a):
+        def quantize_dealt(pair):
             nc.vector.quantize_mx(
-                out=w1_code[a, 1][:].bitcast(FP8X4),
-                scales=w1_scale[a, 1][:],
-                in_=dealt_bf[a][:].rearrange("p t m x -> p (t m x)"),
+                out=dealt_code[pair][:].rearrange("p a c -> p (a c)").bitcast(FP8X4),
+                scales=dealt_scale[pair][:].rearrange("p a c -> p (a c)"),
+                in_=dealt_bf[pair][:].rearrange("p a t m x -> p (a t m x)"),
             )
 
-        h, h_acc = {}, {}
+        def stationary(a, b, t):
+            if b == 0:
+                rows = slice(P * t, P * (t + 1))
+                return w1_code[a, 0][:, rows], w1_scale[a, 0][:, rows]
+            rows = slice(P * (t % 2), P * (t % 2 + 1))
+            return dealt_code[t // 2][:, a, rows], dealt_scale[t // 2][:, a, rows]
 
-        def multiply_h(b, t):
+        h = {}
+
+        def tile_of_h(b, t):
             h[b, t] = sbuf("h%d%d" % (b, t), [P, S], F32)
-            h_acc[b, t] = [bank(2 * t + side, [P, BANK], "h_acc%d%d%d" % (b, t, side)) for side in range(2)]
-            rows = slice(P * t, P * (t + 1))
+            first = (b, t) == (0, 0)
+            banks = (0, 5, 1, 6) if first else (2 * t, 2 * t + 1)
+            width = S // len(banks)
+            accs = [bank(number, [P, width], "h_acc%d%d%d" % (b, t, number)) for number in banks]
             for a in range(PASSES):
-                if (b, t, a) == (0, 0, 1):
+                codes, scales = stationary(a, b, t)
+                if first and a == 1:
                     warm = bank(7, [P, BANK], "warm")
                     for repeat in range(2):
                         nc.tensor.matmul_mx(
                             out=warm[:],
-                            lhsT=w1_code[0, 0][:, rows].bitcast(FP8X4),
-                            lhsT_scale=w1_scale[0, 0][:, rows],
+                            lhsT=w1_code[0, 0][:, 0:P].bitcast(FP8X4),
+                            lhsT_scale=w1_scale[0, 0][:, 0:P],
                             rhs=v_words[1, 0].bitcast(FP8X4),
                             rhs_scale=v_scale[4:P, 0:BANK],
                             start=True,
                             stop=True,
                         )
-                for side in range(2):
-                    cols = slice(BANK * side, BANK * (side + 1))
+                for part, acc in enumerate(accs):
+                    side, within = divmod(part * width, BANK)
                     nc.tensor.matmul_mx(
-                        out=h_acc[b, t][side][:],
-                        lhsT=w1_code[a, b][:, rows].bitcast(FP8X4),
-                        lhsT_scale=w1_scale[a, b][:, rows],
-                        rhs=v_words[a, side].bitcast(FP8X4),
-                        rhs_scale=v_scale[4 * a : P, cols],
+                        out=acc[:],
+                        lhsT=codes.bitcast(FP8X4),
+                        lhsT_scale=scales,
+                        rhs=v_words[a, side][:, within : within + width].bitcast(FP8X4),
+                        rhs_scale=v_scale[4 * a : P, part * width : (part + 1) * width],
                         start=(a == 0),
                         stop=(a == PASSES - 1),
                     )
-
-        def add_bias(b, t, side):
-            bias = bias_of[b, t]
-            cols = slice(BANK * side, BANK * (side + 1))
-            if (b, t, side) == (0, 0, 1):
-                nc.vector.tensor_scalar(h[b, t][:, cols], h_acc[b, t][side][:], bias, None, ALU.add)
-            else:
-                nc.scalar.activation(h[b, t][:, cols], h_acc[b, t][side][:], ACT.Identity, bias=bias)
+            for part, acc in enumerate(accs):
+                cols = slice(part * width, (part + 1) * width)
+                if first and part % 2:
+                    nc.vector.tensor_scalar(h[b, t][:, cols], acc[:], bias_of[b, t], None, ALU.add)
+                else:
+                    nc.scalar.activation(h[b, t][:, cols], acc[:], ACT.Identity, bias=bias_of[b, t])
 
         z_code = [sbuf("z_code%d" % b, [P, PAIRS], U32) for b in range(PASSES)]
         z_scale = sbuf("z_scale", [P, PASSES, PAIRS], U8)
@@ -249,7 +258,7 @@ def tile_list_grasp_pair_wrench_kernel(
                 gather(fingers[f][:, t, j0:j1], 1, t, f, j0, j1)
 
         def pair_max(b, j0, j1):
-            z_bf = sbuf("z_bf%d_%d" % (b, j0), [P, j1 - j0, PACK], BF16)
+            z_bf = sbuf("z_bf%d_%d" % (b, j0), [P, j1 - j0, PACK], BF16, tag="z_bf1")
             nc.vector.tensor_tensor(
                 z_bf[:].rearrange("p (c u) t -> p c t u", u=2),
                 fingers[0][:, :, j0:j1].rearrange("p t (c u) -> p c t u", u=2),
@@ -371,11 +380,6 @@ def tile_list_grasp_pair_wrench_kernel(
                 out=out[rows, HALF * half : HALF * (half + 1)].rearrange("(e p) j -> p e j", p=P), in_=result
             )
 
-        def tile_of_h(b, t):
-            multiply_h(b, t)
-            add_bias(b, t, 0)
-            add_bias(b, t, 1)
-
         def dealt_tile(t, j1=PAIRS):
             tile_of_h(1, t)
             gather_fingers(t, 0, j1)
@@ -390,65 +394,74 @@ def tile_list_grasp_pair_wrench_kernel(
         gather_plain(0, 0)
         gather_plain(0, 1)
         quantize_piece(2, 0)
-        plain_max(0, "piece_raw20")
+        quantize_piece(2, 1)
+        plain_max(0, "piece_raw21")
         tile_of_h(0, 1)
         gather_plain(1, 0)
-        quantize_piece(2, 1)
-        gather_plain(1, 1, "piece_raw21")
+        gather_plain(1, 1)
         plain_max(1)
         move_z(0)
         move_z(1)
         load_ws(1)
         load_bias(1, 2, 3)
+        dealt_bf[0] = sbuf("w1_bf0", [P, PASSES, 2, P, PACK], BF16)
         round_dealt(0, 0)
         tile_of_h(0, 2)
         gather_plain(2, 0)
         gather_plain(2, 1)
-        round_dealt(0, 2)
-        quantize_dealt(0)
-        plain_max(2, "w1_raw0")
-        move_z(2)
         round_dealt(1, 0)
-        round_dealt(1, 2)
-        quantize_dealt(1)
+        quantize_dealt(0)
         tile_of_h(0, 3)
+        plain_max(2, "w1_bf0")
+        move_z(2)
         gather_plain(3, 0)
         gather_plain(3, 1)
+        dealt_bf[1] = sbuf("w1_bf1", [P, PASSES, 2, P, PACK], BF16, tag="b1_03")
+        round_dealt(0, 1)
+        round_dealt(1, 1)
+        quantize_dealt(1)
         plain_max(3)
         move_z(3)
         load_bias(1, 3, 4)
         load_wm_and_bs()
-        ws_bf = sbuf("ws_bf0", [P, 4 * P, PACK], BF16, tag="plain_finger31")
-        round_ws_gpsimd(0, 0, 4 * P, ws_bf[:])
+        ws_bf = sbuf("ws_bf0", [P, N, PACK], BF16, tag="b1_03")
+        round_ws_gpsimd(0, 0, 4 * P, ws_bf[:, 0 : 4 * P, :])
+        round_ws_gpsimd(0, 4 * P, N, ws_bf[:, 4 * P : N, :])
         dealt_tile(0)
         dealt_tile(1)
-        quantize_ws(0, 0, 4 * P, ws_bf[:], False)
-        ws_bf = sbuf("ws_bf1", [P, 4 * P, PACK], BF16, tag="plain_finger31")
-        round_ws_gpsimd(1, 0, 4 * P, ws_bf[:])
+        quantize_ws(0, 0, 4 * P, ws_bf[:, 0 : 4 * P, :], False)
+        quantize_ws(0, 4 * P, N, ws_bf[:, 4 * P : N, :], False)
         dealt_tile(2)
         quantize_z(weave_planes(), 0, 0, PAIRS)
-        dealt_tile(3, HALF)
-        quantize_ws(1, 0, 4 * P, ws_bf[:], False)
-        ws_last = sbuf("ws_last", [P, PASSES, 2 * P, PACK], BF16, tag="z_planes")
-        quantize_ws(0, 4 * P, N, ws_last[:, 0, :, :])
-        first_pass(0, 0, 0, 1)
-        first_pass(0, 1, 2, 3)
-        first_pass(1, 0, 6, 7)
-        first_pass(0, 2, 4, 5)
+        dealt_tile(3)
+        ws_last = sbuf("ws_last", [P, N, PACK], BF16, tag="z_planes")
         z_bf = pair_max(1, 0, HALF)
-        quantize_ws(1, 4 * P, N, ws_last[:, 1, :, :])
+        quantize_ws(1, 0, 4 * P, ws_last[:, 0 : 4 * P, :])
+        for q in range(COUPLES):
+            multiply_g(0, q, 0, q)
+        for q in range(2):
+            multiply_m(0, q, 0, 3 + q)
+        for q in range(COUPLES):
+            multiply_g(1, q, 0, 5 + q)
         quantize_z(z_bf, 1, 0, HALF)
-        second_pass(0)
-
-        gather_fingers(3, HALF, PAIRS)
-        first_pass(1, 1, 1, 3)
+        quantize_ws(1, 4 * P, N, ws_last[:, 4 * P : N, :])
+        for q in range(COUPLES):
+            multiply_g(0, q, 1)
+            gate(0, q)
+            if q < 2:
+                multiply_m(0, q, 1)
         z_bf = pair_max(1, HALF, PAIRS)
         finish(0, 0)
-        first_pass(1, 2, 0, 5)
+        multiply_m(0, 2, 0, 0)
+        multiply_m(0, 2, 1)
         quantize_z(z_bf, 1, HALF, PAIRS)
-        finish(0, 1)
-        finish(0, 2)
-        second_pass(1)
+        for q in range(1, COUPLES):
+            finish(0, q)
+        for q in range(COUPLES):
+            multiply_g(1, q, 1)
+            gate(1, q)
+            multiply_m(1, q, 0, (1, 3, 4)[q])
+            multiply_m(1, q, 1)
         for q in range(COUPLES):
             for e in range(2):
                 finish(1, q, e, e + 1)

@@ -1,6 +1,7 @@
 from contextlib import ExitStack
 
 import concourse.mybir as mybir
+from concourse.masks import make_identity
 
 K, H, N, T, S, PAIRS = 1024, 1024, 768, 4096, 1024, 512
 FLOPS = 2 * K * H * S + 2 * 2 * H * N * PAIRS
@@ -83,6 +84,19 @@ def tile_list_grasp_pair_wrench_kernel(
 
         bias_of = {}
 
+        def load_first_biases():
+            rows = sbuf("bias_rows", [P, P], F32)
+            identity = sbuf("identity", [P, P], F32)
+            nc.gpsimd.memset(rows[:], 0.0)
+            make_identity(nc, identity[:])
+            nc.sync.dma_start(out=rows[0:2, :], in_=b1[0 : 2 * P].rearrange("(t p) -> t p", p=P))
+            turned = bank(4, [P, P], "turned")
+            nc.tensor.transpose(turned[:], rows[:], identity[:])
+            columns = sbuf("bias_columns", [P, 2], F32)
+            nc.scalar.copy(columns[:], turned[:, 0:2])
+            for t in range(2):
+                bias_of[0, t] = columns[:, t : t + 1]
+
         def load_bias(b, t0, t1):
             rows = b1[PASS * b : PASS * (b + 1)].rearrange("(p t) -> p t" if b else "(t p) -> p t", t=PACK)
             column = sbuf("b1_%d%d" % (b, t0), [P, t1 - t0], F32)
@@ -111,19 +125,18 @@ def tile_list_grasp_pair_wrench_kernel(
         load_piece(0, (0,))
         load_words(1, 0, T)
         load_piece(0, (1,))
+        load_first_biases()
         load_piece(1)
         nc.sync.dma_start(pos1_sb[:], pos1)
-        load_bias(0, 0, 1)
         nc.sync.dma_start(pos2_sb[:], pos2)
         load_piece(2, (0,))
         load_piece(2, (1,))
-        load_bias(0, 1, 2)
         load_dealt(0)
         load_bias(0, 2, 3)
         load_dealt(1)
         load_bias(0, 3, 4)
         load_ws(0)
-        load_bias(1, 0, 2)
+        load_bias(1, 0, 3)
         wm_sb = sbuf("wm_sb", [P, PASSES, 2 * N], U8)
         bs_sb = sbuf("bs_sb", [P, N // P], F32)
 
@@ -165,10 +178,15 @@ def tile_list_grasp_pair_wrench_kernel(
         def quantize_piece(n, a, copy=nc.scalar.copy):
             c0, c1 = PIECES[n]
             rounded = sbuf("piece_bf%d%d" % (n, a), [P, c1 - c0, PACK], BF16)
-            copy(
-                rounded[:].rearrange("p (c u) x -> p c x u", u=4),
-                piece_raw[n, a][:].rearrange("p x (c u) -> p c x u", u=4),
-            )
+            if copy is None:
+                nc.gpsimd.tensor_scalar(
+                    rounded[:], piece_raw[n, a][:].rearrange("p x c -> p c x"), 1.0, 0.0, ALU.mult, ALU.add
+                )
+            else:
+                copy(
+                    rounded[:].rearrange("p (c u) x -> p c x u", u=4),
+                    piece_raw[n, a][:].rearrange("p x (c u) -> p c x u", u=4),
+                )
             nc.vector.quantize_mx(
                 out=w1_code[a, 0][:, c0:c1].bitcast(FP8X4),
                 scales=w1_scale[a, 0][:, c0:c1],
@@ -201,8 +219,8 @@ def tile_list_grasp_pair_wrench_kernel(
 
         h = {}
 
-        def tile_of_h(b, t):
-            h[b, t] = sbuf("h%d%d" % (b, t), [P, S], F32)
+        def tile_of_h(b, t, tag=""):
+            h[b, t] = sbuf("h%d%d" % (b, t), [P, S], F32, tag=tag)
             first = (b, t) == (0, 0)
             banks = (0, 5, 1, 6) if first else (2 * t, 2 * t + 1)
             width = S // len(banks)
@@ -239,8 +257,7 @@ def tile_list_grasp_pair_wrench_kernel(
                 else:
                     nc.scalar.activation(h[b, t][:, cols], acc[:], ACT.Identity, bias=bias_of[b, t])
 
-        z_code = [sbuf("z_code%d" % b, [P, PAIRS], U32) for b in range(PASSES)]
-        z_scale = sbuf("z_scale", [P, PASSES, PAIRS], U8)
+        z_code, z_scale = {}, {}
 
         fingers = [sbuf("finger%d" % f, [P, PACK, PAIRS], F32) for f in range(2)]
         plain_fingers = {}
@@ -289,11 +306,13 @@ def tile_list_grasp_pair_wrench_kernel(
             )
             return z_bf
 
-        def quantize_z(z_bf, b, j0, j1):
+        def quantize_z(z_bf, b, half, tag=""):
+            z_code[b, half] = sbuf("z_code%d%d" % (b, half), [P, HALF], U32, tag=tag)
+            z_scale[b, half] = sbuf("z_scale%d%d" % (b, half), [P, HALF], U8)
             nc.vector.quantize_mx(
-                out=z_code[b][:, j0:j1].bitcast(FP8X4),
-                scales=z_scale[:, b, j0:j1],
-                in_=z_bf[:].rearrange("p j t -> p (j t)"),
+                out=z_code[b, half][:].bitcast(FP8X4),
+                scales=z_scale[b, half][:],
+                in_=z_bf.rearrange("p j t -> p (j t)"),
             )
 
         ws_code = sbuf("ws_code", [P, PASSES, N], U32)
@@ -321,15 +340,14 @@ def tile_list_grasp_pair_wrench_kernel(
         def multiply_g(half, q, b, number=None, tiles=range(2)):
             if b == 0:
                 g_acc[half, q] = bank(number, [P, 2, HALF], "g_acc%d%d" % (half, q))
-            cols = slice(HALF * half, HALF * (half + 1))
             for e in tiles:
                 rows = slice(P * (2 * q + e), P * (2 * q + e + 1))
                 nc.tensor.matmul_mx(
                     out=g_acc[half, q][:, e, :],
                     lhsT=ws_code[:, b, rows].bitcast(FP8X4),
                     lhsT_scale=ws_scale[:, b, rows],
-                    rhs=z_code[b][:, cols].bitcast(FP8X4),
-                    rhs_scale=z_scale[:, b, cols],
+                    rhs=z_code[b, half][:].bitcast(FP8X4),
+                    rhs_scale=z_scale[b, half][:],
                     start=(b, e) == (0, 0),
                     stop=(b, e) == (1, 1),
                 )
@@ -340,13 +358,13 @@ def tile_list_grasp_pair_wrench_kernel(
             for e in tiles:
                 c = 2 * q + e
                 for piece in range(HALF // P):
-                    cols = slice(HALF * half + P * piece, HALF * half + P * (piece + 1))
+                    cols = slice(P * piece, P * (piece + 1))
                     nc.tensor.matmul_mx(
                         out=m_acc[half, q][:, e, P * piece : P * (piece + 1)],
                         lhsT=wm_sb[:, b, 2 * P * c : 2 * P * (c + 1)].bitcast(FP4X4),
                         lhsT_scale=wm_scale[:, b, P // 4 * c : P // 4 * (c + 1)].bitcast(U8),
-                        rhs=z_code[b][:, cols].bitcast(FP8X4),
-                        rhs_scale=z_scale[:, b, cols],
+                        rhs=z_code[b, half][:, cols].bitcast(FP8X4),
+                        rhs_scale=z_scale[b, half][:, cols],
                         start=(b, e, piece) == (0, 0, 0),
                         stop=(b, e, piece) == (1, 1, 1),
                     )
@@ -388,22 +406,21 @@ def tile_list_grasp_pair_wrench_kernel(
         gather_words(0)
         gather_words(1)
         quantize_piece(0, 1)
-        for a in range(PASSES):
-            quantize_piece(1, a)
+        quantize_piece(1, 0)
+        quantize_piece(1, 1, None)
         tile_of_h(0, 0)
         gather_plain(0, 0)
         gather_plain(0, 1)
         quantize_piece(2, 0)
         quantize_piece(2, 1)
-        plain_max(0, "piece_raw21")
-        tile_of_h(0, 1)
+        plain_max(0, "piece_raw20")
+        tile_of_h(0, 1, "piece_raw21")
         gather_plain(1, 0)
         gather_plain(1, 1)
         plain_max(1)
         move_z(0)
         move_z(1)
         load_ws(1)
-        load_bias(1, 2, 3)
         dealt_bf[0] = sbuf("w1_bf0", [P, PASSES, 2, P, PACK], BF16)
         round_dealt(0, 0)
         tile_of_h(0, 2)
@@ -432,8 +449,10 @@ def tile_list_grasp_pair_wrench_kernel(
         quantize_ws(0, 0, 4 * P, ws_bf[:, 0 : 4 * P, :], False)
         quantize_ws(0, 4 * P, N, ws_bf[:, 4 * P : N, :], False)
         dealt_tile(2)
-        quantize_z(weave_planes(), 0, 0, PAIRS)
+        woven = weave_planes()
+        quantize_z(woven[:, 0:HALF, :], 0, 0)
         dealt_tile(3)
+        quantize_z(woven[:, HALF:PAIRS, :], 0, 1, "h13")
         ws_last = sbuf("ws_last", [P, N, PACK], BF16, tag="z_planes")
         z_bf = pair_max(1, 0, HALF)
         quantize_ws(1, 0, 4 * P, ws_last[:, 0 : 4 * P, :])
@@ -443,7 +462,7 @@ def tile_list_grasp_pair_wrench_kernel(
             multiply_m(0, q, 0, 3 + q)
         for q in range(COUPLES):
             multiply_g(1, q, 0, 5 + q)
-        quantize_z(z_bf, 1, 0, HALF)
+        quantize_z(z_bf[:], 1, 0)
         quantize_ws(1, 4 * P, N, ws_last[:, 4 * P : N, :])
         for q in range(COUPLES):
             multiply_g(0, q, 1)
@@ -454,7 +473,7 @@ def tile_list_grasp_pair_wrench_kernel(
         finish(0, 0)
         multiply_m(0, 2, 0, 0)
         multiply_m(0, 2, 1)
-        quantize_z(z_bf, 1, HALF, PAIRS)
+        quantize_z(z_bf[:], 1, 1)
         for q in range(1, COUPLES):
             finish(0, q)
         for q in range(COUPLES):

@@ -27,6 +27,7 @@ PER_COLUMN = 16
 HALF = PAIRS // 2
 COUPLES = N // (2 * P)
 FIRST_WORDS = 1536
+PLAIN_GROUPS = ((0, 1), (1, 2), (1, 2), (3, 1))
 PIECES = ((0, 128), (128, 256), (256, 512))
 
 
@@ -222,7 +223,7 @@ def tile_list_grasp_pair_wrench_kernel(
         def tile_of_h(b, t, tag=""):
             h[b, t] = sbuf("h%d%d" % (b, t), [P, S], F32, tag=tag)
             first = (b, t) == (0, 0)
-            banks = (0, 5, 1, 6) if first else (2 * t, 2 * t + 1)
+            banks = (0, 5, 1, 6) if first else (2, 3) if (b, t) == (0, 3) else (2 * t, 2 * t + 1)
             width = S // len(banks)
             accs = [bank(number, [P, width], "h_acc%d%d%d" % (b, t, number)) for number in banks]
             for a in range(PASSES):
@@ -267,8 +268,10 @@ def tile_list_grasp_pair_wrench_kernel(
             nc.vector.tensor_copy(picked, h[b, t][:].indirect((pos1_sb, pos2_sb)[f][:, entries]))
 
         def gather_plain(q, f, tag=""):
-            plain_fingers[q, f] = sbuf("plain_finger%d%d" % (q, f), [P, PAIRS], F32, tag=tag)
-            gather(plain_fingers[q, f][:], 0, q, f, 0, PAIRS)
+            first, count = PLAIN_GROUPS[q]
+            if q == first:
+                plain_fingers[first, f] = sbuf("plain_finger%d%d" % (q, f), [P, count, PAIRS], F32, tag=tag)
+            gather(plain_fingers[first, f][:, q - first, :], 0, q, f, 0, PAIRS)
 
         def gather_fingers(t, j0, j1):
             for f in range(2):
@@ -287,9 +290,11 @@ def tile_list_grasp_pair_wrench_kernel(
         z_planes = sbuf("z_planes", [P, PACK, PAIRS], BF16)
 
         def plain_max(q, tag=""):
-            z_plain = sbuf("z_plain%d" % q, [P, PAIRS], BF16, tag=tag)
+            count = PLAIN_GROUPS[q][1]
+            z_plain = sbuf("z_plain%d" % q, [P, count, PAIRS], BF16, tag=tag)
             nc.vector.tensor_tensor(z_plain[:], plain_fingers[q, 0][:], plain_fingers[q, 1][:], ALU.max)
-            z_moves.append((q, z_plain))
+            for i in range(count):
+                z_moves.append((q + i, z_plain[:, i, :]))
 
         z_moves = []
 
@@ -417,9 +422,7 @@ def tile_list_grasp_pair_wrench_kernel(
         tile_of_h(0, 1, "piece_raw21")
         gather_plain(1, 0)
         gather_plain(1, 1)
-        plain_max(1)
         move_z(0)
-        move_z(1)
         load_ws(1)
         dealt_bf[0] = sbuf("w1_bf0", [P, PASSES, 2, P, PACK], BF16)
         round_dealt(0, 0)
@@ -429,7 +432,8 @@ def tile_list_grasp_pair_wrench_kernel(
         round_dealt(1, 0)
         quantize_dealt(0)
         tile_of_h(0, 3)
-        plain_max(2, "w1_bf0")
+        plain_max(1, "w1_bf0")
+        move_z(1)
         move_z(2)
         gather_plain(3, 0)
         gather_plain(3, 1)
@@ -437,22 +441,22 @@ def tile_list_grasp_pair_wrench_kernel(
         round_dealt(0, 1)
         round_dealt(1, 1)
         quantize_dealt(1)
-        plain_max(3)
+        plain_max(3, "w1_raw1")
         move_z(3)
         load_bias(1, 3, 4)
         load_wm_and_bs()
-        ws_bf = sbuf("ws_bf0", [P, N, PACK], BF16, tag="b1_03")
-        round_ws_gpsimd(0, 0, 4 * P, ws_bf[:, 0 : 4 * P, :])
-        round_ws_gpsimd(0, 4 * P, N, ws_bf[:, 4 * P : N, :])
+        ws_bf = sbuf("ws_bf0", [P, 4 * P, PACK], BF16, tag="plain_finger31")
+        round_ws_gpsimd(0, 0, 4 * P, ws_bf[:])
         dealt_tile(0)
         dealt_tile(1)
-        quantize_ws(0, 0, 4 * P, ws_bf[:, 0 : 4 * P, :], False)
-        quantize_ws(0, 4 * P, N, ws_bf[:, 4 * P : N, :], False)
+        quantize_ws(0, 0, 4 * P, ws_bf[:], False)
+        ws_end = sbuf("ws_end", [P, 2 * P, PACK], BF16, tag="plain_finger30")
+        quantize_ws(0, 4 * P, N, ws_end[:])
         dealt_tile(2)
         woven = weave_planes()
         quantize_z(woven[:, 0:HALF, :], 0, 0)
         dealt_tile(3)
-        quantize_z(woven[:, HALF:PAIRS, :], 0, 1, "h13")
+        quantize_z(woven[:, HALF:PAIRS, :], 0, 1, "b1_13")
         ws_last = sbuf("ws_last", [P, N, PACK], BF16, tag="z_planes")
         z_bf = pair_max(1, 0, HALF)
         quantize_ws(1, 0, 4 * P, ws_last[:, 0 : 4 * P, :])

@@ -94,7 +94,7 @@ def tile_list_grasp_pair_wrench_kernel(
             turned = bank(4, [P, P], "turned")
             nc.tensor.transpose(turned[:], rows[:], identity[:])
             columns = sbuf("bias_columns", [P, 2], F32)
-            nc.scalar.copy(columns[:], turned[:, 0:2])
+            nc.vector.tensor_copy(columns[:], turned[:, 0:2])
             for t in range(2):
                 bias_of[0, t] = columns[:, t : t + 1]
 
@@ -176,9 +176,9 @@ def tile_list_grasp_pair_wrench_kernel(
             w1_code[a, 0] = sbuf("w1_code%d" % a, [P, PASS], U32)
             w1_scale[a, 0] = sbuf("w1_scale%d" % a, [P, PASS], U8)
 
-        def quantize_piece(n, a, copy=nc.scalar.copy):
+        def quantize_piece(n, a, copy=nc.scalar.copy, tag=""):
             c0, c1 = PIECES[n]
-            rounded = sbuf("piece_bf%d%d" % (n, a), [P, c1 - c0, PACK], BF16)
+            rounded = sbuf("piece_bf%d%d" % (n, a), [P, c1 - c0, PACK], BF16, tag=tag)
             if copy is None:
                 nc.gpsimd.tensor_scalar(
                     rounded[:], piece_raw[n, a][:].rearrange("p x c -> p c x"), 1.0, 0.0, ALU.mult, ALU.add
@@ -223,7 +223,7 @@ def tile_list_grasp_pair_wrench_kernel(
         def tile_of_h(b, t, tag=""):
             h[b, t] = sbuf("h%d%d" % (b, t), [P, S], F32, tag=tag)
             first = (b, t) == (0, 0)
-            banks = (0, 5, 1, 6) if first else (2, 3) if (b, t) == (0, 3) else (2 * t, 2 * t + 1)
+            banks = (0, 5, 1, 6) if first else (4, 5) if (b, t) == (0, 3) else (2 * t, 2 * t + 1)
             width = S // len(banks)
             accs = [bank(number, [P, width], "h_acc%d%d%d" % (b, t, number)) for number in banks]
             for a in range(PASSES):
@@ -303,13 +303,11 @@ def tile_list_grasp_pair_wrench_kernel(
             for t in range(PACK):
                 nc.sync.dma_start(out=z_planes[32 * q : 32 * (q + 1), t, :], in_=z_plain[t:P:PACK, :])
 
-        def weave_planes():
-            z_bf = sbuf("z_bf0", [P, PAIRS, PACK], BF16)
+        def weave_planes(z_bf):
             nc.scalar.copy(
-                z_bf[:].rearrange("p (c u) t -> p c t u", u=4),
+                z_bf.rearrange("p (c u) t -> p c t u", u=4),
                 z_planes[:].rearrange("p t (c u) -> p c t u", u=4),
             )
-            return z_bf
 
         def quantize_z(z_bf, b, half, tag=""):
             z_code[b, half] = sbuf("z_code%d%d" % (b, half), [P, HALF], U32, tag=tag)
@@ -320,8 +318,7 @@ def tile_list_grasp_pair_wrench_kernel(
                 in_=z_bf.rearrange("p j t -> p (j t)"),
             )
 
-        ws_code = sbuf("ws_code", [P, PASSES, N], U32)
-        ws_scale = sbuf("ws_scale", [P, PASSES, N], U8)
+        ws_q = {}
 
         def round_ws_gpsimd(b, n0, n1, rounded):
             nc.gpsimd.tensor_scalar(
@@ -334,11 +331,13 @@ def tile_list_grasp_pair_wrench_kernel(
                     rounded.rearrange("p (c u) x -> p c x u", u=4),
                     ws_raw[b][:, :, n0:n1].rearrange("p x (c u) -> p c x u", u=4),
                 )
+            codes = sbuf("ws_code%d_%d" % (b, n0), [P, n1 - n0], U32)
+            scales = sbuf("ws_scale%d_%d" % (b, n0), [P, n1 - n0], U8)
             nc.vector.quantize_mx(
-                out=ws_code[:, b, n0:n1].bitcast(FP8X4),
-                scales=ws_scale[:, b, n0:n1],
-                in_=rounded.rearrange("p n x -> p (n x)"),
+                out=codes[:].bitcast(FP8X4), scales=scales[:], in_=rounded.rearrange("p n x -> p (n x)")
             )
+            for c in range(n0 // P, n1 // P):
+                ws_q[b, c] = codes[:, P * c - n0 : P * (c + 1) - n0], scales[:, P * c - n0 : P * (c + 1) - n0]
 
         m_acc, g_acc, gates = {}, {}, {}
 
@@ -346,11 +345,10 @@ def tile_list_grasp_pair_wrench_kernel(
             if b == 0:
                 g_acc[half, q] = bank(number, [P, 2, HALF], "g_acc%d%d" % (half, q))
             for e in tiles:
-                rows = slice(P * (2 * q + e), P * (2 * q + e + 1))
                 nc.tensor.matmul_mx(
                     out=g_acc[half, q][:, e, :],
-                    lhsT=ws_code[:, b, rows].bitcast(FP8X4),
-                    lhsT_scale=ws_scale[:, b, rows],
+                    lhsT=ws_q[b, 2 * q + e][0].bitcast(FP8X4),
+                    lhsT_scale=ws_q[b, 2 * q + e][1],
                     rhs=z_code[b, half][:].bitcast(FP8X4),
                     rhs_scale=z_scale[b, half][:],
                     start=(b, e) == (0, 0),
@@ -412,16 +410,16 @@ def tile_list_grasp_pair_wrench_kernel(
         gather_words(1)
         quantize_piece(0, 1)
         quantize_piece(1, 0)
-        quantize_piece(1, 1, None)
-        tile_of_h(0, 0)
+        quantize_piece(1, 1)
+        tile_of_h(0, 0, "piece_raw11")
         gather_plain(0, 0)
         gather_plain(0, 1)
-        quantize_piece(2, 0)
+        tile_of_h(0, 1)
+        quantize_piece(2, 0, None, "piece_bf11")
         quantize_piece(2, 1)
-        plain_max(0, "piece_raw20")
-        tile_of_h(0, 1, "piece_raw21")
-        gather_plain(1, 0)
-        gather_plain(1, 1)
+        plain_max(0, "piece_raw21")
+        gather_plain(1, 0, "piece_bf21")
+        gather_plain(1, 1, "plain_finger00")
         move_z(0)
         load_ws(1)
         dealt_bf[0] = sbuf("w1_bf0", [P, PASSES, 2, P, PACK], BF16)
@@ -450,11 +448,24 @@ def tile_list_grasp_pair_wrench_kernel(
         dealt_tile(0)
         dealt_tile(1)
         quantize_ws(0, 0, 4 * P, ws_bf[:], False)
-        ws_end = sbuf("ws_end", [P, 2 * P, PACK], BF16, tag="plain_finger30")
-        quantize_ws(0, 4 * P, N, ws_end[:])
+        joined = sbuf("joined", [P, 2 * P + PAIRS, PACK], BF16, tag="plain_finger30")
+        nc.scalar.copy(
+            joined[:, 0 : 2 * P, :].rearrange("p (c u) x -> p c x u", u=4),
+            ws_raw[0][:, :, 4 * P : N].rearrange("p x (c u) -> p c x u", u=4),
+        )
         dealt_tile(2)
-        woven = weave_planes()
-        quantize_z(woven[:, 0:HALF, :], 0, 0)
+        woven = joined[:, 2 * P :, :]
+        weave_planes(woven)
+        codes = sbuf("joined_code", [P, 2 * P + HALF], U32)
+        scales = sbuf("joined_scale", [P, 2 * P + HALF], U8)
+        nc.vector.quantize_mx(
+            out=codes[:].bitcast(FP8X4),
+            scales=scales[:],
+            in_=joined[:, 0 : 2 * P + HALF, :].rearrange("p c x -> p (c x)"),
+        )
+        for e in range(2):
+            ws_q[0, 4 + e] = codes[:, P * e : P * (e + 1)], scales[:, P * e : P * (e + 1)]
+        z_code[0, 0], z_scale[0, 0] = codes[:, 2 * P :], scales[:, 2 * P :]
         dealt_tile(3)
         quantize_z(woven[:, HALF:PAIRS, :], 0, 1, "b1_13")
         ws_last = sbuf("ws_last", [P, N, PACK], BF16, tag="z_planes")
@@ -474,10 +485,11 @@ def tile_list_grasp_pair_wrench_kernel(
             if q < 2:
                 multiply_m(0, q, 1)
         z_bf = pair_max(1, HALF, PAIRS)
-        finish(0, 0)
+        finish(0, 0, 0, 1)
         multiply_m(0, 2, 0, 0)
         multiply_m(0, 2, 1)
         quantize_z(z_bf[:], 1, 1)
+        finish(0, 0, 1, 2)
         for q in range(1, COUPLES):
             finish(0, q)
         for q in range(COUPLES):

@@ -52,7 +52,8 @@ def tile_list_grasp_pair_wrench_kernel(
 
         scale_window = sbuf("scale_window", [P, T // 4], I32)
         wm_scale = sbuf("wm_scale", [P, PASSES, N // 4], I32)
-        nc.vector.memset(scale_window[:], 0)
+        nc.vector.memset(scale_window[32:64, :], 0)
+        nc.vector.memset(scale_window[64:P, :], 0)
         v_scale = sbuf("v_scale", [P, S], U8)
         nc.vector.memset(v_scale[:].bitcast(I32), 0)
         nc.vector.memset(wm_scale[:], 0)
@@ -67,10 +68,9 @@ def tile_list_grasp_pair_wrench_kernel(
                 in_=tab_words[a].rearrange("p t x -> p (t x)").bitcast(I32)[:, t0:t1],
             )
 
-        load_words(0, 0, FIRST_WORDS)
         nc.sync.dma_start(offs_sb[:], offs)
-        nc.sync.dma_start(out=scale_window[0:P:4, :], in_=tab_scales.rearrange("a g t -> (a g) t").bitcast(I32))
-        load_words(0, FIRST_WORDS, T)
+        nc.sync.dma_start(out=scale_window[0:32, :], in_=tab_scales.rearrange("a g t -> (a g) t").bitcast(I32))
+        load_words(0, 0, T)
 
         piece_raw = {}
 
@@ -157,7 +157,7 @@ def tile_list_grasp_pair_wrench_kernel(
             for row in range(4):
                 nc.scalar.dma_start(
                     out=v_scale[4 * a + row : P : 32, :].bitcast(I32),
-                    in_=picked_scale[64 * a + 4 * row : 64 * (a + 1) : 16, :].bitcast(I32),
+                    in_=picked_scale[16 * a + row : 16 * (a + 1) : 4, :].bitcast(I32),
                 )
         v_words = {}
         words_0 = sbuf("v_words0", [P, S], U32)

@@ -74,11 +74,11 @@ def tile_list_grasp_pair_wrench_kernel(
 
         piece_raw = {}
 
-        def load_piece(n, passes=range(PASSES)):
+        def load_piece(n, passes=range(PASSES), queue=nc.sync):
             c0, c1 = PIECES[n]
             for a in passes:
                 piece_raw[n, a] = sbuf("piece_raw%d%d" % (n, a), [P, PACK, c1 - c0], F32)
-                nc.sync.dma_start(
+                queue.dma_start(
                     out=piece_raw[n, a][:],
                     in_=w1[PASS * a : PASS * (a + 1), c0:c1].rearrange("(p x) c -> p x c", x=PACK),
                 )
@@ -123,7 +123,7 @@ def tile_list_grasp_pair_wrench_kernel(
                 out=ws_raw[b][:], in_=ws[PASS * b : PASS * (b + 1), :].rearrange("(p x) n -> p x n", x=PACK)
             )
 
-        load_piece(0, (0,))
+        load_piece(0, (0,), nc.scalar)
         load_words(1, 0, T)
         load_piece(0, (1,))
         load_first_biases()

@@ -57,9 +57,6 @@ def tile_list_grasp_pair_wrench_kernel(
         v_scale = sbuf("v_scale", [P, S], U8)
         nc.vector.memset(v_scale[:].bitcast(I32), 0)
         nc.vector.memset(wm_scale[:], 0)
-        table_warm = sbuf("table_warm", [P, 2], F32)
-        nc.vector.memset(table_warm[:, 0:1], 0.0)
-        nc.scalar.activation(table_warm[:, 1:2], table_warm[:, 0:1], ACT.Sigmoid)
         word_window = [sbuf("word_window%d" % a, [P, T], I32) for a in range(PASSES)]
 
         def load_words(a, t0, t1):
@@ -228,18 +225,6 @@ def tile_list_grasp_pair_wrench_kernel(
             accs = [bank(number, [P, width], "h_acc%d%d%d" % (b, t, number)) for number in banks]
             for a in range(PASSES):
                 codes, scales = stationary(a, b, t)
-                if first and a == 1:
-                    warm = bank(7, [P, BANK], "warm")
-                    for repeat in range(2):
-                        nc.tensor.matmul_mx(
-                            out=warm[:],
-                            lhsT=w1_code[0, 0][:, 0:P].bitcast(FP8X4),
-                            lhsT_scale=w1_scale[0, 0][:, 0:P],
-                            rhs=v_words[1, 0].bitcast(FP8X4),
-                            rhs_scale=v_scale[4:P, 0:BANK],
-                            start=True,
-                            stop=True,
-                        )
                 for part, acc in enumerate(accs):
                     side, within = divmod(part * width, BANK)
                     nc.tensor.matmul_mx(

@@ -54,8 +54,8 @@ def tile_list_grasp_pair_wrench_kernel(
         wm_scale = sbuf("wm_scale", [P, PASSES, N // 4], I32)
         nc.vector.memset(scale_window[32:64, :], 0)
         nc.vector.memset(scale_window[64:P, :], 0)
-        v_scale = sbuf("v_scale", [P, S], U8)
-        nc.vector.memset(v_scale[:].bitcast(I32), 0)
+        v_scale = sbuf("v_scale", [P, PASSES, S], U8)
+        nc.vector.memset(v_scale[:].rearrange("p a s -> p (a s)").bitcast(I32), 0)
         nc.vector.memset(wm_scale[:], 0)
         word_window = [sbuf("word_window%d" % a, [P, T], I32) for a in range(PASSES)]
 
@@ -66,7 +66,7 @@ def tile_list_grasp_pair_wrench_kernel(
             )
 
         nc.sync.dma_start(offs_sb[:], offs)
-        nc.sync.dma_start(out=scale_window[0:32, :], in_=tab_scales.rearrange("a g t -> (a g) t").bitcast(I32))
+        nc.sync.dma_start(out=scale_window[0:32, :], in_=tab_scales.bitcast(I32).rearrange("a g w -> g a w"))
         load_words(0, 0, T)
 
         piece_raw = {}
@@ -150,12 +150,11 @@ def tile_list_grasp_pair_wrench_kernel(
 
         picked_scale = sbuf("picked_scale", [P, S], U8)
         nc.vector.tensor_copy(picked_scale[:], scale_window[:].bitcast(U8).indirect(offs_sb[:]))
-        for a in range(PASSES):
-            for row in range(4):
-                nc.scalar.dma_start(
-                    out=v_scale[4 * a + row : P : 32, :].bitcast(I32),
-                    in_=picked_scale[16 * a + row : 16 * (a + 1) : 4, :].bitcast(I32),
-                )
+        for quad in range(QUADS):
+            nc.scalar.dma_start(
+                out=v_scale[32 * quad : 32 * quad + 4, :, :].bitcast(I32),
+                in_=picked_scale[8 * quad : 8 * quad + 8, :].bitcast(I32),
+            )
         v_words = {}
         words_0 = sbuf("v_words0", [P, S], U32)
         nc.vector.tensor_copy(words_0[:], word_window[0][:].bitcast(U32).indirect(offs_sb[:]))
@@ -232,7 +231,7 @@ def tile_list_grasp_pair_wrench_kernel(
                         lhsT=codes.bitcast(FP8X4),
                         lhsT_scale=scales,
                         rhs=v_words[a, side][:, within : within + width].bitcast(FP8X4),
-                        rhs_scale=v_scale[4 * a : P, part * width : (part + 1) * width],
+                        rhs_scale=v_scale[:, a, part * width : (part + 1) * width],
                         start=(a == 0),
                         stop=(a == PASSES - 1),
                     )

@@ -27,8 +27,7 @@ PER_COLUMN = 16
 HALF = PAIRS // 2
 COUPLES = N // (2 * P)
 FIRST_WORDS = 1536
-PLAIN_GROUPS = ((0, 1), (1, 2), (1, 2), (3, 1))
-PIECES = ((0, 128), (128, 256), (256, 512))
+PIECES = ((0, 128), (128, 256), (256, 512), (256, 384), (384, 512))
 
 
 def tile_list_grasp_pair_wrench_kernel(
@@ -82,18 +81,21 @@ def tile_list_grasp_pair_wrench_kernel(
 
         bias_of = {}
 
-        def load_first_biases():
+        def load_plain_biases():
             rows = sbuf("bias_rows", [P, P], F32)
             identity = sbuf("identity", [P, P], F32)
             nc.gpsimd.memset(rows[:], 0.0)
             make_identity(nc, identity[:])
-            nc.sync.dma_start(out=rows[0:2, :], in_=b1[0 : 2 * P].rearrange("(t p) -> t p", p=P))
+            nc.scalar.dma_start(out=rows[0:PACK, :], in_=b1[0:PASS].rearrange("(t p) -> t p", p=P))
             turned = bank(4, [P, P], "turned")
             nc.tensor.transpose(turned[:], rows[:], identity[:])
-            columns = sbuf("bias_columns", [P, 2], F32)
-            nc.vector.tensor_copy(columns[:], turned[:, 0:2])
-            for t in range(2):
-                bias_of[0, t] = columns[:, t : t + 1]
+            columns = sbuf("bias_columns", [P, PACK], F32)
+            nc.vector.tensor_copy(columns[:], turned[:, 0:PACK])
+            for t in range(PACK):
+                bias_of[0, t] = [columns[:, t : t + 1]] * 2
+            third = sbuf("bias_third", [P, 1], F32)
+            nc.vector.tensor_copy(third[:], turned[:, 2:3])
+            bias_of[0, 2] = [columns[:, 2:3], third[:]]
 
         def load_bias(b, t0, t1):
             rows = b1[PASS * b : PASS * (b + 1)].rearrange("(p t) -> p t" if b else "(t p) -> p t", t=PACK)
@@ -101,7 +103,7 @@ def tile_list_grasp_pair_wrench_kernel(
             with nc.allow_non_contiguous_dma(reason="one bias value for each partition and tile of h"):
                 nc.sync.dma_start(out=column[:], in_=rows[:, t0:t1])
             for t in range(t0, t1):
-                bias_of[b, t] = column[:, t - t0 : t - t0 + 1]
+                bias_of[b, t] = [column[:, t - t0 : t - t0 + 1]] * 2
 
         w1_raw = []
 
@@ -121,16 +123,16 @@ def tile_list_grasp_pair_wrench_kernel(
             )
 
         load_piece(0, (0,), nc.scalar)
+        load_plain_biases()
         load_words(1, 0, T)
         load_piece(0, (1,))
-        load_first_biases()
         load_piece(1)
         nc.sync.dma_start(pos1_sb[:], pos1)
         nc.sync.dma_start(pos2_sb[:], pos2)
         load_piece(2, (0,))
-        load_piece(2, (1,))
+        load_piece(3, (1,))
+        load_piece(4, (1,))
         load_dealt(0)
-        load_bias(0, 2, 3)
         load_dealt(1)
         load_bias(0, 3, 4)
         load_ws(0)
@@ -167,38 +169,51 @@ def tile_list_grasp_pair_wrench_kernel(
             nc.vector.tensor_copy(words[:], word_window[1][:].bitcast(U32).indirect(offs_sb[:, entries]))
             v_words[1, side] = words[:]
 
-        w1_code, w1_scale = {}, {}
-        for a in range(PASSES):
-            w1_code[a, 0] = sbuf("w1_code%d" % a, [P, PASS], U32)
-            w1_scale[a, 0] = sbuf("w1_scale%d" % a, [P, PASS], U8)
+        plain_code = [sbuf("plain_code%d" % q, [P, PASSES, P], U32) for q in range(PACK)]
+        plain_scale = [sbuf("plain_scale%d" % q, [P, PASSES, P], U8) for q in range(PACK)]
 
-        def quantize_piece(n, a, copy=nc.scalar.copy, tag=""):
-            c0, c1 = PIECES[n]
-            rounded = sbuf("piece_bf%d%d" % (n, a), [P, c1 - c0, PACK], BF16, tag=tag)
-            if copy is None:
-                nc.gpsimd.tensor_scalar(
-                    rounded[:], piece_raw[n, a][:].rearrange("p x c -> p c x"), 1.0, 0.0, ALU.mult, ALU.add
-                )
-            else:
-                copy(
-                    rounded[:].rearrange("p (c u) x -> p c x u", u=4),
-                    piece_raw[n, a][:].rearrange("p x (c u) -> p c x u", u=4),
-                )
+        def round_plain(engine, rounded, raw):
+            if engine is nc.gpsimd:
+                nc.gpsimd.tensor_scalar(rounded, raw.rearrange("p x c -> p c x"), 1.0, 0.0, ALU.mult, ALU.add)
+                return
+            copy = nc.scalar.copy if engine is nc.scalar else nc.vector.tensor_copy
+            copy(rounded.rearrange("p (c u) x -> p c x u", u=4), raw.rearrange("p x (c u) -> p c x u", u=4))
+
+        def quantize_first(a, shares):
+            rounded = sbuf("first_bf%d" % a, [P, P, PACK], BF16)
+            for engine, c0, c1 in shares:
+                round_plain(engine, rounded[:, c0:c1, :], piece_raw[0, a][:, :, c0:c1])
             nc.vector.quantize_mx(
-                out=w1_code[a, 0][:, c0:c1].bitcast(FP8X4),
-                scales=w1_scale[a, 0][:, c0:c1],
+                out=plain_code[0][:, a, :].bitcast(FP8X4),
+                scales=plain_scale[0][:, a, :],
                 in_=rounded[:].rearrange("p c x -> p (c x)"),
             )
+
+        def quantize_plain(q, raws, engines, tag=""):
+            rounded = sbuf("plain_bf%d" % q, [P, PASSES, P, PACK], BF16, tag=tag)
+            for a in range(PASSES):
+                round_plain(engines[a], rounded[:, a, :, :], raws[a])
+            nc.vector.quantize_mx(
+                out=plain_code[q][:].rearrange("p a c -> p (a c)").bitcast(FP8X4),
+                scales=plain_scale[q][:].rearrange("p a c -> p (a c)"),
+                in_=rounded[:].rearrange("p a c x -> p (a c x)"),
+            )
+
+        def quantize_late(i, tag):
+            raws = (piece_raw[2, 0][:, :, P * i : P * (i + 1)], piece_raw[3 + i, 1][:])
+            quantize_plain(2 + i, raws, (nc.gpsimd, nc.gpsimd), tag)
 
         dealt_bf = {}
         dealt_code = [sbuf("dealt_code%d" % pair, [P, PASSES, 2 * P], U32) for pair in range(2)]
         dealt_scale = [sbuf("dealt_scale%d" % pair, [P, PASSES, 2 * P], U8) for pair in range(2)]
 
-        def round_dealt(a, pair):
-            nc.scalar.copy(
-                dealt_bf[pair][:, a, :, :, :].rearrange("p t m x -> p m x t"),
-                w1_raw[a][:].rearrange("p x (m t) -> p m x t", t=PACK)[:, :, :, 2 * pair : 2 * pair + 2],
-            )
+        def round_dealt(a, pair, on_scalar=True):
+            rounded = dealt_bf[pair][:, a, :, :, :].rearrange("p t m x -> p m x t")
+            raw = w1_raw[a][:].rearrange("p x (m t) -> p m x t", t=PACK)[:, :, :, 2 * pair : 2 * pair + 2]
+            if on_scalar:
+                nc.scalar.copy(rounded, raw)
+            else:
+                nc.gpsimd.tensor_scalar(rounded, raw, 1.0, 0.0, ALU.mult, ALU.add)
 
         def quantize_dealt(pair):
             nc.vector.quantize_mx(
@@ -209,8 +224,7 @@ def tile_list_grasp_pair_wrench_kernel(
 
         def stationary(a, b, t):
             if b == 0:
-                rows = slice(P * t, P * (t + 1))
-                return w1_code[a, 0][:, rows], w1_scale[a, 0][:, rows]
+                return plain_code[t][:, a, :], plain_scale[t][:, a, :]
             rows = slice(P * (t % 2), P * (t % 2 + 1))
             return dealt_code[t // 2][:, a, rows], dealt_scale[t // 2][:, a, rows]
 
@@ -219,28 +233,30 @@ def tile_list_grasp_pair_wrench_kernel(
         def tile_of_h(b, t, tag=""):
             h[b, t] = sbuf("h%d%d" % (b, t), [P, S], F32, tag=tag)
             first = (b, t) == (0, 0)
-            banks = (0, 5, 1, 6) if first else (4, 5) if (b, t) == (0, 3) else (2 * t, 2 * t + 1)
-            width = S // len(banks)
-            accs = [bank(number, [P, width], "h_acc%d%d%d" % (b, t, number)) for number in banks]
+            banks = (0, 1, 5) if first else (4, 5) if (b, t) == (0, 3) else (2 * t, 2 * t + 1)
+            parts = ((0, 512), (512, 768), (768, 1024)) if first else ((0, 512), (512, 1024))
+            accs = [
+                bank(number, [P, c1 - c0], "h_acc%d%d%d" % (b, t, number)) for number, (c0, c1) in zip(banks, parts)
+            ]
             for a in range(PASSES):
                 codes, scales = stationary(a, b, t)
-                for part, acc in enumerate(accs):
-                    side, within = divmod(part * width, BANK)
+                for acc, (c0, c1) in zip(accs, parts):
+                    side = c0 // BANK
                     nc.tensor.matmul_mx(
                         out=acc[:],
                         lhsT=codes.bitcast(FP8X4),
                         lhsT_scale=scales,
-                        rhs=v_words[a, side][:, within : within + width].bitcast(FP8X4),
-                        rhs_scale=v_scale[:, a, part * width : (part + 1) * width],
+                        rhs=v_words[a, side][:, c0 - BANK * side : c1 - BANK * side].bitcast(FP8X4),
+                        rhs_scale=v_scale[:, a, c0:c1],
                         start=(a == 0),
                         stop=(a == PASSES - 1),
                     )
-            for part, acc in enumerate(accs):
-                cols = slice(part * width, (part + 1) * width)
-                if first and part % 2:
-                    nc.vector.tensor_scalar(h[b, t][:, cols], acc[:], bias_of[b, t], None, ALU.add)
+            for part, (acc, (c0, c1)) in enumerate(zip(accs, parts)):
+                bias = bias_of[b, t][c0 // BANK]
+                if first and part == 1:
+                    nc.vector.tensor_scalar(h[b, t][:, c0:c1], acc[:], bias, None, ALU.add)
                 else:
-                    nc.scalar.activation(h[b, t][:, cols], acc[:], ACT.Identity, bias=bias_of[b, t])
+                    nc.scalar.activation(h[b, t][:, c0:c1], acc[:], ACT.Identity, bias=bias)
 
         z_code, z_scale = {}, {}
 
@@ -252,10 +268,8 @@ def tile_list_grasp_pair_wrench_kernel(
             nc.vector.tensor_copy(picked, h[b, t][:].indirect((pos1_sb, pos2_sb)[f][:, entries]))
 
         def gather_plain(q, f, tag=""):
-            first, count = PLAIN_GROUPS[q]
-            if q == first:
-                plain_fingers[first, f] = sbuf("plain_finger%d%d" % (q, f), [P, count, PAIRS], F32, tag=tag)
-            gather(plain_fingers[first, f][:, q - first, :], 0, q, f, 0, PAIRS)
+            plain_fingers[q, f] = sbuf("plain_finger%d%d" % (q, f), [P, PAIRS], F32, tag=tag)
+            gather(plain_fingers[q, f][:], 0, q, f, 0, PAIRS)
 
         def gather_fingers(t, j0, j1):
             for f in range(2):
@@ -274,16 +288,8 @@ def tile_list_grasp_pair_wrench_kernel(
         z_planes = sbuf("z_planes", [P, PACK, PAIRS], BF16)
 
         def plain_max(q, tag=""):
-            count = PLAIN_GROUPS[q][1]
-            z_plain = sbuf("z_plain%d" % q, [P, count, PAIRS], BF16, tag=tag)
+            z_plain = sbuf("z_plain%d" % q, [P, PAIRS], BF16, tag=tag)
             nc.vector.tensor_tensor(z_plain[:], plain_fingers[q, 0][:], plain_fingers[q, 1][:], ALU.max)
-            for i in range(count):
-                z_moves.append((q + i, z_plain[:, i, :]))
-
-        z_moves = []
-
-        def move_z(q):
-            z_plain = dict(z_moves)[q]
             for t in range(PACK):
                 nc.sync.dma_start(out=z_planes[32 * q : 32 * (q + 1), t, :], in_=z_plain[t:P:PACK, :])
 
@@ -389,50 +395,46 @@ def tile_list_grasp_pair_wrench_kernel(
             tile_of_h(1, t)
             gather_fingers(t, 0, j1)
 
-        quantize_piece(0, 0, nc.vector.tensor_copy)
+        quantize_first(0, ((nc.vector, 0, P),))
         gather_words(0)
-        gather_words(1)
-        quantize_piece(0, 1)
-        quantize_piece(1, 0)
-        quantize_piece(1, 1)
-        tile_of_h(0, 0, "piece_raw11")
-        gather_plain(0, 0)
+        quantize_first(1, ((nc.scalar, 0, P // 2), (nc.gpsimd, P // 2, P)))
+        gather_words(1, "piece_raw01")
+        tile_of_h(0, 0)
+        quantize_plain(1, (piece_raw[1, 0][:], piece_raw[1, 1][:]), (nc.scalar, nc.gpsimd))
+        gather_plain(0, 0, "piece_raw11")
         gather_plain(0, 1)
         tile_of_h(0, 1)
-        quantize_piece(2, 0, None, "piece_bf11")
-        quantize_piece(2, 1)
-        plain_max(0, "piece_raw21")
-        gather_plain(1, 0, "piece_bf21")
-        gather_plain(1, 1, "plain_finger00")
-        move_z(0)
+        quantize_late(0, "plain_bf1")
+        plain_max(0, "piece_raw31")
         load_ws(1)
-        dealt_bf[0] = sbuf("w1_bf0", [P, PASSES, 2, P, PACK], BF16)
-        round_dealt(0, 0)
+        gather_plain(1, 0, "plain_bf1")
+        gather_plain(1, 1, "piece_raw11")
         tile_of_h(0, 2)
-        gather_plain(2, 0)
-        gather_plain(2, 1)
+        quantize_late(1, "plain_finger01")
+        plain_max(1, "piece_raw41")
+        gather_plain(2, 0, "plain_finger01")
+        gather_plain(2, 1, "plain_bf1")
+        dealt_bf[0] = sbuf("w1_bf0", [P, PASSES, 2, P, PACK], BF16, tag="bias_third")
+        round_dealt(0, 0)
         round_dealt(1, 0)
         quantize_dealt(0)
         tile_of_h(0, 3)
-        plain_max(1, "w1_bf0")
-        move_z(1)
-        move_z(2)
-        gather_plain(3, 0)
-        gather_plain(3, 1)
-        dealt_bf[1] = sbuf("w1_bf1", [P, PASSES, 2, P, PACK], BF16, tag="b1_03")
+        gather_plain(3, 0, "piece_raw11")
+        plain_max(2, "b1_03")
+        gather_plain(3, 1, "plain_finger01")
+        dealt_bf[1] = sbuf("w1_bf1", [P, PASSES, 2, P, PACK], BF16, tag="bias_third")
         round_dealt(0, 1)
         round_dealt(1, 1)
         quantize_dealt(1)
         plain_max(3, "w1_raw1")
-        move_z(3)
         load_bias(1, 3, 4)
         load_wm_and_bs()
-        ws_bf = sbuf("ws_bf0", [P, 4 * P, PACK], BF16, tag="plain_finger31")
+        ws_bf = sbuf("ws_bf0", [P, 4 * P, PACK], BF16, tag="plain_finger01")
         round_ws_gpsimd(0, 0, 4 * P, ws_bf[:])
         dealt_tile(0)
         dealt_tile(1)
         quantize_ws(0, 0, 4 * P, ws_bf[:], False)
-        joined = sbuf("joined", [P, 2 * P + PAIRS, PACK], BF16, tag="plain_finger30")
+        joined = sbuf("joined", [P, 2 * P + PAIRS, PACK], BF16, tag="piece_raw11")
         nc.scalar.copy(
             joined[:, 0 : 2 * P, :].rearrange("p (c u) x -> p c x u", u=4),
             ws_raw[0][:, :, 4 * P : N].rearrange("p x (c u) -> p c x u", u=4),

@@ -26,8 +26,7 @@ QUADS = 4
 PER_COLUMN = 16
 HALF = PAIRS // 2
 COUPLES = N // (2 * P)
-FIRST_WORDS = 1536
-PIECES = ((0, 128), (128, 256), (256, 512), (256, 384), (384, 512))
+WIDE = 4 * P
 
 
 def tile_list_grasp_pair_wrench_kernel(
@@ -39,8 +38,8 @@ def tile_list_grasp_pair_wrench_kernel(
         keep = ctx.enter_context(tc.tile_pool(name="keep", bufs=1))
         psum = ctx.enter_context(tc.psum_pool(name="psum", bufs=1))
 
-        def sbuf(name, shape, dtype, tag="", bufs=1):
-            return keep.tile(shape, dtype, name=name, tag=tag or name, bufs=bufs, align_bytes=64)
+        def sbuf(name, shape, dtype, after=""):
+            return keep.tile(shape, dtype, name=name, tag=after or name, bufs=1, align_bytes=64)
 
         def bank(number, shape, name):
             return psum.tile(shape, F32, name=name, tag="bank%d" % number)
@@ -56,46 +55,44 @@ def tile_list_grasp_pair_wrench_kernel(
         v_scale = sbuf("v_scale", [P, PASSES, S], U8)
         nc.vector.memset(v_scale[:].rearrange("p a s -> p (a s)").bitcast(I32), 0)
         nc.vector.memset(wm_scale[:], 0)
-        word_window = [sbuf("word_window%d" % a, [P, T], I32) for a in range(PASSES)]
+        word_window = {}
 
-        def load_words(a, t0, t1):
-            nc.sync.dma_start(
-                out=word_window[a][:, t0:t1],
-                in_=tab_words[a].rearrange("p t x -> p (t x)").bitcast(I32)[:, t0:t1],
-            )
+        def load_words(a, after=""):
+            word_window[a] = sbuf("word_window%d" % a, [P, T], I32, after)
+            nc.sync.dma_start(out=word_window[a][:], in_=tab_words[a].rearrange("p t x -> p (t x)").bitcast(I32))
 
         nc.sync.dma_start(offs_sb[:], offs)
         nc.sync.dma_start(out=scale_window[0:32, :], in_=tab_scales.bitcast(I32).rearrange("a g w -> g a w"))
-        load_words(0, 0, T)
+        load_words(0)
 
-        piece_raw = {}
+        plain_raw = {}
 
-        def load_piece(n, passes=range(PASSES), queue=nc.sync):
-            c0, c1 = PIECES[n]
-            for a in passes:
-                piece_raw[n, a] = sbuf("piece_raw%d%d" % (n, a), [P, PACK, c1 - c0], F32)
-                queue.dma_start(
-                    out=piece_raw[n, a][:],
-                    in_=w1[PASS * a : PASS * (a + 1), c0:c1].rearrange("(p x) c -> p x c", x=PACK),
-                )
+        def load_plain(a, t, tiles=1):
+            raw = sbuf("plain_raw%d%d" % (t, a), [P, PACK, tiles * P], F32)
+            nc.sync.dma_start(
+                out=raw[:],
+                in_=w1[PASS * a : PASS * (a + 1), P * t : P * (t + tiles)].rearrange("(p x) c -> p x c", x=PACK),
+            )
+            for i in range(tiles):
+                plain_raw[t + i, a] = raw[:, :, P * i : P * (i + 1)]
 
         bias_of = {}
 
-        def load_plain_biases():
+        def load_first_biases():
             rows = sbuf("bias_rows", [P, P], F32)
             identity = sbuf("identity", [P, P], F32)
             nc.gpsimd.memset(rows[:], 0.0)
             make_identity(nc, identity[:])
-            nc.scalar.dma_start(out=rows[0:PACK, :], in_=b1[0:PASS].rearrange("(t p) -> t p", p=P))
+            nc.scalar.dma_start(out=rows[0:3, :], in_=b1[0 : 3 * P].rearrange("(t p) -> t p", p=P))
             turned = bank(4, [P, P], "turned")
             nc.tensor.transpose(turned[:], rows[:], identity[:])
-            columns = sbuf("bias_columns", [P, PACK], F32)
-            nc.vector.tensor_copy(columns[:], turned[:, 0:PACK])
-            for t in range(PACK):
+            columns = sbuf("bias_columns", [P, 3], F32)
+            nc.vector.tensor_copy(columns[:], turned[:, 0:3])
+            for t in range(2):
                 bias_of[0, t] = [columns[:, t : t + 1]] * 2
-            third = sbuf("bias_third", [P, 1], F32)
-            nc.vector.tensor_copy(third[:], turned[:, 2:3])
-            bias_of[0, 2] = [columns[:, 2:3], third[:]]
+            last_of_2 = sbuf("bias_last_of_2", [P, 1], F32)
+            nc.vector.tensor_copy(last_of_2[:], turned[:, 2:3])
+            bias_of[0, 2] = [columns[:, 2:3], last_of_2[:]]
 
         def load_bias(b, t0, t1):
             rows = b1[PASS * b : PASS * (b + 1)].rearrange("(p t) -> p t" if b else "(t p) -> p t", t=PACK)
@@ -105,12 +102,12 @@ def tile_list_grasp_pair_wrench_kernel(
             for t in range(t0, t1):
                 bias_of[b, t] = [column[:, t - t0 : t - t0 + 1]] * 2
 
-        w1_raw = []
+        dealt_raw = []
 
         def load_dealt(a):
-            w1_raw.append(sbuf("w1_raw%d" % a, [P, PACK, PASS], F32))
+            dealt_raw.append(sbuf("dealt_raw%d" % a, [P, PACK, PASS], F32))
             nc.sync.dma_start(
-                out=w1_raw[a][:],
+                out=dealt_raw[a][:],
                 in_=w1[PASS * a : PASS * (a + 1), PASS:H].rearrange("(p x) c -> p x c", x=PACK),
             )
 
@@ -122,16 +119,24 @@ def tile_list_grasp_pair_wrench_kernel(
                 out=ws_raw[b][:], in_=ws[PASS * b : PASS * (b + 1), :].rearrange("(p x) n -> p x n", x=PACK)
             )
 
-        load_piece(0, (0,), nc.scalar)
-        load_plain_biases()
-        load_words(1, 0, T)
-        load_piece(0, (1,))
-        load_piece(1)
+        load_plain(0, 0)
+        load_first_biases()
+        picked_scale = sbuf("picked_scale", [P, S], U8)
+        nc.vector.tensor_copy(picked_scale[:], scale_window[:].bitcast(U8).indirect(offs_sb[:]))
+        for quad in range(QUADS):
+            nc.sync.dma_start(
+                out=v_scale[32 * quad : 32 * quad + 4, :, :].bitcast(I32),
+                in_=picked_scale[8 * quad : 8 * quad + 8, :].bitcast(I32),
+            )
+        load_words(1, "scale_window")
+        load_plain(1, 0)
+        load_plain(0, 1)
+        load_plain(1, 1)
         nc.sync.dma_start(pos1_sb[:], pos1)
         nc.sync.dma_start(pos2_sb[:], pos2)
-        load_piece(2, (0,))
-        load_piece(3, (1,))
-        load_piece(4, (1,))
+        load_plain(0, 2, tiles=2)
+        load_plain(1, 2)
+        load_plain(1, 3)
         load_dealt(0)
         load_dealt(1)
         load_bias(0, 3, 4)
@@ -150,76 +155,61 @@ def tile_list_grasp_pair_wrench_kernel(
             with nc.allow_non_contiguous_dma(reason="one bias value for each partition and output tile"):
                 nc.sync.dma_start(out=bs_sb[:], in_=bs.rearrange("(c p) -> p c", p=P))
 
-        picked_scale = sbuf("picked_scale", [P, S], U8)
-        nc.vector.tensor_copy(picked_scale[:], scale_window[:].bitcast(U8).indirect(offs_sb[:]))
-        for quad in range(QUADS):
-            nc.scalar.dma_start(
-                out=v_scale[32 * quad : 32 * quad + 4, :, :].bitcast(I32),
-                in_=picked_scale[8 * quad : 8 * quad + 8, :].bitcast(I32),
-            )
         v_words = {}
         words_0 = sbuf("v_words0", [P, S], U32)
         nc.vector.tensor_copy(words_0[:], word_window[0][:].bitcast(U32).indirect(offs_sb[:]))
         for side in range(2):
             v_words[0, side] = words_0[:, BANK * side : BANK * (side + 1)]
 
-        def gather_words(side, tag=""):
+        def gather_last_words(side, after=""):
             entries = slice(side * BANK // PER_COLUMN, (side + 1) * BANK // PER_COLUMN)
-            words = sbuf("v_words1%d" % side, [P, BANK], U32, tag=tag)
+            words = sbuf("v_words1%d" % side, [P, BANK], U32, after)
             nc.vector.tensor_copy(words[:], word_window[1][:].bitcast(U32).indirect(offs_sb[:, entries]))
             v_words[1, side] = words[:]
 
-        plain_code = [sbuf("plain_code%d" % q, [P, PASSES, P], U32) for q in range(PACK)]
-        plain_scale = [sbuf("plain_scale%d" % q, [P, PASSES, P], U8) for q in range(PACK)]
-
-        def round_plain(engine, rounded, raw):
+        def round_rows(engine, rounded, raw):
             if engine is nc.gpsimd:
                 nc.gpsimd.tensor_scalar(rounded, raw.rearrange("p x c -> p c x"), 1.0, 0.0, ALU.mult, ALU.add)
                 return
             copy = nc.scalar.copy if engine is nc.scalar else nc.vector.tensor_copy
-            copy(rounded.rearrange("p (c u) x -> p c x u", u=4), raw.rearrange("p x (c u) -> p c x u", u=4))
+            copy(rounded.rearrange("p (d u) x -> p d x u", u=4), raw.rearrange("p x (d u) -> p d x u", u=4))
+
+        def quantize(codes, scales, rounded):
+            nc.vector.quantize_mx(out=codes.bitcast(FP8X4), scales=scales, in_=rounded)
+
+        plain_code = [sbuf("plain_code%d" % t, [P, PASSES, P], U32) for t in range(PACK)]
+        plain_scale = [sbuf("plain_scale%d" % t, [P, PASSES, P], U8) for t in range(PACK)]
 
         def quantize_first(a, shares):
             rounded = sbuf("first_bf%d" % a, [P, P, PACK], BF16)
             for engine, c0, c1 in shares:
-                round_plain(engine, rounded[:, c0:c1, :], piece_raw[0, a][:, :, c0:c1])
-            nc.vector.quantize_mx(
-                out=plain_code[0][:, a, :].bitcast(FP8X4),
-                scales=plain_scale[0][:, a, :],
-                in_=rounded[:].rearrange("p c x -> p (c x)"),
-            )
+                round_rows(engine, rounded[:, c0:c1, :], plain_raw[0, a][:, :, c0:c1])
+            quantize(plain_code[0][:, a, :], plain_scale[0][:, a, :], rounded[:].rearrange("p c x -> p (c x)"))
 
-        def quantize_plain(q, raws, engines, tag=""):
-            rounded = sbuf("plain_bf%d" % q, [P, PASSES, P, PACK], BF16, tag=tag)
+        def quantize_plain(t, engines, after=""):
+            rounded = sbuf("plain_bf%d" % t, [P, PASSES, P, PACK], BF16, after)
             for a in range(PASSES):
-                round_plain(engines[a], rounded[:, a, :, :], raws[a])
-            nc.vector.quantize_mx(
-                out=plain_code[q][:].rearrange("p a c -> p (a c)").bitcast(FP8X4),
-                scales=plain_scale[q][:].rearrange("p a c -> p (a c)"),
-                in_=rounded[:].rearrange("p a c x -> p (a c x)"),
+                round_rows(engines[a], rounded[:, a, :, :], plain_raw[t, a])
+            quantize(
+                plain_code[t][:].rearrange("p a c -> p (a c)"),
+                plain_scale[t][:].rearrange("p a c -> p (a c)"),
+                rounded[:].rearrange("p a c x -> p (a c x)"),
             )
 
-        def quantize_late(i, tag):
-            raws = (piece_raw[2, 0][:, :, P * i : P * (i + 1)], piece_raw[3 + i, 1][:])
-            quantize_plain(2 + i, raws, (nc.gpsimd, nc.gpsimd), tag)
+        dealt_code = [sbuf("dealt_code%d" % twin, [P, PASSES, 2 * P], U32) for twin in range(2)]
+        dealt_scale = [sbuf("dealt_scale%d" % twin, [P, PASSES, 2 * P], U8) for twin in range(2)]
 
-        dealt_bf = {}
-        dealt_code = [sbuf("dealt_code%d" % pair, [P, PASSES, 2 * P], U32) for pair in range(2)]
-        dealt_scale = [sbuf("dealt_scale%d" % pair, [P, PASSES, 2 * P], U8) for pair in range(2)]
-
-        def round_dealt(a, pair, on_scalar=True):
-            rounded = dealt_bf[pair][:, a, :, :, :].rearrange("p t m x -> p m x t")
-            raw = w1_raw[a][:].rearrange("p x (m t) -> p m x t", t=PACK)[:, :, :, 2 * pair : 2 * pair + 2]
-            if on_scalar:
-                nc.scalar.copy(rounded, raw)
-            else:
-                nc.gpsimd.tensor_scalar(rounded, raw, 1.0, 0.0, ALU.mult, ALU.add)
-
-        def quantize_dealt(pair):
-            nc.vector.quantize_mx(
-                out=dealt_code[pair][:].rearrange("p a c -> p (a c)").bitcast(FP8X4),
-                scales=dealt_scale[pair][:].rearrange("p a c -> p (a c)"),
-                in_=dealt_bf[pair][:].rearrange("p a t m x -> p (a t m x)"),
+        def quantize_dealt(twin, after):
+            rounded = sbuf("dealt_bf%d" % twin, [P, PASSES, 2, P, PACK], BF16, after)
+            for a in range(PASSES):
+                nc.scalar.copy(
+                    rounded[:, a, :, :, :].rearrange("p t m x -> p m x t"),
+                    dealt_raw[a][:].rearrange("p x (m t) -> p m x t", t=PACK)[:, :, :, 2 * twin : 2 * twin + 2],
+                )
+            quantize(
+                dealt_code[twin][:].rearrange("p a c -> p (a c)"),
+                dealt_scale[twin][:].rearrange("p a c -> p (a c)"),
+                rounded[:].rearrange("p a t m x -> p (a t m x)"),
             )
 
         def stationary(a, b, t):
@@ -230,11 +220,11 @@ def tile_list_grasp_pair_wrench_kernel(
 
         h = {}
 
-        def tile_of_h(b, t, tag=""):
-            h[b, t] = sbuf("h%d%d" % (b, t), [P, S], F32, tag=tag)
-            first = (b, t) == (0, 0)
-            banks = (0, 1, 5) if first else (4, 5) if (b, t) == (0, 3) else (2 * t, 2 * t + 1)
-            parts = ((0, 512), (512, 768), (768, 1024)) if first else ((0, 512), (512, 1024))
+        def tile_of_h(b, t, banks):
+            h[b, t] = sbuf("h%d%d" % (b, t), [P, S], F32)
+            cut = len(banks) == 3
+            edges = (0, BANK, BANK + BANK // 2, S) if cut else (0, BANK, S)
+            parts = list(zip(edges[:-1], edges[1:]))
             accs = [
                 bank(number, [P, c1 - c0], "h_acc%d%d%d" % (b, t, number)) for number, (c0, c1) in zip(banks, parts)
             ]
@@ -251,90 +241,68 @@ def tile_list_grasp_pair_wrench_kernel(
                         start=(a == 0),
                         stop=(a == PASSES - 1),
                     )
-            for part, (acc, (c0, c1)) in enumerate(zip(accs, parts)):
+            for acc, (c0, c1) in zip(accs, parts):
                 bias = bias_of[b, t][c0 // BANK]
-                if first and part == 1:
+                if cut and c0 == BANK:
                     nc.vector.tensor_scalar(h[b, t][:, c0:c1], acc[:], bias, None, ALU.add)
                 else:
                     nc.scalar.activation(h[b, t][:, c0:c1], acc[:], ACT.Identity, bias=bias)
 
         z_code, z_scale = {}, {}
-
-        fingers = [sbuf("finger%d" % f, [P, PACK, PAIRS], F32) for f in range(2)]
+        dealt_fingers = [sbuf("dealt_finger%d" % f, [P, PACK, PAIRS], F32) for f in range(2)]
         plain_fingers = {}
 
-        def gather(picked, b, t, f, j0, j1):
-            entries = slice(j0 // PER_COLUMN, j1 // PER_COLUMN)
-            nc.vector.tensor_copy(picked, h[b, t][:].indirect((pos1_sb, pos2_sb)[f][:, entries]))
+        def gather(picked, b, t, f):
+            nc.vector.tensor_copy(picked, h[b, t][:].indirect((pos1_sb, pos2_sb)[f][:]))
 
-        def gather_plain(q, f, tag=""):
-            plain_fingers[q, f] = sbuf("plain_finger%d%d" % (q, f), [P, PAIRS], F32, tag=tag)
-            gather(plain_fingers[q, f][:], 0, q, f, 0, PAIRS)
+        def gather_plain(t, f, after=""):
+            plain_fingers[t, f] = sbuf("plain_finger%d%d" % (t, f), [P, PAIRS], F32, after)
+            gather(plain_fingers[t, f][:], 0, t, f)
 
-        def gather_fingers(t, j0, j1):
+        def dealt_tile(t):
+            tile_of_h(1, t, (2 * t, 2 * t + 1))
             for f in range(2):
-                gather(fingers[f][:, t, j0:j1], 1, t, f, j0, j1)
+                gather(dealt_fingers[f][:, t, :], 1, t, f)
 
-        def pair_max(b, j0, j1):
-            z_bf = sbuf("z_bf%d_%d" % (b, j0), [P, j1 - j0, PACK], BF16, tag="z_bf1")
+        def dealt_max(half):
+            z_bf = sbuf("z_bf1_%d" % half, [P, HALF, PACK], BF16, "z_bf1")
+            j = slice(HALF * half, HALF * (half + 1))
             nc.vector.tensor_tensor(
-                z_bf[:].rearrange("p (c u) t -> p c t u", u=2),
-                fingers[0][:, :, j0:j1].rearrange("p t (c u) -> p c t u", u=2),
-                fingers[1][:, :, j0:j1].rearrange("p t (c u) -> p c t u", u=2),
+                z_bf[:].rearrange("p (d u) t -> p d t u", u=2),
+                dealt_fingers[0][:, :, j].rearrange("p t (d u) -> p d t u", u=2),
+                dealt_fingers[1][:, :, j].rearrange("p t (d u) -> p d t u", u=2),
                 ALU.max,
             )
             return z_bf
 
-        z_planes = sbuf("z_planes", [P, PACK, PAIRS], BF16)
+        z_moved = sbuf("z_moved", [P, PACK, PAIRS], BF16)
 
-        def plain_max(q, tag=""):
-            z_plain = sbuf("z_plain%d" % q, [P, PAIRS], BF16, tag=tag)
-            nc.vector.tensor_tensor(z_plain[:], plain_fingers[q, 0][:], plain_fingers[q, 1][:], ALU.max)
-            for t in range(PACK):
-                nc.sync.dma_start(out=z_planes[32 * q : 32 * (q + 1), t, :], in_=z_plain[t:P:PACK, :])
+        def plain_max(t, after):
+            z_plain = sbuf("z_plain%d" % t, [P, PAIRS], BF16, after)
+            nc.vector.tensor_tensor(z_plain[:], plain_fingers[t, 0][:], plain_fingers[t, 1][:], ALU.max)
+            for x in range(PACK):
+                nc.sync.dma_start(out=z_moved[32 * t : 32 * (t + 1), x, :], in_=z_plain[x:P:PACK, :])
 
-        def weave_planes(z_bf):
-            nc.scalar.copy(
-                z_bf.rearrange("p (c u) t -> p c t u", u=4),
-                z_planes[:].rearrange("p t (c u) -> p c t u", u=4),
-            )
-
-        def quantize_z(z_bf, b, half, tag=""):
-            z_code[b, half] = sbuf("z_code%d%d" % (b, half), [P, HALF], U32, tag=tag)
+        def quantize_z(z_bf, b, half, after=""):
+            z_code[b, half] = sbuf("z_code%d%d" % (b, half), [P, HALF], U32, after)
             z_scale[b, half] = sbuf("z_scale%d%d" % (b, half), [P, HALF], U8)
-            nc.vector.quantize_mx(
-                out=z_code[b, half][:].bitcast(FP8X4),
-                scales=z_scale[b, half][:],
-                in_=z_bf.rearrange("p j t -> p (j t)"),
-            )
+            quantize(z_code[b, half][:], z_scale[b, half][:], z_bf.rearrange("p j x -> p (j x)"))
 
         ws_q = {}
 
-        def round_ws_gpsimd(b, n0, n1, rounded):
-            nc.gpsimd.tensor_scalar(
-                rounded, ws_raw[b][:, :, n0:n1].rearrange("p x n -> p n x"), 1.0, 0.0, ALU.mult, ALU.add
-            )
-
-        def quantize_ws(b, n0, n1, rounded, on_scalar=True):
-            if on_scalar:
-                nc.scalar.copy(
-                    rounded.rearrange("p (c u) x -> p c x u", u=4),
-                    ws_raw[b][:, :, n0:n1].rearrange("p x (c u) -> p c x u", u=4),
-                )
+        def quantize_ws(b, n0, n1, rounded):
             codes = sbuf("ws_code%d_%d" % (b, n0), [P, n1 - n0], U32)
             scales = sbuf("ws_scale%d_%d" % (b, n0), [P, n1 - n0], U8)
-            nc.vector.quantize_mx(
-                out=codes[:].bitcast(FP8X4), scales=scales[:], in_=rounded.rearrange("p n x -> p (n x)")
-            )
+            quantize(codes[:], scales[:], rounded.rearrange("p n x -> p (n x)"))
             for c in range(n0 // P, n1 // P):
                 ws_q[b, c] = codes[:, P * c - n0 : P * (c + 1) - n0], scales[:, P * c - n0 : P * (c + 1) - n0]
 
         m_acc, g_acc, gates = {}, {}, {}
 
-        def multiply_g(half, q, b, number=None, tiles=range(2)):
+        def multiply_g(half, q, b, number=None):
             if b == 0:
                 g_acc[half, q] = bank(number, [P, 2, HALF], "g_acc%d%d" % (half, q))
-            for e in tiles:
+            for e in range(2):
                 nc.tensor.matmul_mx(
                     out=g_acc[half, q][:, e, :],
                     lhsT=ws_q[b, 2 * q + e][0].bitcast(FP8X4),
@@ -345,15 +313,15 @@ def tile_list_grasp_pair_wrench_kernel(
                     stop=(b, e) == (1, 1),
                 )
 
-        def multiply_m(half, q, b, number=None, tiles=range(2)):
+        def multiply_m(half, q, b, number=None):
             if b == 0:
                 m_acc[half, q] = bank(number, [P, 2, HALF], "m_acc%d%d" % (half, q))
-            for e in tiles:
+            for e in range(2):
                 c = 2 * q + e
                 for piece in range(HALF // P):
                     cols = slice(P * piece, P * (piece + 1))
                     nc.tensor.matmul_mx(
-                        out=m_acc[half, q][:, e, P * piece : P * (piece + 1)],
+                        out=m_acc[half, q][:, e, cols],
                         lhsT=wm_sb[:, b, 2 * P * c : 2 * P * (c + 1)].bitcast(FP4X4),
                         lhsT_scale=wm_scale[:, b, P // 4 * c : P // 4 * (c + 1)].bitcast(U8),
                         rhs=z_code[b, half][:, cols].bitcast(FP8X4),
@@ -362,21 +330,8 @@ def tile_list_grasp_pair_wrench_kernel(
                         stop=(b, e, piece) == (1, 1, 1),
                     )
 
-        def first_pass(half, q, m_bank, g_bank):
-            multiply_g(half, q, 0, g_bank)
-            multiply_m(half, q, 0, m_bank)
-
-        def second_pass(half):
-            multiply_g(half, 0, 1)
-            for q in range(COUPLES):
-                gate(half, q)
-                multiply_m(half, q, 1, tiles=(0,))
-                if q + 1 < COUPLES:
-                    multiply_g(half, q + 1, 1)
-                multiply_m(half, q, 1, tiles=(1,))
-
         def gate(half, q):
-            gates[half, q] = sbuf("gate%d%d" % (half, q), [P, 2, HALF], F32, tag="h%d%d" % (half, q))
+            gates[half, q] = sbuf("gate%d%d" % (half, q), [P, 2, HALF], F32, "h%d%d" % (half, q))
             for e in range(2):
                 c = 2 * q + e
                 nc.scalar.activation(
@@ -391,98 +346,94 @@ def tile_list_grasp_pair_wrench_kernel(
                 out=out[rows, HALF * half : HALF * (half + 1)].rearrange("(e p) j -> p e j", p=P), in_=result
             )
 
-        def dealt_tile(t, j1=PAIRS):
-            tile_of_h(1, t)
-            gather_fingers(t, 0, j1)
-
         quantize_first(0, ((nc.vector, 0, P),))
-        gather_words(0)
+        gather_last_words(0)
         quantize_first(1, ((nc.scalar, 0, P // 2), (nc.gpsimd, P // 2, P)))
-        gather_words(1, "piece_raw01")
-        tile_of_h(0, 0)
-        quantize_plain(1, (piece_raw[1, 0][:], piece_raw[1, 1][:]), (nc.scalar, nc.gpsimd))
-        gather_plain(0, 0, "piece_raw11")
+        gather_last_words(1, "plain_raw01")
+        tile_of_h(0, 0, (0, 1, 5))
+
+        ring_a, ring_b, ring_c = "plain_bf1", "plain_raw11", "plain_finger01"
+        quantize_plain(1, (nc.scalar, nc.gpsimd))
+        gather_plain(0, 0, ring_b)
         gather_plain(0, 1)
-        tile_of_h(0, 1)
-        quantize_late(0, "plain_bf1")
-        plain_max(0, "piece_raw31")
+        tile_of_h(0, 1, (2, 3))
+        quantize_plain(2, (nc.gpsimd, nc.gpsimd), ring_a)
+        plain_max(0, "plain_raw21")
         load_ws(1)
-        gather_plain(1, 0, "plain_bf1")
-        gather_plain(1, 1, "piece_raw11")
-        tile_of_h(0, 2)
-        quantize_late(1, "plain_finger01")
-        plain_max(1, "piece_raw41")
-        gather_plain(2, 0, "plain_finger01")
-        gather_plain(2, 1, "plain_bf1")
-        dealt_bf[0] = sbuf("w1_bf0", [P, PASSES, 2, P, PACK], BF16, tag="bias_third")
-        round_dealt(0, 0)
-        round_dealt(1, 0)
-        quantize_dealt(0)
-        tile_of_h(0, 3)
-        gather_plain(3, 0, "piece_raw11")
+        gather_plain(1, 0, ring_a)
+        gather_plain(1, 1, ring_b)
+        tile_of_h(0, 2, (4, 5))
+        quantize_plain(3, (nc.gpsimd, nc.gpsimd), ring_c)
+        plain_max(1, "plain_raw31")
+        gather_plain(2, 0, ring_c)
+        gather_plain(2, 1, ring_a)
+        quantize_dealt(0, "bias_last_of_2")
+        tile_of_h(0, 3, (4, 5))
+        gather_plain(3, 0, ring_b)
         plain_max(2, "b1_03")
-        gather_plain(3, 1, "plain_finger01")
-        dealt_bf[1] = sbuf("w1_bf1", [P, PASSES, 2, P, PACK], BF16, tag="bias_third")
-        round_dealt(0, 1)
-        round_dealt(1, 1)
-        quantize_dealt(1)
-        plain_max(3, "w1_raw1")
+        gather_plain(3, 1, ring_c)
+        quantize_dealt(1, "bias_last_of_2")
+        plain_max(3, "dealt_raw1")
         load_bias(1, 3, 4)
         load_wm_and_bs()
-        ws_bf = sbuf("ws_bf0", [P, 4 * P, PACK], BF16, tag="plain_finger01")
-        round_ws_gpsimd(0, 0, 4 * P, ws_bf[:])
+
+        ws_first = sbuf("ws_first", [P, WIDE, PACK], BF16, ring_c)
+        round_rows(nc.gpsimd, ws_first[:], ws_raw[0][:, :, 0:WIDE])
         dealt_tile(0)
         dealt_tile(1)
-        quantize_ws(0, 0, 4 * P, ws_bf[:], False)
-        joined = sbuf("joined", [P, 2 * P + PAIRS, PACK], BF16, tag="piece_raw11")
-        nc.scalar.copy(
-            joined[:, 0 : 2 * P, :].rearrange("p (c u) x -> p c x u", u=4),
-            ws_raw[0][:, :, 4 * P : N].rearrange("p x (c u) -> p c x u", u=4),
-        )
+        quantize_ws(0, 0, WIDE, ws_first[:])
+        rest = N - WIDE
+        joined = sbuf("joined", [P, rest + PAIRS, PACK], BF16, ring_b)
+        round_rows(nc.scalar, joined[:, 0:rest, :], ws_raw[0][:, :, WIDE:N])
         dealt_tile(2)
-        woven = joined[:, 2 * P :, :]
-        weave_planes(woven)
-        codes = sbuf("joined_code", [P, 2 * P + HALF], U32)
-        scales = sbuf("joined_scale", [P, 2 * P + HALF], U8)
-        nc.vector.quantize_mx(
-            out=codes[:].bitcast(FP8X4),
-            scales=scales[:],
-            in_=joined[:, 0 : 2 * P + HALF, :].rearrange("p c x -> p (c x)"),
-        )
-        for e in range(2):
-            ws_q[0, 4 + e] = codes[:, P * e : P * (e + 1)], scales[:, P * e : P * (e + 1)]
-        z_code[0, 0], z_scale[0, 0] = codes[:, 2 * P :], scales[:, 2 * P :]
+        woven = joined[:, rest:, :]
+        round_rows(nc.scalar, woven, z_moved[:])
+        codes = sbuf("joined_code", [P, rest + HALF], U32)
+        scales = sbuf("joined_scale", [P, rest + HALF], U8)
+        quantize(codes[:], scales[:], joined[:, 0 : rest + HALF, :].rearrange("p c x -> p (c x)"))
+        for e in range(rest // P):
+            ws_q[0, WIDE // P + e] = codes[:, P * e : P * (e + 1)], scales[:, P * e : P * (e + 1)]
+        z_code[0, 0], z_scale[0, 0] = codes[:, rest:], scales[:, rest:]
         dealt_tile(3)
+
         quantize_z(woven[:, HALF:PAIRS, :], 0, 1, "b1_13")
-        ws_last = sbuf("ws_last", [P, N, PACK], BF16, tag="z_planes")
-        z_bf = pair_max(1, 0, HALF)
-        quantize_ws(1, 0, 4 * P, ws_last[:, 0 : 4 * P, :])
+        ws_last = sbuf("ws_last", [P, N, PACK], BF16, "z_moved")
+        z_bf = dealt_max(0)
+        round_rows(nc.scalar, ws_last[:, 0:WIDE, :], ws_raw[1][:, :, 0:WIDE])
+        quantize_ws(1, 0, WIDE, ws_last[:, 0:WIDE, :])
         for q in range(COUPLES):
             multiply_g(0, q, 0, q)
-        for q in range(2):
-            multiply_m(0, q, 0, 3 + q)
         for q in range(COUPLES):
-            multiply_g(1, q, 0, 5 + q)
+            multiply_m(0, q, 0, COUPLES + q)
+        for q in range(COUPLES - 1):
+            multiply_m(1, q, 0, 2 * COUPLES + q)
         quantize_z(z_bf[:], 1, 0)
-        quantize_ws(1, 4 * P, N, ws_last[:, 4 * P : N, :])
+        round_rows(nc.scalar, ws_last[:, WIDE:N, :], ws_raw[1][:, :, WIDE:N])
+        quantize_ws(1, WIDE, N, ws_last[:, WIDE:N, :])
         for q in range(COUPLES):
             multiply_g(0, q, 1)
             gate(0, q)
-            if q < 2:
-                multiply_m(0, q, 1)
-        z_bf = pair_max(1, HALF, PAIRS)
+            multiply_m(0, q, 1)
+        z_bf = dealt_max(1)
         finish(0, 0, 0, 1)
-        multiply_m(0, 2, 0, 0)
-        multiply_m(0, 2, 1)
+        last = COUPLES - 1
+        for q in range(last):
+            multiply_g(1, q, 0, q)
         quantize_z(z_bf[:], 1, 1)
         finish(0, 0, 1, 2)
         for q in range(1, COUPLES):
             finish(0, q)
-        for q in range(COUPLES):
-            multiply_g(1, q, 1)
-            gate(1, q)
-            multiply_m(1, q, 0, (1, 3, 4)[q])
-            multiply_m(1, q, 1)
+        multiply_g(1, 0, 1)
+        gate(1, 0)
+        multiply_m(1, 0, 1)
+        multiply_g(1, 1, 1)
+        gate(1, 1)
+        multiply_g(1, last, 0, last)
+        multiply_g(1, last, 1)
+        gate(1, last)
+        multiply_m(1, 1, 1)
+        multiply_m(1, last, 0, COUPLES)
+        multiply_m(1, last, 1)
         for q in range(COUPLES):
             for e in range(2):
                 finish(1, q, e, e + 1)

@@ -1,3 +1,4 @@
+import math
 from contextlib import ExitStack
 
 import concourse.mybir as mybir
@@ -27,6 +28,8 @@ PER_COLUMN = 16
 HALF = PAIRS // 2
 COUPLES = N // (2 * P)
 WIDE = 4 * P
+ALIGN = 64
+KIB = 1024
 
 
 def tile_list_grasp_pair_wrench_kernel(
@@ -38,8 +41,21 @@ def tile_list_grasp_pair_wrench_kernel(
         keep = ctx.enter_context(tc.tile_pool(name="keep", bufs=1))
         psum = ctx.enter_context(tc.psum_pool(name="psum", bufs=1))
 
-        def sbuf(name, shape, dtype, after=""):
-            return keep.tile(shape, dtype, name=name, tag=after or name, bufs=1, align_bytes=64)
+        place = {"end": (0, 0, 0)}
+
+        def sbuf(name, shape, dtype, over="", at=0, lead=0, trail=0):
+            size = math.prod(shape[1:]) * (4 if dtype in (F32, I32, U32) else 2 if dtype == BF16 else 1)
+            if over:
+                first, low, high = place[over]
+                first = first + at
+                assert low <= first and first + size <= high
+            else:
+                low = place["end"][2]
+                first = low + lead
+                high = first + -(-size // ALIGN) * ALIGN + trail
+                place["end"] = (high, high, high)
+            place[name] = (first, low, high)
+            return keep.tile(shape, dtype, name=name, bufs=1, align_bytes=ALIGN, offset=first)
 
         def bank(number, shape, name):
             return psum.tile(shape, F32, name=name, tag="bank%d" % number)
@@ -50,24 +66,52 @@ def tile_list_grasp_pair_wrench_kernel(
 
         scale_window = sbuf("scale_window", [P, T // 4], I32)
         wm_scale = sbuf("wm_scale", [P, PASSES, N // 4], I32)
+        v_scale = sbuf("v_scale", [P, PASSES, S], U8)
         nc.vector.memset(scale_window[32:64, :], 0)
         nc.vector.memset(scale_window[64:P, :], 0)
-        v_scale = sbuf("v_scale", [P, PASSES, S], U8)
         nc.vector.memset(v_scale[:].rearrange("p a s -> p (a s)").bitcast(I32), 0)
         nc.vector.memset(wm_scale[:], 0)
-        word_window = {}
-
-        def load_words(a, after=""):
-            word_window[a] = sbuf("word_window%d" % a, [P, T], I32, after)
-            nc.sync.dma_start(out=word_window[a][:], in_=tab_words[a].rearrange("p t x -> p (t x)").bitcast(I32))
 
         nc.sync.dma_start(offs_sb[:], offs)
         nc.sync.dma_start(out=scale_window[0:32, :], in_=tab_scales.bitcast(I32).rearrange("a g w -> g a w"))
+        word_window = [sbuf("word_window%d" % a, [P, T], I32) for a in range(PASSES)]
+
+        def load_words(a):
+            nc.sync.dma_start(out=word_window[a][:], in_=tab_words[a].rearrange("p t x -> p (t x)").bitcast(I32))
+
         load_words(0)
+        bias_rows = sbuf("bias_rows", [P, PASS], F32)
+        identity = sbuf("identity", [P, P], F32)
+        b1_row = P - PASSES
+        bs_row = b1_row - 2
+        nc.gpsimd.memset(bias_rows[0:bs_row, 0 : N // 2], 0.0)
+        nc.gpsimd.memset(bias_rows[0:b1_row, N // 2 : PASS], 0.0)
+        make_identity(nc, identity[:])
+        nc.sync.dma_start(out=bias_rows[b1_row:P, :], in_=b1.rearrange("(b r) -> b r", b=PASSES))
+        nc.sync.dma_start(out=bias_rows[bs_row:b1_row, 0 : N // 2], in_=bs.rearrange("(u n) -> u n", u=2))
+        load_words(1)
+        turned = [bank(6 + b, [P, PACK, P], "turned%d" % b) for b in range(PASSES)]
+        for t in range(PACK):
+            nc.tensor.transpose(turned[0][:, t, :], bias_rows[:, P * t : P * (t + 1)], identity[:])
+        for t in range(PACK):
+            nc.tensor.transpose(turned[1][:, t, :], bias_rows[:, t:PASS:PACK], identity[:])
+        bias_of = {}
+        for b, own, room in ((0, 2, 4 * KIB), (1, 3, KIB)):
+            columns = sbuf("bias_columns%d" % b, [P, PACK], F32)
+            nc.scalar.copy(columns[:], turned[b][:, :, b1_row + b])
+            for t in range(PACK):
+                bias_of[b, t] = [columns[:, t : t + 1]] * 2
+            last = sbuf("bias_last%d" % b, [P, 1], F32, trail=room)
+            nc.scalar.copy(last[:], turned[b][:, own, b1_row + b : b1_row + b + 1])
+            bias_of[b, own] = [columns[:, own : own + 1], last[:]]
+        bs_sb = sbuf("bs_sb", [P, N // P], F32)
+        nc.scalar.copy(
+            bs_sb[:].rearrange("p (u t) -> p t u", u=2), turned[0][:, 0 : N // (2 * P), bs_row:b1_row]
+        )
 
         plain_raw = {}
 
-        def load_plain(a, t, tiles=1):
+        def load_plain(t, a, tiles=1):
             raw = sbuf("plain_raw%d%d" % (t, a), [P, PACK, tiles * P], F32)
             nc.sync.dma_start(
                 out=raw[:],
@@ -75,32 +119,6 @@ def tile_list_grasp_pair_wrench_kernel(
             )
             for i in range(tiles):
                 plain_raw[t + i, a] = raw[:, :, P * i : P * (i + 1)]
-
-        bias_of = {}
-
-        def load_first_biases():
-            rows = sbuf("bias_rows", [P, P], F32)
-            identity = sbuf("identity", [P, P], F32)
-            nc.gpsimd.memset(rows[:], 0.0)
-            make_identity(nc, identity[:])
-            nc.scalar.dma_start(out=rows[0:3, :], in_=b1[0 : 3 * P].rearrange("(t p) -> t p", p=P))
-            turned = bank(4, [P, P], "turned")
-            nc.tensor.transpose(turned[:], rows[:], identity[:])
-            columns = sbuf("bias_columns", [P, 3], F32)
-            nc.vector.tensor_copy(columns[:], turned[:, 0:3])
-            for t in range(2):
-                bias_of[0, t] = [columns[:, t : t + 1]] * 2
-            last_of_2 = sbuf("bias_last_of_2", [P, 1], F32)
-            nc.vector.tensor_copy(last_of_2[:], turned[:, 2:3])
-            bias_of[0, 2] = [columns[:, 2:3], last_of_2[:]]
-
-        def load_bias(b, t0, t1):
-            rows = b1[PASS * b : PASS * (b + 1)].rearrange("(p t) -> p t" if b else "(t p) -> p t", t=PACK)
-            column = sbuf("b1_%d%d" % (b, t0), [P, t1 - t0], F32)
-            with nc.allow_non_contiguous_dma(reason="one bias value for each partition and tile of h"):
-                nc.sync.dma_start(out=column[:], in_=rows[:, t0:t1])
-            for t in range(t0, t1):
-                bias_of[b, t] = [column[:, t - t0 : t - t0 + 1]] * 2
 
         dealt_raw = []
 
@@ -120,7 +138,6 @@ def tile_list_grasp_pair_wrench_kernel(
             )
 
         load_plain(0, 0)
-        load_first_biases()
         picked_scale = sbuf("picked_scale", [P, S], U8)
         nc.vector.tensor_copy(picked_scale[:], scale_window[:].bitcast(U8).indirect(offs_sb[:]))
         for quad in range(QUADS):
@@ -128,125 +145,112 @@ def tile_list_grasp_pair_wrench_kernel(
                 out=v_scale[32 * quad : 32 * quad + 4, :, :].bitcast(I32),
                 in_=picked_scale[8 * quad : 8 * quad + 8, :].bitcast(I32),
             )
-        load_words(1, "scale_window")
-        load_plain(1, 0)
         load_plain(0, 1)
+        load_plain(1, 0)
         load_plain(1, 1)
         nc.sync.dma_start(pos1_sb[:], pos1)
         nc.sync.dma_start(pos2_sb[:], pos2)
-        load_plain(0, 2, tiles=2)
-        load_plain(1, 2)
-        load_plain(1, 3)
+        load_plain(2, 0, tiles=2)
+        load_plain(2, 1)
+        load_plain(3, 1)
         load_dealt(0)
         load_dealt(1)
-        load_bias(0, 3, 4)
         load_ws(0)
-        load_bias(1, 0, 3)
         wm_sb = sbuf("wm_sb", [P, PASSES, 2 * N], U8)
-        bs_sb = sbuf("bs_sb", [P, N // P], F32)
 
-        def load_wm_and_bs():
+        def load_wm():
             nc.sync.dma_start(out=wm_sb[:].bitcast(I32), in_=wm_words.bitcast(I32).rearrange("b p w -> p b w"))
             for quad in range(QUADS):
                 nc.sync.dma_start(
                     out=wm_scale[32 * quad : 32 * quad + 4, :, :],
                     in_=wm_scales[:, 4 * quad : 4 * quad + 4, :].bitcast(I32).rearrange("b row w -> row b w"),
                 )
-            with nc.allow_non_contiguous_dma(reason="one bias value for each partition and output tile"):
-                nc.sync.dma_start(out=bs_sb[:], in_=bs.rearrange("(c p) -> p c", p=P))
 
         v_words = {}
-        words_0 = sbuf("v_words0", [P, S], U32)
-        nc.vector.tensor_copy(words_0[:], word_window[0][:].bitcast(U32).indirect(offs_sb[:]))
-        for side in range(2):
-            v_words[0, side] = words_0[:, BANK * side : BANK * (side + 1)]
 
-        def gather_last_words(side, after=""):
-            entries = slice(side * BANK // PER_COLUMN, (side + 1) * BANK // PER_COLUMN)
-            words = sbuf("v_words1%d" % side, [P, BANK], U32, after)
-            nc.vector.tensor_copy(words[:], word_window[1][:].bitcast(U32).indirect(offs_sb[:, entries]))
-            v_words[1, side] = words[:]
+        def gather_words(a, c0, c1, over=""):
+            words = sbuf("v_words%d_%d" % (a, c0), [P, c1 - c0], U32, over)
+            entries = slice(c0 // PER_COLUMN, c1 // PER_COLUMN)
+            nc.vector.tensor_copy(words[:], word_window[a][:].bitcast(U32).indirect(offs_sb[:, entries]))
+            v_words[a, c0] = words
+
+        def words_of(a, c0, c1):
+            runs = []
+            for (b, first), words in v_words.items():
+                low, high = max(c0, first), min(c1, first + words.shape[1])
+                if b == a and low < high:
+                    runs.append((low, high, words[:, low - first : high - first]))
+            return runs
 
         def round_rows(engine, rounded, raw):
             if engine is nc.gpsimd:
                 nc.gpsimd.tensor_scalar(rounded, raw.rearrange("p x c -> p c x"), 1.0, 0.0, ALU.mult, ALU.add)
-                return
-            copy = nc.scalar.copy if engine is nc.scalar else nc.vector.tensor_copy
-            copy(rounded.rearrange("p (d u) x -> p d x u", u=4), raw.rearrange("p x (d u) -> p d x u", u=4))
+            else:
+                nc.scalar.copy(
+                    rounded.rearrange("p (d u) x -> p d x u", u=4), raw.rearrange("p x (d u) -> p d x u", u=4)
+                )
 
         def quantize(codes, scales, rounded):
             nc.vector.quantize_mx(out=codes.bitcast(FP8X4), scales=scales, in_=rounded)
 
-        plain_code = [sbuf("plain_code%d" % t, [P, PASSES, P], U32) for t in range(PACK)]
-        plain_scale = [sbuf("plain_scale%d" % t, [P, PASSES, P], U8) for t in range(PACK)]
+        stationary = {}
 
-        def quantize_first(a, shares):
-            rounded = sbuf("first_bf%d" % a, [P, P, PACK], BF16)
+        def quantize_w1(name, rounded, parts):
+            codes = sbuf("code_" + name, [P, len(parts) * P], U32)
+            scales = sbuf("scale_" + name, [P, len(parts) * P], U8)
+            quantize(codes[:], scales[:], rounded)
+            for i, part in enumerate(parts):
+                stationary[part] = codes[:, P * i : P * (i + 1)], scales[:, P * i : P * (i + 1)]
+
+        def round_pass(t, a, shares, lead=0, trail=0):
+            rounded = sbuf("plain_bf%d%d" % (t, a), [P, P, PACK], BF16, lead=lead, trail=trail)
             for engine, c0, c1 in shares:
-                round_rows(engine, rounded[:, c0:c1, :], plain_raw[0, a][:, :, c0:c1])
-            quantize(plain_code[0][:, a, :], plain_scale[0][:, a, :], rounded[:].rearrange("p c x -> p (c x)"))
+                round_rows(engine, rounded[:, c0:c1, :], plain_raw[t, a][:, :, c0:c1])
+            return rounded[:].rearrange("p c x -> p (c x)")
 
-        def quantize_plain(t, engines, after=""):
-            rounded = sbuf("plain_bf%d" % t, [P, PASSES, P, PACK], BF16, after)
+        def round_plain(t, engines, over, at=0):
+            rounded = sbuf("plain_bf%d" % t, [P, PASSES, P, PACK], BF16, over, at)
             for a in range(PASSES):
                 round_rows(engines[a], rounded[:, a, :, :], plain_raw[t, a])
-            quantize(
-                plain_code[t][:].rearrange("p a c -> p (a c)"),
-                plain_scale[t][:].rearrange("p a c -> p (a c)"),
-                rounded[:].rearrange("p a c x -> p (a c x)"),
+            return rounded[:].rearrange("p a c x -> p (a c x)")
+
+        def round_dealt(a, t0, t1, over=""):
+            rounded = sbuf("dealt_bf%d%d" % (a, t0), [P, t1 - t0, P, PACK], BF16, over)
+            nc.scalar.copy(
+                rounded[:].rearrange("p t m x -> p m x t"),
+                dealt_raw[a][:].rearrange("p x (m t) -> p m x t", t=PACK)[:, :, :, t0:t1],
             )
+            return rounded[:].rearrange("p t m x -> p (t m x)")
 
-        dealt_code = [sbuf("dealt_code%d" % twin, [P, PASSES, 2 * P], U32) for twin in range(2)]
-        dealt_scale = [sbuf("dealt_scale%d" % twin, [P, PASSES, 2 * P], U8) for twin in range(2)]
+        h, h_acc = {}, {}
 
-        def quantize_dealt(twin, after):
-            rounded = sbuf("dealt_bf%d" % twin, [P, PASSES, 2, P, PACK], BF16, after)
-            for a in range(PASSES):
-                nc.scalar.copy(
-                    rounded[:, a, :, :, :].rearrange("p t m x -> p m x t"),
-                    dealt_raw[a][:].rearrange("p x (m t) -> p m x t", t=PACK)[:, :, :, 2 * twin : 2 * twin + 2],
-                )
-            quantize(
-                dealt_code[twin][:].rearrange("p a c -> p (a c)"),
-                dealt_scale[twin][:].rearrange("p a c -> p (a c)"),
-                rounded[:].rearrange("p a t m x -> p (a t m x)"),
-            )
-
-        def stationary(a, b, t):
-            if b == 0:
-                return plain_code[t][:, a, :], plain_scale[t][:, a, :]
-            rows = slice(P * (t % 2), P * (t % 2 + 1))
-            return dealt_code[t // 2][:, a, rows], dealt_scale[t // 2][:, a, rows]
-
-        h = {}
-
-        def tile_of_h(b, t, banks):
-            h[b, t] = sbuf("h%d%d" % (b, t), [P, S], F32)
-            cut = len(banks) == 3
-            edges = (0, BANK, BANK + BANK // 2, S) if cut else (0, BANK, S)
-            parts = list(zip(edges[:-1], edges[1:]))
-            accs = [
-                bank(number, [P, c1 - c0], "h_acc%d%d%d" % (b, t, number)) for number, (c0, c1) in zip(banks, parts)
-            ]
-            for a in range(PASSES):
-                codes, scales = stationary(a, b, t)
-                for acc, (c0, c1) in zip(accs, parts):
-                    side = c0 // BANK
+        def multiply_h(b, t, a, parts):
+            for number, c0, c1 in parts:
+                if a == 0:
+                    h_acc[b, t, c0] = bank(number, [P, c1 - c0], "h_acc%d%d_%d" % (b, t, c0))
+                codes, scales = stationary[b, t, a]
+                for low, high, words in words_of(a, c0, c1):
                     nc.tensor.matmul_mx(
-                        out=acc[:],
+                        out=h_acc[b, t, c0][:, low - c0 : high - c0],
                         lhsT=codes.bitcast(FP8X4),
                         lhsT_scale=scales,
-                        rhs=v_words[a, side][:, c0 - BANK * side : c1 - BANK * side].bitcast(FP8X4),
-                        rhs_scale=v_scale[:, a, c0:c1],
+                        rhs=words.bitcast(FP8X4),
+                        rhs_scale=v_scale[:, a, low:high],
                         start=(a == 0),
-                        stop=(a == PASSES - 1),
+                        stop=(a == PASSES - 1 and high == c1),
                     )
-            for acc, (c0, c1) in zip(accs, parts):
+
+        def empty_h(b, t, parts, over="", at=0, on_vector=-1):
+            h[b, t] = sbuf("h%d%d" % (b, t), [P, S], F32, over, at)
+            for number, c0, c1 in parts:
                 bias = bias_of[b, t][c0 // BANK]
-                if cut and c0 == BANK:
-                    nc.vector.tensor_scalar(h[b, t][:, c0:c1], acc[:], bias, None, ALU.add)
+                if c0 == on_vector:
+                    nc.vector.tensor_scalar(h[b, t][:, c0:c1], h_acc[b, t, c0][:], bias, None, ALU.add)
                 else:
-                    nc.scalar.activation(h[b, t][:, c0:c1], acc[:], ACT.Identity, bias=bias)
+                    nc.scalar.activation(h[b, t][:, c0:c1], h_acc[b, t, c0][:], ACT.Identity, bias=bias)
+
+        def sides(first, second):
+            return ((first, 0, BANK), (second, BANK, S))
 
         z_code, z_scale = {}, {}
         dealt_fingers = [sbuf("dealt_finger%d" % f, [P, PACK, PAIRS], F32) for f in range(2)]
@@ -255,17 +259,16 @@ def tile_list_grasp_pair_wrench_kernel(
         def gather(picked, b, t, f):
             nc.vector.tensor_copy(picked, h[b, t][:].indirect((pos1_sb, pos2_sb)[f][:]))
 
-        def gather_plain(t, f, after=""):
-            plain_fingers[t, f] = sbuf("plain_finger%d%d" % (t, f), [P, PAIRS], F32, after)
+        def gather_plain(t, f, over="", at=0, trail=0):
+            plain_fingers[t, f] = sbuf("finger%d%d" % (t, f), [P, PAIRS], F32, over, at, trail=trail)
             gather(plain_fingers[t, f][:], 0, t, f)
 
-        def dealt_tile(t):
-            tile_of_h(1, t, (2 * t, 2 * t + 1))
+        def gather_dealt(t):
             for f in range(2):
                 gather(dealt_fingers[f][:, t, :], 1, t, f)
 
-        def dealt_max(half):
-            z_bf = sbuf("z_bf1_%d" % half, [P, HALF, PACK], BF16, "z_bf1")
+        def dealt_max(half, over=""):
+            z_bf = sbuf("z_bf1_%d" % half, [P, HALF, PACK], BF16, over)
             j = slice(HALF * half, HALF * (half + 1))
             nc.vector.tensor_tensor(
                 z_bf[:].rearrange("p (d u) t -> p d t u", u=2),
@@ -275,16 +278,16 @@ def tile_list_grasp_pair_wrench_kernel(
             )
             return z_bf
 
-        z_moved = sbuf("z_moved", [P, PACK, PAIRS], BF16)
+        z_moved = sbuf("z_moved", [P, PACK, PAIRS], BF16, lead=2 * KIB, trail=4 * KIB)
 
-        def plain_max(t, after):
-            z_plain = sbuf("z_plain%d" % t, [P, PAIRS], BF16, after)
+        def plain_max(t, over, at=0):
+            z_plain = sbuf("z_plain%d" % t, [P, PAIRS], BF16, over, at)
             nc.vector.tensor_tensor(z_plain[:], plain_fingers[t, 0][:], plain_fingers[t, 1][:], ALU.max)
             for x in range(PACK):
                 nc.sync.dma_start(out=z_moved[32 * t : 32 * (t + 1), x, :], in_=z_plain[x:P:PACK, :])
 
-        def quantize_z(z_bf, b, half, after=""):
-            z_code[b, half] = sbuf("z_code%d%d" % (b, half), [P, HALF], U32, after)
+        def quantize_z(z_bf, b, half, over=""):
+            z_code[b, half] = sbuf("z_code%d%d" % (b, half), [P, HALF], U32, over)
             z_scale[b, half] = sbuf("z_scale%d%d" % (b, half), [P, HALF], U8)
             quantize(z_code[b, half][:], z_scale[b, half][:], z_bf.rearrange("p j x -> p (j x)"))
 
@@ -297,95 +300,112 @@ def tile_list_grasp_pair_wrench_kernel(
             for c in range(n0 // P, n1 // P):
                 ws_q[b, c] = codes[:, P * c - n0 : P * (c + 1) - n0], scales[:, P * c - n0 : P * (c + 1) - n0]
 
-        m_acc, g_acc, gates = {}, {}, {}
+        acc, gates = {}, {}
 
-        def multiply_g(half, q, b, number=None):
+        def multiply(kind, half, q, b, number=None):
             if b == 0:
-                g_acc[half, q] = bank(number, [P, 2, HALF], "g_acc%d%d" % (half, q))
+                acc[kind, half, q] = bank(number, [P, 2, HALF], "%s_acc%d%d" % (kind, half, q))
             for e in range(2):
+                c = 2 * q + e
+                if kind == "g":
+                    codes, scales = ws_q[b, c][0].bitcast(FP8X4), ws_q[b, c][1]
+                else:
+                    codes = wm_sb[:, b, 2 * P * c : 2 * P * (c + 1)].bitcast(FP4X4)
+                    scales = wm_scale[:, b, P // 4 * c : P // 4 * (c + 1)].bitcast(U8)
                 nc.tensor.matmul_mx(
-                    out=g_acc[half, q][:, e, :],
-                    lhsT=ws_q[b, 2 * q + e][0].bitcast(FP8X4),
-                    lhsT_scale=ws_q[b, 2 * q + e][1],
+                    out=acc[kind, half, q][:, e, :],
+                    lhsT=codes,
+                    lhsT_scale=scales,
                     rhs=z_code[b, half][:].bitcast(FP8X4),
                     rhs_scale=z_scale[b, half][:],
                     start=(b, e) == (0, 0),
                     stop=(b, e) == (1, 1),
                 )
 
-        def multiply_m(half, q, b, number=None):
-            if b == 0:
-                m_acc[half, q] = bank(number, [P, 2, HALF], "m_acc%d%d" % (half, q))
-            for e in range(2):
-                c = 2 * q + e
-                for piece in range(HALF // P):
-                    cols = slice(P * piece, P * (piece + 1))
-                    nc.tensor.matmul_mx(
-                        out=m_acc[half, q][:, e, cols],
-                        lhsT=wm_sb[:, b, 2 * P * c : 2 * P * (c + 1)].bitcast(FP4X4),
-                        lhsT_scale=wm_scale[:, b, P // 4 * c : P // 4 * (c + 1)].bitcast(U8),
-                        rhs=z_code[b, half][:, cols].bitcast(FP8X4),
-                        rhs_scale=z_scale[b, half][:, cols],
-                        start=(b, e, piece) == (0, 0, 0),
-                        stop=(b, e, piece) == (1, 1, 1),
-                    )
-
         def gate(half, q):
             gates[half, q] = sbuf("gate%d%d" % (half, q), [P, 2, HALF], F32, "h%d%d" % (half, q))
             for e in range(2):
                 c = 2 * q + e
                 nc.scalar.activation(
-                    gates[half, q][:, e, :], g_acc[half, q][:, e, :], ACT.Sigmoid, bias=bs_sb[:, c : c + 1]
+                    gates[half, q][:, e, :], acc["g", half, q][:, e, :], ACT.Sigmoid, bias=bs_sb[:, c : c + 1]
                 )
 
         def finish(half, q, e0=0, e1=2):
             result = gates[half, q][:, e0:e1, :]
-            nc.vector.tensor_tensor(result, m_acc[half, q][:, e0:e1, :], result, ALU.mult)
+            nc.vector.tensor_tensor(result, acc["m", half, q][:, e0:e1, :], result, ALU.mult)
             rows = slice(P * (2 * q + e0), P * (2 * q + e1))
             nc.sync.dma_start(
                 out=out[rows, HALF * half : HALF * (half + 1)].rearrange("(e p) j -> p e j", p=P), in_=result
             )
 
-        quantize_first(0, ((nc.vector, 0, P),))
-        gather_last_words(0)
-        quantize_first(1, ((nc.scalar, 0, P // 2), (nc.gpsimd, P // 2, P)))
-        gather_last_words(1, "plain_raw01")
-        tile_of_h(0, 0, (0, 1, 5))
-
-        ring_a, ring_b, ring_c = "plain_bf1", "plain_raw11", "plain_finger01"
-        quantize_plain(1, (nc.scalar, nc.gpsimd))
-        gather_plain(0, 0, ring_b)
-        gather_plain(0, 1)
-        tile_of_h(0, 1, (2, 3))
-        quantize_plain(2, (nc.gpsimd, nc.gpsimd), ring_a)
+        both = ((nc.scalar, 0, P // 2), (nc.gpsimd, P // 2, P))
+        alone = ((nc.gpsimd, 0, P),)
+        cut = BANK + BANK // 2
+        first_parts = ((0, 0, BANK), (1, BANK, cut), (2, cut, S))
+        gather_words(0, 0, S)
+        gather_words(1, 0, BANK)
+        quantize_w1("00", round_pass(0, 0, both), [(0, 0, 0)])
+        multiply_h(0, 0, 0, first_parts)
+        gather_words(1, BANK, cut, "plain_bf00")
+        quantize_w1("01", round_pass(0, 1, both), [(0, 0, 1)])
+        gather_words(1, cut, S, "plain_bf01")
+        multiply_h(0, 0, 1, first_parts)
+        empty_h(0, 0, first_parts, on_vector=BANK)
+        quantize_w1("10", round_pass(1, 0, alone, trail=KIB), [(0, 1, 0)])
+        multiply_h(0, 1, 0, sides(3, 4))
+        rounded = round_pass(1, 1, alone, lead=3 * KIB // 2, trail=3 * KIB // 2)
+        gather_plain(0, 0, "plain_bf10")
+        quantize_w1("11", rounded, [(0, 1, 1)])
+        rounded = round_plain(2, (nc.scalar, nc.gpsimd), "plain_bf11", KIB // 2)
+        multiply_h(0, 1, 1, sides(3, 4))
+        empty_h(0, 1, sides(3, 4))
+        gather_plain(0, 1, "plain_bf11", -3 * KIB // 2)
+        quantize_w1("2", rounded, [(0, 2, 0), (0, 2, 1)])
         plain_max(0, "plain_raw21")
         load_ws(1)
-        gather_plain(1, 0, ring_a)
-        gather_plain(1, 1, ring_b)
-        tile_of_h(0, 2, (4, 5))
-        quantize_plain(3, (nc.gpsimd, nc.gpsimd), ring_c)
+        for a in range(PASSES):
+            multiply_h(0, 2, a, sides(5, 6))
+        empty_h(0, 2, sides(5, 6))
+        rounded = round_plain(3, (nc.gpsimd, nc.gpsimd), "finger01")
+        gather_plain(1, 0, "plain_bf2")
+        gather_plain(1, 1, "finger00")
+        quantize_w1("3", rounded, [(0, 3, 0), (0, 3, 1)])
         plain_max(1, "plain_raw31")
-        gather_plain(2, 0, ring_c)
-        gather_plain(2, 1, ring_a)
-        quantize_dealt(0, "bias_last_of_2")
-        tile_of_h(0, 3, (4, 5))
-        gather_plain(3, 0, ring_b)
-        plain_max(2, "b1_03")
-        gather_plain(3, 1, ring_c)
-        quantize_dealt(1, "bias_last_of_2")
+        for a in range(PASSES):
+            multiply_h(0, 3, a, sides(7, 0))
+        rounded = round_dealt(0, 0, PACK, "bias_last0")
+        gather_plain(2, 0, "plain_bf3")
+        gather_plain(2, 1, "finger10")
+        quantize_w1("d0", rounded, [(1, t, 0) for t in range(PACK)])
+        plain_max(2, "dealt_raw0", 4 * KIB)
+        for t in range(2):
+            multiply_h(1, t, 0, sides(2 * t + 1, 2 * t + 2))
+        quantize_w1("d10", round_dealt(1, 0, 2), [(1, 0, 1), (1, 1, 1)])
+        for t in range(2):
+            multiply_h(1, t, 1, sides(2 * t + 1, 2 * t + 2))
+        empty_h(0, 3, sides(7, 0), "dealt_raw0")
+        rounded = round_dealt(1, 2, PACK)
+        gather_plain(3, 0, trail=4 * KIB)
+        gather_plain(3, 1, trail=2 * KIB)
+        quantize_w1("d12", rounded, [(1, 2, 1), (1, 3, 1)])
         plain_max(3, "dealt_raw1")
-        load_bias(1, 3, 4)
-        load_wm_and_bs()
+        load_wm()
 
-        ws_first = sbuf("ws_first", [P, WIDE, PACK], BF16, ring_c)
+        ws_first = sbuf("ws_first", [P, WIDE, PACK], BF16, "finger31")
         round_rows(nc.gpsimd, ws_first[:], ws_raw[0][:, :, 0:WIDE])
-        dealt_tile(0)
-        dealt_tile(1)
+        for t in range(2):
+            empty_h(1, t, sides(2 * t + 1, 2 * t + 2))
+        for t, banks in ((2, sides(7, 0)), (3, sides(1, 2))):
+            for a in range(PASSES):
+                multiply_h(1, t, a, banks)
+        gather_dealt(0)
+        gather_dealt(1)
         quantize_ws(0, 0, WIDE, ws_first[:])
         rest = N - WIDE
-        joined = sbuf("joined", [P, rest + PAIRS, PACK], BF16, ring_b)
+        joined = sbuf("joined", [P, rest + PAIRS, PACK], BF16, "finger30")
         round_rows(nc.scalar, joined[:, 0:rest, :], ws_raw[0][:, :, WIDE:N])
-        dealt_tile(2)
+        empty_h(1, 2, sides(7, 0))
+        gather_dealt(2)
         woven = joined[:, rest:, :]
         round_rows(nc.scalar, woven, z_moved[:])
         codes = sbuf("joined_code", [P, rest + HALF], U32)
@@ -394,46 +414,47 @@ def tile_list_grasp_pair_wrench_kernel(
         for e in range(rest // P):
             ws_q[0, WIDE // P + e] = codes[:, P * e : P * (e + 1)], scales[:, P * e : P * (e + 1)]
         z_code[0, 0], z_scale[0, 0] = codes[:, rest:], scales[:, rest:]
-        dealt_tile(3)
+        empty_h(1, 3, sides(1, 2), "z_moved", -2 * KIB)
+        gather_dealt(3)
 
-        quantize_z(woven[:, HALF:PAIRS, :], 0, 1, "b1_13")
-        ws_last = sbuf("ws_last", [P, N, PACK], BF16, "z_moved")
+        quantize_z(woven[:, HALF:PAIRS, :], 0, 1, "bias_last1")
+        ws_last = sbuf("ws_last", [P, N, PACK], BF16, "z_moved", 2 * KIB)
         z_bf = dealt_max(0)
         round_rows(nc.scalar, ws_last[:, 0:WIDE, :], ws_raw[1][:, :, 0:WIDE])
         quantize_ws(1, 0, WIDE, ws_last[:, 0:WIDE, :])
         for q in range(COUPLES):
-            multiply_g(0, q, 0, q)
+            multiply("g", 0, q, 0, q)
         for q in range(COUPLES):
-            multiply_m(0, q, 0, COUPLES + q)
+            multiply("m", 0, q, 0, COUPLES + q)
         for q in range(COUPLES - 1):
-            multiply_m(1, q, 0, 2 * COUPLES + q)
+            multiply("m", 1, q, 0, 2 * COUPLES + q)
         quantize_z(z_bf[:], 1, 0)
         round_rows(nc.scalar, ws_last[:, WIDE:N, :], ws_raw[1][:, :, WIDE:N])
         quantize_ws(1, WIDE, N, ws_last[:, WIDE:N, :])
         for q in range(COUPLES):
-            multiply_g(0, q, 1)
+            multiply("g", 0, q, 1)
             gate(0, q)
-            multiply_m(0, q, 1)
-        z_bf = dealt_max(1)
+            multiply("m", 0, q, 1)
+        z_bf = dealt_max(1, "z_bf1_0")
         finish(0, 0, 0, 1)
         last = COUPLES - 1
         for q in range(last):
-            multiply_g(1, q, 0, q)
+            multiply("g", 1, q, 0, q)
         quantize_z(z_bf[:], 1, 1)
         finish(0, 0, 1, 2)
         for q in range(1, COUPLES):
             finish(0, q)
-        multiply_g(1, 0, 1)
+        multiply("g", 1, 0, 1)
         gate(1, 0)
-        multiply_m(1, 0, 1)
-        multiply_g(1, 1, 1)
+        multiply("m", 1, 0, 1)
+        multiply("g", 1, 1, 1)
         gate(1, 1)
-        multiply_g(1, last, 0, last)
-        multiply_g(1, last, 1)
+        multiply("g", 1, last, 0, last)
+        multiply("g", 1, last, 1)
         gate(1, last)
-        multiply_m(1, 1, 1)
-        multiply_m(1, last, 0, COUPLES)
-        multiply_m(1, last, 1)
+        multiply("m", 1, 1, 1)
+        multiply("m", 1, last, 0, COUPLES)
+        multiply("m", 1, last, 1)
         for q in range(COUPLES):
             for e in range(2):
                 finish(1, q, e, e + 1)

@@ -216,10 +216,11 @@ def tile_list_grasp_pair_wrench_kernel(
 
         def round_dealt(a, t0, t1, over=""):
             rounded = sbuf("dealt_bf%d%d" % (a, t0), [P, t1 - t0, P, PACK], BF16, over)
-            nc.scalar.copy(
-                rounded[:].rearrange("p t m x -> p m x t"),
-                dealt_raw[a][:].rearrange("p x (m t) -> p m x t", t=PACK)[:, :, :, t0:t1],
-            )
+            for t in range(t0, t1, 2):
+                nc.scalar.copy(
+                    rounded[:, t - t0 : t - t0 + 2, :, :].rearrange("p t m x -> p m x t"),
+                    dealt_raw[a][:].rearrange("p x (m t) -> p m x t", t=PACK)[:, :, :, t : t + 2],
+                )
             return rounded[:].rearrange("p t m x -> p (t m x)")
 
         h, h_acc = {}, {}

@@ -89,6 +89,8 @@ def tile_list_grasp_pair_wrench_kernel(
         make_identity(nc, identity[:])
         nc.sync.dma_start(out=bias_rows[b1_row:P, :], in_=b1.rearrange("(b r) -> b r", b=PASSES))
         nc.sync.dma_start(out=bias_rows[bs_row:b1_row, 0 : N // 2], in_=bs.rearrange("(u n) -> u n", u=2))
+        nc.sync.dma_start(pos1_sb[:], pos1)
+        nc.sync.dma_start(pos2_sb[:], pos2)
         load_words(1)
         turned = [bank(6 + b, [P, PACK, P], "turned%d" % b) for b in range(PASSES)]
         for t in range(PACK):
@@ -96,14 +98,14 @@ def tile_list_grasp_pair_wrench_kernel(
         for t in range(PACK):
             nc.tensor.transpose(turned[1][:, t, :], bias_rows[:, t:PASS:PACK], identity[:])
         bias_of = {}
-        for b, own, room in ((0, 2, 4 * KIB), (1, 3, KIB)):
+        for b in range(PASSES):
             columns = sbuf("bias_columns%d" % b, [P, PACK], F32)
             nc.scalar.copy(columns[:], turned[b][:, :, b1_row + b])
             for t in range(PACK):
                 bias_of[b, t] = [columns[:, t : t + 1]] * 2
-            last = sbuf("bias_last%d" % b, [P, 1], F32, trail=room)
-            nc.scalar.copy(last[:], turned[b][:, own, b1_row + b : b1_row + b + 1])
-            bias_of[b, own] = [columns[:, own : own + 1], last[:]]
+        bias_last = sbuf("bias_last1", [P, 1], F32, trail=KIB)
+        nc.scalar.copy(bias_last[:], turned[1][:, PACK - 1, P - 1 : P])
+        bias_of[1, PACK - 1] = [bias_of[1, PACK - 1][0], bias_last[:]]
         bs_sb = sbuf("bs_sb", [P, N // P], F32)
         nc.scalar.copy(
             bs_sb[:].rearrange("p (u t) -> p t u", u=2), turned[0][:, 0 : N // (2 * P), bs_row:b1_row]
@@ -111,8 +113,8 @@ def tile_list_grasp_pair_wrench_kernel(
 
         plain_raw = {}
 
-        def load_plain(t, a, tiles=1):
-            raw = sbuf("plain_raw%d%d" % (t, a), [P, PACK, tiles * P], F32)
+        def load_plain(t, a, tiles=1, margin=0):
+            raw = sbuf("plain_raw%d%d" % (t, a), [P, PACK, tiles * P], F32, lead=margin, trail=margin)
             nc.sync.dma_start(
                 out=raw[:],
                 in_=w1[PASS * a : PASS * (a + 1), P * t : P * (t + tiles)].rearrange("(p x) c -> p x c", x=PACK),
@@ -120,13 +122,14 @@ def tile_list_grasp_pair_wrench_kernel(
             for i in range(tiles):
                 plain_raw[t + i, a] = raw[:, :, P * i : P * (i + 1)]
 
-        dealt_raw = []
+        dealt_raw = {}
 
-        def load_dealt(a):
-            dealt_raw.append(sbuf("dealt_raw%d" % a, [P, PACK, PASS], F32))
+        def load_dealt(a, piece, width, lead=0):
+            dealt_raw[a, piece] = sbuf("dealt_raw%d%d" % (a, piece), [P, PACK, width], F32, lead=lead)
+            c0 = PASS + width * piece
             nc.sync.dma_start(
-                out=dealt_raw[a][:],
-                in_=w1[PASS * a : PASS * (a + 1), PASS:H].rearrange("(p x) c -> p x c", x=PACK),
+                out=dealt_raw[a, piece][:],
+                in_=w1[PASS * a : PASS * (a + 1), c0 : c0 + width].rearrange("(p x) c -> p x c", x=PACK),
             )
 
         ws_raw = []
@@ -138,6 +141,7 @@ def tile_list_grasp_pair_wrench_kernel(
             )
 
         load_plain(0, 0)
+        load_plain(0, 1)
         picked_scale = sbuf("picked_scale", [P, S], U8)
         nc.vector.tensor_copy(picked_scale[:], scale_window[:].bitcast(U8).indirect(offs_sb[:]))
         for quad in range(QUADS):
@@ -145,16 +149,14 @@ def tile_list_grasp_pair_wrench_kernel(
                 out=v_scale[32 * quad : 32 * quad + 4, :, :].bitcast(I32),
                 in_=picked_scale[8 * quad : 8 * quad + 8, :].bitcast(I32),
             )
-        load_plain(0, 1)
         load_plain(1, 0)
-        load_plain(1, 1)
-        nc.sync.dma_start(pos1_sb[:], pos1)
-        nc.sync.dma_start(pos2_sb[:], pos2)
+        load_plain(1, 1, margin=KIB)
         load_plain(2, 0, tiles=2)
         load_plain(2, 1)
         load_plain(3, 1)
-        load_dealt(0)
-        load_dealt(1)
+        load_dealt(0, 0, PASS // 2)
+        load_dealt(0, 1, PASS // 2, lead=KIB)
+        load_dealt(1, 0, PASS)
         load_ws(0)
         wm_sb = sbuf("wm_sb", [P, PASSES, 2 * N], U8)
 
@@ -202,25 +204,31 @@ def tile_list_grasp_pair_wrench_kernel(
             for i, part in enumerate(parts):
                 stationary[part] = codes[:, P * i : P * (i + 1)], scales[:, P * i : P * (i + 1)]
 
-        def round_pass(t, a, shares, lead=0, trail=0):
-            rounded = sbuf("plain_bf%d%d" % (t, a), [P, P, PACK], BF16, lead=lead, trail=trail)
+        def round_pass(t, a, shares):
+            rounded = sbuf("plain_bf%d%d" % (t, a), [P, P, PACK], BF16)
             for engine, c0, c1 in shares:
                 round_rows(engine, rounded[:, c0:c1, :], plain_raw[t, a][:, :, c0:c1])
             return rounded[:].rearrange("p c x -> p (c x)")
 
-        def round_plain(t, engines, over, at=0):
-            rounded = sbuf("plain_bf%d" % t, [P, PASSES, P, PACK], BF16, over, at)
+        def round_plain(t, engines, over=""):
+            rounded = sbuf("plain_bf%d" % t, [P, PASSES, P, PACK], BF16, over)
             for a in range(PASSES):
                 round_rows(engines[a], rounded[:, a, :, :], plain_raw[t, a])
             return rounded[:].rearrange("p a c x -> p (a c x)")
 
-        def round_dealt(a, t0, t1, over=""):
-            rounded = sbuf("dealt_bf%d%d" % (a, t0), [P, t1 - t0, P, PACK], BF16, over)
-            for t in range(t0, t1, 2):
-                nc.scalar.copy(
-                    rounded[:, t - t0 : t - t0 + 2, :, :].rearrange("p t m x -> p m x t"),
-                    dealt_raw[a][:].rearrange("p x (m t) -> p m x t", t=PACK)[:, :, :, t : t + 2],
-                )
+        def deal(rounded, raw, t):
+            nc.scalar.copy(
+                rounded.rearrange("p t m x -> p m x t"),
+                raw.rearrange("p x (m t) -> p m x t", t=PACK)[:, :, :, t : t + 2],
+            )
+
+        def round_dealt_first(rounded, piece):
+            for t in range(0, PACK, 2):
+                deal(rounded[:, t : t + 2, P // 2 * piece : P // 2 * (piece + 1), :], dealt_raw[0, piece][:], t)
+
+        def round_dealt_last(t):
+            rounded = sbuf("dealt_bf1%d" % t, [P, 2, P, PACK], BF16)
+            deal(rounded[:], dealt_raw[1, 0][:], t)
             return rounded[:].rearrange("p t m x -> p (t m x)")
 
         h, h_acc = {}, {}
@@ -340,33 +348,34 @@ def tile_list_grasp_pair_wrench_kernel(
             )
 
         both = ((nc.scalar, 0, P // 2), (nc.gpsimd, P // 2, P))
-        alone = ((nc.gpsimd, 0, P),)
         cut = BANK + BANK // 2
         first_parts = ((0, 0, BANK), (1, BANK, cut), (2, cut, S))
         gather_words(0, 0, S)
         gather_words(1, 0, BANK)
         quantize_w1("00", round_pass(0, 0, both), [(0, 0, 0)])
-        multiply_h(0, 0, 0, first_parts)
-        gather_words(1, BANK, cut, "plain_bf00")
+        gather_words(1, BANK, cut, "plain_raw00")
         quantize_w1("01", round_pass(0, 1, both), [(0, 0, 1)])
-        gather_words(1, cut, S, "plain_bf01")
-        multiply_h(0, 0, 1, first_parts)
+        gather_words(1, cut, S, "plain_raw01")
+        for part in first_parts:
+            for a in range(PASSES):
+                multiply_h(0, 0, a, [part])
+        rounded = round_plain(1, (nc.scalar, nc.gpsimd))
         empty_h(0, 0, first_parts, on_vector=BANK)
-        quantize_w1("10", round_pass(1, 0, alone, trail=KIB), [(0, 1, 0)])
-        multiply_h(0, 1, 0, sides(3, 4))
-        rounded = round_pass(1, 1, alone, lead=3 * KIB // 2, trail=3 * KIB // 2)
-        gather_plain(0, 0, "plain_bf10")
-        quantize_w1("11", rounded, [(0, 1, 1)])
-        rounded = round_plain(2, (nc.scalar, nc.gpsimd), "plain_bf11", KIB // 2)
-        multiply_h(0, 1, 1, sides(3, 4))
+        quantize_w1("1", rounded, [(0, 1, 0), (0, 1, 1)])
+        for a in range(PASSES):
+            multiply_h(0, 1, a, sides(3, 4))
         empty_h(0, 1, sides(3, 4))
-        gather_plain(0, 1, "plain_bf11", -3 * KIB // 2)
+        rounded = round_plain(2, (nc.gpsimd, nc.gpsimd), "plain_bf1")
+        gather_plain(0, 0, "plain_raw11", -KIB)
+        gather_plain(0, 1, "plain_raw11", KIB)
         quantize_w1("2", rounded, [(0, 2, 0), (0, 2, 1)])
         plain_max(0, "plain_raw21")
         load_ws(1)
         for a in range(PASSES):
             multiply_h(0, 2, a, sides(5, 6))
-        empty_h(0, 2, sides(5, 6))
+        dealt_first = sbuf("dealt_bf0", [P, PACK, P, PACK], BF16)
+        round_dealt_first(dealt_first, 0)
+        empty_h(0, 2, sides(5, 6), "dealt_raw00")
         rounded = round_plain(3, (nc.gpsimd, nc.gpsimd), "finger01")
         gather_plain(1, 0, "plain_bf2")
         gather_plain(1, 1, "finger00")
@@ -374,22 +383,23 @@ def tile_list_grasp_pair_wrench_kernel(
         plain_max(1, "plain_raw31")
         for a in range(PASSES):
             multiply_h(0, 3, a, sides(7, 0))
-        rounded = round_dealt(0, 0, PACK, "bias_last0")
+        round_dealt_first(dealt_first, 1)
+        rounded = dealt_first[:].rearrange("p t m x -> p (t m x)")
         gather_plain(2, 0, "plain_bf3")
         gather_plain(2, 1, "finger10")
         quantize_w1("d0", rounded, [(1, t, 0) for t in range(PACK)])
-        plain_max(2, "dealt_raw0", 4 * KIB)
+        plain_max(2, "dealt_raw01", 3 * KIB)
         for t in range(2):
             multiply_h(1, t, 0, sides(2 * t + 1, 2 * t + 2))
-        quantize_w1("d10", round_dealt(1, 0, 2), [(1, 0, 1), (1, 1, 1)])
+        quantize_w1("d10", round_dealt_last(0), [(1, 0, 1), (1, 1, 1)])
         for t in range(2):
             multiply_h(1, t, 1, sides(2 * t + 1, 2 * t + 2))
-        empty_h(0, 3, sides(7, 0), "dealt_raw0")
-        rounded = round_dealt(1, 2, PACK)
+        empty_h(0, 3, sides(7, 0), "dealt_raw01", -KIB)
+        rounded = round_dealt_last(2)
         gather_plain(3, 0, trail=4 * KIB)
         gather_plain(3, 1, trail=2 * KIB)
         quantize_w1("d12", rounded, [(1, 2, 1), (1, 3, 1)])
-        plain_max(3, "dealt_raw1")
+        plain_max(3, "dealt_raw10")
         load_wm()
 
         ws_first = sbuf("ws_first", [P, WIDE, PACK], BF16, "finger31")

@@ -64,7 +64,7 @@ def tile_list_grasp_pair_wrench_kernel(
         pos1_sb = lists.tile([P, PAIRS // PER_COLUMN], U16, name="pos1_sb")
         pos2_sb = lists.tile([P, PAIRS // PER_COLUMN], U16, name="pos2_sb")
 
-        scale_window = sbuf("scale_window", [P, T // 4], I32)
+        scale_window = sbuf("scale_window", [P, T // 4], I32, trail=12 * KIB)
         wm_scale = sbuf("wm_scale", [P, PASSES, N // 4], I32)
         v_scale = sbuf("v_scale", [P, PASSES, S], U8)
         nc.vector.memset(scale_window[32:64, :], 0)
@@ -74,12 +74,12 @@ def tile_list_grasp_pair_wrench_kernel(
 
         nc.sync.dma_start(offs_sb[:], offs)
         nc.sync.dma_start(out=scale_window[0:32, :], in_=tab_scales.bitcast(I32).rearrange("a g w -> g a w"))
-        word_window = [sbuf("word_window%d" % a, [P, T], I32) for a in range(PASSES)]
+        word_window = {}
 
-        def load_words(a):
+        def load_words(a, over=""):
+            word_window[a] = sbuf("word_window%d" % a, [P, T], I32, over)
             nc.sync.dma_start(out=word_window[a][:], in_=tab_words[a].rearrange("p t x -> p (t x)").bitcast(I32))
 
-        load_words(0)
         bias_rows = sbuf("bias_rows", [P, PASS], F32)
         identity = sbuf("identity", [P, P], F32)
         b1_row = P - PASSES
@@ -89,9 +89,7 @@ def tile_list_grasp_pair_wrench_kernel(
         make_identity(nc, identity[:])
         nc.sync.dma_start(out=bias_rows[b1_row:P, :], in_=b1.rearrange("(b r) -> b r", b=PASSES))
         nc.sync.dma_start(out=bias_rows[bs_row:b1_row, 0 : N // 2], in_=bs.rearrange("(u n) -> u n", u=2))
-        nc.sync.dma_start(pos1_sb[:], pos1)
-        nc.sync.dma_start(pos2_sb[:], pos2)
-        load_words(1)
+        load_words(0)
         turned = [bank(6 + b, [P, PACK, P], "turned%d" % b) for b in range(PASSES)]
         for t in range(PACK):
             nc.tensor.transpose(turned[0][:, t, :], bias_rows[:, P * t : P * (t + 1)], identity[:])
@@ -141,7 +139,6 @@ def tile_list_grasp_pair_wrench_kernel(
             )
 
         load_plain(0, 0)
-        load_plain(0, 1)
         picked_scale = sbuf("picked_scale", [P, S], U8)
         nc.vector.tensor_copy(picked_scale[:], scale_window[:].bitcast(U8).indirect(offs_sb[:]))
         for quad in range(QUADS):
@@ -149,8 +146,12 @@ def tile_list_grasp_pair_wrench_kernel(
                 out=v_scale[32 * quad : 32 * quad + 4, :, :].bitcast(I32),
                 in_=picked_scale[8 * quad : 8 * quad + 8, :].bitcast(I32),
             )
+        load_words(1, "scale_window")
+        load_plain(0, 1, margin=KIB // 2)
         load_plain(1, 0)
         load_plain(1, 1, margin=KIB)
+        nc.sync.dma_start(pos1_sb[:], pos1)
+        nc.sync.dma_start(pos2_sb[:], pos2)
         load_plain(2, 0, tiles=2)
         load_plain(2, 1)
         load_plain(3, 1)
@@ -170,8 +171,8 @@ def tile_list_grasp_pair_wrench_kernel(
 
         v_words = {}
 
-        def gather_words(a, c0, c1, over=""):
-            words = sbuf("v_words%d_%d" % (a, c0), [P, c1 - c0], U32, over)
+        def gather_words(a, c0, c1, over="", at=0):
+            words = sbuf("v_words%d_%d" % (a, c0), [P, c1 - c0], U32, over, at)
             entries = slice(c0 // PER_COLUMN, c1 // PER_COLUMN)
             nc.vector.tensor_copy(words[:], word_window[a][:].bitcast(U32).indirect(offs_sb[:, entries]))
             v_words[a, c0] = words
@@ -351,14 +352,13 @@ def tile_list_grasp_pair_wrench_kernel(
         cut = BANK + BANK // 2
         first_parts = ((0, 0, BANK), (1, BANK, cut), (2, cut, S))
         gather_words(0, 0, S)
-        gather_words(1, 0, BANK)
         quantize_w1("00", round_pass(0, 0, both), [(0, 0, 0)])
-        gather_words(1, BANK, cut, "plain_raw00")
+        multiply_h(0, 0, 0, first_parts)
+        gather_words(1, 0, BANK)
         quantize_w1("01", round_pass(0, 1, both), [(0, 0, 1)])
-        gather_words(1, cut, S, "plain_raw01")
-        for part in first_parts:
-            for a in range(PASSES):
-                multiply_h(0, 0, a, [part])
+        gather_words(1, BANK, cut, "plain_raw01", -KIB // 2)
+        gather_words(1, cut, S, "plain_raw01", KIB // 2)
+        multiply_h(0, 0, 1, first_parts)
         rounded = round_plain(1, (nc.scalar, nc.gpsimd))
         empty_h(0, 0, first_parts, on_vector=BANK)
         quantize_w1("1", rounded, [(0, 1, 0), (0, 1, 1)])

@@ -72,24 +72,33 @@ def tile_list_grasp_pair_wrench_kernel(
         nc.vector.memset(v_scale[:].rearrange("p a s -> p (a s)").bitcast(I32), 0)
         nc.vector.memset(wm_scale[:], 0)
 
-        nc.sync.dma_start(offs_sb[:], offs)
         nc.sync.dma_start(out=scale_window[0:32, :], in_=tab_scales.bitcast(I32).rearrange("a g w -> g a w"))
+        nc.sync.dma_start(offs_sb[:], offs)
         word_window = {}
 
         def load_words(a, over=""):
             word_window[a] = sbuf("word_window%d" % a, [P, T], I32, over)
             nc.sync.dma_start(out=word_window[a][:], in_=tab_words[a].rearrange("p t x -> p (t x)").bitcast(I32))
 
+        plain_raw = {}
+
+        def load_plain(t, a, tiles=1, margin=0):
+            raw = sbuf("plain_raw%d%d" % (t, a), [P, PACK, tiles * P], F32, lead=margin, trail=margin)
+            nc.sync.dma_start(
+                out=raw[:],
+                in_=w1[PASS * a : PASS * (a + 1), P * t : P * (t + tiles)].rearrange("(p x) c -> p x c", x=PACK),
+            )
+            for i in range(tiles):
+                plain_raw[t + i, a] = raw[:, :, P * i : P * (i + 1)]
+
         bias_rows = sbuf("bias_rows", [P, PASS], F32)
         identity = sbuf("identity", [P, P], F32)
         b1_row = P - PASSES
-        bs_row = b1_row - 2
-        nc.gpsimd.memset(bias_rows[0:bs_row, 0 : N // 2], 0.0)
-        nc.gpsimd.memset(bias_rows[0:b1_row, N // 2 : PASS], 0.0)
+        nc.gpsimd.memset(bias_rows[0:b1_row, :], 0.0)
         make_identity(nc, identity[:])
-        nc.sync.dma_start(out=bias_rows[b1_row:P, :], in_=b1.rearrange("(b r) -> b r", b=PASSES))
-        nc.sync.dma_start(out=bias_rows[bs_row:b1_row, 0 : N // 2], in_=bs.rearrange("(u n) -> u n", u=2))
         load_words(0)
+        load_plain(0, 0)
+        nc.sync.dma_start(out=bias_rows[b1_row:P, :], in_=b1.rearrange("(b r) -> b r", b=PASSES))
         turned = [bank(6 + b, [P, PACK, P], "turned%d" % b) for b in range(PASSES)]
         for t in range(PACK):
             nc.tensor.transpose(turned[0][:, t, :], bias_rows[:, P * t : P * (t + 1)], identity[:])
@@ -105,20 +114,6 @@ def tile_list_grasp_pair_wrench_kernel(
         nc.scalar.copy(bias_last[:], turned[1][:, PACK - 1, P - 1 : P])
         bias_of[1, PACK - 1] = [bias_of[1, PACK - 1][0], bias_last[:]]
         bs_sb = sbuf("bs_sb", [P, N // P], F32)
-        nc.scalar.copy(
-            bs_sb[:].rearrange("p (u t) -> p t u", u=2), turned[0][:, 0 : N // (2 * P), bs_row:b1_row]
-        )
-
-        plain_raw = {}
-
-        def load_plain(t, a, tiles=1, margin=0):
-            raw = sbuf("plain_raw%d%d" % (t, a), [P, PACK, tiles * P], F32, lead=margin, trail=margin)
-            nc.sync.dma_start(
-                out=raw[:],
-                in_=w1[PASS * a : PASS * (a + 1), P * t : P * (t + tiles)].rearrange("(p x) c -> p x c", x=PACK),
-            )
-            for i in range(tiles):
-                plain_raw[t + i, a] = raw[:, :, P * i : P * (i + 1)]
 
         dealt_raw = {}
 
@@ -138,7 +133,6 @@ def tile_list_grasp_pair_wrench_kernel(
                 out=ws_raw[b][:], in_=ws[PASS * b : PASS * (b + 1), :].rearrange("(p x) n -> p x n", x=PACK)
             )
 
-        load_plain(0, 0)
         picked_scale = sbuf("picked_scale", [P, S], U8)
         nc.vector.tensor_copy(picked_scale[:], scale_window[:].bitcast(U8).indirect(offs_sb[:]))
         for quad in range(QUADS):
@@ -147,7 +141,7 @@ def tile_list_grasp_pair_wrench_kernel(
                 in_=picked_scale[8 * quad : 8 * quad + 8, :].bitcast(I32),
             )
         load_words(1, "scale_window")
-        load_plain(0, 1, margin=KIB // 2)
+        load_plain(0, 1)
         load_plain(1, 0)
         load_plain(1, 1, margin=KIB)
         nc.sync.dma_start(pos1_sb[:], pos1)
@@ -168,11 +162,13 @@ def tile_list_grasp_pair_wrench_kernel(
                     out=wm_scale[32 * quad : 32 * quad + 4, :, :],
                     in_=wm_scales[:, 4 * quad : 4 * quad + 4, :].bitcast(I32).rearrange("b row w -> row b w"),
                 )
+            with nc.allow_non_contiguous_dma(reason="one bias value for each partition and output tile"):
+                nc.sync.dma_start(out=bs_sb[:], in_=bs.rearrange("(c p) -> p c", p=P))
 
         v_words = {}
 
-        def gather_words(a, c0, c1, over="", at=0):
-            words = sbuf("v_words%d_%d" % (a, c0), [P, c1 - c0], U32, over, at)
+        def gather_words(a, c0, c1, over=""):
+            words = sbuf("v_words%d_%d" % (a, c0), [P, c1 - c0], U32, over)
             entries = slice(c0 // PER_COLUMN, c1 // PER_COLUMN)
             nc.vector.tensor_copy(words[:], word_window[a][:].bitcast(U32).indirect(offs_sb[:, entries]))
             v_words[a, c0] = words
@@ -354,14 +350,12 @@ def tile_list_grasp_pair_wrench_kernel(
         gather_words(0, 0, S)
         quantize_w1("00", round_pass(0, 0, both), [(0, 0, 0)])
         multiply_h(0, 0, 0, first_parts)
-        gather_words(1, 0, BANK)
+        gather_words(1, 0, cut)
         quantize_w1("01", round_pass(0, 1, both), [(0, 0, 1)])
-        gather_words(1, BANK, cut, "plain_raw01", -KIB // 2)
-        gather_words(1, cut, S, "plain_raw01", KIB // 2)
+        gather_words(1, cut, S, "plain_raw01")
         multiply_h(0, 0, 1, first_parts)
-        rounded = round_plain(1, (nc.scalar, nc.gpsimd))
-        empty_h(0, 0, first_parts, on_vector=BANK)
-        quantize_w1("1", rounded, [(0, 1, 0), (0, 1, 1)])
+        quantize_w1("1", round_plain(1, (nc.scalar, nc.gpsimd)), [(0, 1, 0), (0, 1, 1)])
+        empty_h(0, 0, first_parts, on_vector=cut)
         for a in range(PASSES):
             multiply_h(0, 1, a, sides(3, 4))
         empty_h(0, 1, sides(3, 4))
@@ -396,14 +390,14 @@ def tile_list_grasp_pair_wrench_kernel(
             multiply_h(1, t, 1, sides(2 * t + 1, 2 * t + 2))
         empty_h(0, 3, sides(7, 0), "dealt_raw01", -KIB)
         rounded = round_dealt_last(2)
-        gather_plain(3, 0, trail=4 * KIB)
-        gather_plain(3, 1, trail=2 * KIB)
+        gather_plain(3, 0)
+        gather_plain(3, 1, trail=8 * KIB)
         quantize_w1("d12", rounded, [(1, 2, 1), (1, 3, 1)])
         plain_max(3, "dealt_raw10")
         load_wm()
 
-        ws_first = sbuf("ws_first", [P, WIDE, PACK], BF16, "finger31")
-        round_rows(nc.gpsimd, ws_first[:], ws_raw[0][:, :, 0:WIDE])
+        joined = sbuf("joined", [P, N + PAIRS, PACK], BF16, "finger31")
+        round_rows(nc.gpsimd, joined[:, 0:N, :], ws_raw[0][:])
         for t in range(2):
             empty_h(1, t, sides(2 * t + 1, 2 * t + 2))
         for t, banks in ((2, sides(7, 0)), (3, sides(1, 2))):
@@ -411,10 +405,7 @@ def tile_list_grasp_pair_wrench_kernel(
                 multiply_h(1, t, a, banks)
         gather_dealt(0)
         gather_dealt(1)
-        quantize_ws(0, 0, WIDE, ws_first[:])
-        rest = N - WIDE
-        joined = sbuf("joined", [P, rest + PAIRS, PACK], BF16, "finger30")
-        round_rows(nc.scalar, joined[:, 0:rest, :], ws_raw[0][:, :, WIDE:N])
+        rest = N
         empty_h(1, 2, sides(7, 0))
         gather_dealt(2)
         woven = joined[:, rest:, :]
@@ -423,7 +414,7 @@ def tile_list_grasp_pair_wrench_kernel(
         scales = sbuf("joined_scale", [P, rest + HALF], U8)
         quantize(codes[:], scales[:], joined[:, 0 : rest + HALF, :].rearrange("p c x -> p (c x)"))
         for e in range(rest // P):
-            ws_q[0, WIDE // P + e] = codes[:, P * e : P * (e + 1)], scales[:, P * e : P * (e + 1)]
+            ws_q[0, e] = codes[:, P * e : P * (e + 1)], scales[:, P * e : P * (e + 1)]
         z_code[0, 0], z_scale[0, 0] = codes[:, rest:], scales[:, rest:]
         empty_h(1, 3, sides(1, 2), "z_moved", -2 * KIB)
         gather_dealt(3)

@@ -135,7 +135,7 @@ def tile_list_grasp_pair_wrench_kernel(
 
         picked_scale = sbuf("picked_scale", [P, S], U8)
         nc.vector.tensor_copy(picked_scale[:], scale_window[:].bitcast(U8).indirect(offs_sb[:]))
-        for quad in range(QUADS):
+        for quad in (0, 2, 1, 3):
             nc.sync.dma_start(
                 out=v_scale[32 * quad : 32 * quad + 4, :, :].bitcast(I32),
                 in_=picked_scale[8 * quad : 8 * quad + 8, :].bitcast(I32),

@@ -27,7 +27,7 @@ QUADS = 4
 PER_COLUMN = 16
 HALF = PAIRS // 2
 COUPLES = N // (2 * P)
-WIDE = 4 * P
+NARROW = 2 * P
 ALIGN = 64
 KIB = 1024
 
@@ -64,20 +64,18 @@ def tile_list_grasp_pair_wrench_kernel(
         pos1_sb = lists.tile([P, PAIRS // PER_COLUMN], U16, name="pos1_sb")
         pos2_sb = lists.tile([P, PAIRS // PER_COLUMN], U16, name="pos2_sb")
 
-        scale_window = sbuf("scale_window", [P, T // 4], I32, trail=12 * KIB)
-        wm_scale = sbuf("wm_scale", [P, PASSES, N // 4], I32)
+        scale_window = sbuf("scale_window", [P, T // 4], I32, trail=14 * KIB)
         v_scale = sbuf("v_scale", [P, PASSES, S], U8)
-        nc.vector.memset(scale_window[32:64, :], 0)
-        nc.vector.memset(scale_window[64:P, :], 0)
+        scale_row = P - 32
+        nc.vector.memset(scale_window[0:scale_row, :], 0)
         nc.vector.memset(v_scale[:].rearrange("p a s -> p (a s)").bitcast(I32), 0)
-        nc.vector.memset(wm_scale[:], 0)
 
-        nc.sync.dma_start(out=scale_window[0:32, :], in_=tab_scales.bitcast(I32).rearrange("a g w -> g a w"))
+        nc.sync.dma_start(out=scale_window[scale_row:P, :], in_=tab_scales.bitcast(I32).rearrange("a g w -> g a w"))
         nc.sync.dma_start(offs_sb[:], offs)
         word_window = {}
 
-        def load_words(a, over=""):
-            word_window[a] = sbuf("word_window%d" % a, [P, T], I32, over)
+        def load_words(a, over="", at=0):
+            word_window[a] = sbuf("word_window%d" % a, [P, T], I32, over, at)
             nc.sync.dma_start(out=word_window[a][:], in_=tab_words[a].rearrange("p t x -> p (t x)").bitcast(I32))
 
         plain_raw = {}
@@ -94,7 +92,7 @@ def tile_list_grasp_pair_wrench_kernel(
         bias_rows = sbuf("bias_rows", [P, PASS], F32)
         identity = sbuf("identity", [P, P], F32)
         b1_row = P - PASSES
-        nc.gpsimd.memset(bias_rows[0:b1_row, :], 0.0)
+        nc.vector.memset(bias_rows[0:b1_row, :], 0.0)
         make_identity(nc, identity[:])
         load_words(0)
         load_plain(0, 0)
@@ -138,9 +136,11 @@ def tile_list_grasp_pair_wrench_kernel(
         for quad in (0, 2, 1, 3):
             nc.sync.dma_start(
                 out=v_scale[32 * quad : 32 * quad + 4, :, :].bitcast(I32),
-                in_=picked_scale[8 * quad : 8 * quad + 8, :].bitcast(I32),
+                in_=picked_scale[scale_row + 8 * quad : scale_row + 8 * (quad + 1), :].bitcast(I32),
             )
-        load_words(1, "scale_window")
+        load_words(1, "scale_window", 2 * KIB)
+        wm_scale = sbuf("wm_scale", [P, PASSES, N // 4], I32, "scale_window")
+        nc.vector.memset(wm_scale[:], 0)
         load_plain(0, 1)
         load_plain(1, 0)
         load_plain(1, 1, margin=KIB)
@@ -219,14 +219,21 @@ def tile_list_grasp_pair_wrench_kernel(
                 raw.rearrange("p x (m t) -> p m x t", t=PACK)[:, :, :, t : t + 2],
             )
 
-        def round_dealt_first(rounded, piece):
+        slots = [(1, t, a) for t, a in ((2, 0), (3, 0), (0, 0), (1, 0), (0, 1), (1, 1), (2, 1), (3, 1))]
+        dealt_bf = sbuf("dealt_bf", [P, len(slots), P, PACK], BF16)
+
+        def round_dealt_first(piece):
             for t in range(0, PACK, 2):
-                deal(rounded[:, t : t + 2, P // 2 * piece : P // 2 * (piece + 1), :], dealt_raw[0, piece][:], t)
+                slot = slots.index((1, t, 0))
+                columns = slice(P // 2 * piece, P // 2 * (piece + 1))
+                deal(dealt_bf[:, slot : slot + 2, columns, :], dealt_raw[0, piece][:], t)
 
         def round_dealt_last(t):
-            rounded = sbuf("dealt_bf1%d" % t, [P, 2, P, PACK], BF16)
-            deal(rounded[:], dealt_raw[1, 0][:], t)
-            return rounded[:].rearrange("p t m x -> p (t m x)")
+            slot = slots.index((1, t, 1))
+            deal(dealt_bf[:, slot : slot + 2, :, :], dealt_raw[1, 0][:], t)
+
+        def quantize_dealt(s0, s1):
+            quantize_w1("d%d" % s0, dealt_bf[:, s0:s1, :, :].rearrange("p s m x -> p (s m x)"), slots[s0:s1])
 
         h, h_acc = {}, {}
 
@@ -308,10 +315,12 @@ def tile_list_grasp_pair_wrench_kernel(
 
         acc, gates = {}, {}
 
-        def multiply(kind, half, q, b, number=None):
+        def multiply(kind, half, q, b, number=None, e0=0, e1=2):
             if b == 0:
-                acc[kind, half, q] = bank(number, [P, 2, HALF], "%s_acc%d%d" % (kind, half, q))
-            for e in range(2):
+                sums = bank(number, [P, e1 - e0, HALF], "%s_acc%d%d%d" % (kind, half, q, e0))
+                for e in range(e0, e1):
+                    acc[kind, half, q, e] = sums[:, e - e0 : e1 - e0, :]
+            for e in range(e0, e1):
                 c = 2 * q + e
                 if kind == "g":
                     codes, scales = ws_q[b, c][0].bitcast(FP8X4), ws_q[b, c][1]
@@ -319,13 +328,13 @@ def tile_list_grasp_pair_wrench_kernel(
                     codes = wm_sb[:, b, 2 * P * c : 2 * P * (c + 1)].bitcast(FP4X4)
                     scales = wm_scale[:, b, P // 4 * c : P // 4 * (c + 1)].bitcast(U8)
                 nc.tensor.matmul_mx(
-                    out=acc[kind, half, q][:, e, :],
+                    out=acc[kind, half, q, e][:, 0, :],
                     lhsT=codes,
                     lhsT_scale=scales,
                     rhs=z_code[b, half][:].bitcast(FP8X4),
                     rhs_scale=z_scale[b, half][:],
-                    start=(b, e) == (0, 0),
-                    stop=(b, e) == (1, 1),
+                    start=(b, e) == (0, e0),
+                    stop=(b, e) == (1, e1 - 1),
                 )
 
         def gate(half, q):
@@ -333,12 +342,12 @@ def tile_list_grasp_pair_wrench_kernel(
             for e in range(2):
                 c = 2 * q + e
                 nc.scalar.activation(
-                    gates[half, q][:, e, :], acc["g", half, q][:, e, :], ACT.Sigmoid, bias=bs_sb[:, c : c + 1]
+                    gates[half, q][:, e, :], acc["g", half, q, e][:, 0, :], ACT.Sigmoid, bias=bs_sb[:, c : c + 1]
                 )
 
         def finish(half, q, e0=0, e1=2):
             result = gates[half, q][:, e0:e1, :]
-            nc.vector.tensor_tensor(result, acc["m", half, q][:, e0:e1, :], result, ALU.mult)
+            nc.vector.tensor_tensor(result, acc["m", half, q, e0][:, 0 : e1 - e0, :], result, ALU.mult)
             rows = slice(P * (2 * q + e0), P * (2 * q + e1))
             nc.sync.dma_start(
                 out=out[rows, HALF * half : HALF * (half + 1)].rearrange("(e p) j -> p e j", p=P), in_=result
@@ -354,21 +363,20 @@ def tile_list_grasp_pair_wrench_kernel(
         quantize_w1("01", round_pass(0, 1, both), [(0, 0, 1)])
         gather_words(1, cut, S, "plain_raw01")
         multiply_h(0, 0, 1, first_parts)
-        quantize_w1("1", round_plain(1, (nc.scalar, nc.gpsimd)), [(0, 1, 0), (0, 1, 1)])
-        empty_h(0, 0, first_parts, on_vector=cut)
+        quantize_w1("1", round_plain(1, (nc.gpsimd, nc.scalar)), [(0, 1, 0), (0, 1, 1)])
+        empty_h(0, 0, first_parts, "plain_raw11", -KIB, on_vector=cut)
         for a in range(PASSES):
             multiply_h(0, 1, a, sides(3, 4))
         empty_h(0, 1, sides(3, 4))
         rounded = round_plain(2, (nc.gpsimd, nc.gpsimd), "plain_bf1")
-        gather_plain(0, 0, "plain_raw11", -KIB)
-        gather_plain(0, 1, "plain_raw11", KIB)
+        gather_plain(0, 0)
+        gather_plain(0, 1)
         quantize_w1("2", rounded, [(0, 2, 0), (0, 2, 1)])
         plain_max(0, "plain_raw21")
         load_ws(1)
         for a in range(PASSES):
             multiply_h(0, 2, a, sides(5, 6))
-        dealt_first = sbuf("dealt_bf0", [P, PACK, P, PACK], BF16)
-        round_dealt_first(dealt_first, 0)
+        round_dealt_first(0)
         empty_h(0, 2, sides(5, 6), "dealt_raw00")
         rounded = round_plain(3, (nc.gpsimd, nc.gpsimd), "finger01")
         gather_plain(1, 0, "plain_bf2")
@@ -377,22 +385,21 @@ def tile_list_grasp_pair_wrench_kernel(
         plain_max(1, "plain_raw31")
         for a in range(PASSES):
             multiply_h(0, 3, a, sides(7, 0))
-        round_dealt_first(dealt_first, 1)
-        rounded = dealt_first[:].rearrange("p t m x -> p (t m x)")
+        round_dealt_first(1)
         gather_plain(2, 0, "plain_bf3")
         gather_plain(2, 1, "finger10")
-        quantize_w1("d0", rounded, [(1, t, 0) for t in range(PACK)])
+        quantize_dealt(0, 3)
         plain_max(2, "dealt_raw01", 3 * KIB)
+        round_dealt_last(0)
+        quantize_dealt(3, 6)
         for t in range(2):
-            multiply_h(1, t, 0, sides(2 * t + 1, 2 * t + 2))
-        quantize_w1("d10", round_dealt_last(0), [(1, 0, 1), (1, 1, 1)])
-        for t in range(2):
-            multiply_h(1, t, 1, sides(2 * t + 1, 2 * t + 2))
+            for a in range(PASSES):
+                multiply_h(1, t, a, sides(2 * t + 1, 2 * t + 2))
         empty_h(0, 3, sides(7, 0), "dealt_raw01", -KIB)
-        rounded = round_dealt_last(2)
+        round_dealt_last(2)
         gather_plain(3, 0)
         gather_plain(3, 1, trail=8 * KIB)
-        quantize_w1("d12", rounded, [(1, 2, 1), (1, 3, 1)])
+        quantize_dealt(6, 8)
         plain_max(3, "dealt_raw10")
         load_wm()
 
@@ -422,8 +429,8 @@ def tile_list_grasp_pair_wrench_kernel(
         quantize_z(woven[:, HALF:PAIRS, :], 0, 1, "bias_last1")
         ws_last = sbuf("ws_last", [P, N, PACK], BF16, "z_moved", 2 * KIB)
         z_bf = dealt_max(0)
-        round_rows(nc.scalar, ws_last[:, 0:WIDE, :], ws_raw[1][:, :, 0:WIDE])
-        quantize_ws(1, 0, WIDE, ws_last[:, 0:WIDE, :])
+        round_rows(nc.scalar, ws_last[:, 0:NARROW, :], ws_raw[1][:, :, 0:NARROW])
+        quantize_ws(1, 0, NARROW, ws_last[:, 0:NARROW, :])
         for q in range(COUPLES):
             multiply("g", 0, q, 0, q)
         for q in range(COUPLES):
@@ -431,13 +438,13 @@ def tile_list_grasp_pair_wrench_kernel(
         for q in range(COUPLES - 1):
             multiply("m", 1, q, 0, 2 * COUPLES + q)
         quantize_z(z_bf[:], 1, 0)
-        round_rows(nc.scalar, ws_last[:, WIDE:N, :], ws_raw[1][:, :, WIDE:N])
-        quantize_ws(1, WIDE, N, ws_last[:, WIDE:N, :])
+        round_rows(nc.scalar, ws_last[:, NARROW:N, :], ws_raw[1][:, :, NARROW:N])
+        quantize_ws(1, NARROW, N, ws_last[:, NARROW:N, :])
         for q in range(COUPLES):
             multiply("g", 0, q, 1)
             gate(0, q)
             multiply("m", 0, q, 1)
-        z_bf = dealt_max(1, "z_bf1_0")
+        z_bf = dealt_max(1, "ws_raw1")
         finish(0, 0, 0, 1)
         last = COUPLES - 1
         for q in range(last):
@@ -451,12 +458,13 @@ def tile_list_grasp_pair_wrench_kernel(
         multiply("m", 1, 0, 1)
         multiply("g", 1, 1, 1)
         gate(1, 1)
+        multiply("m", 1, 1, 1)
         multiply("g", 1, last, 0, last)
         multiply("g", 1, last, 1)
         gate(1, last)
-        multiply("m", 1, 1, 1)
-        multiply("m", 1, last, 0, COUPLES)
-        multiply("m", 1, last, 1)
+        for e, number in enumerate((COUPLES, 0)):
+            for b in range(PASSES):
+                multiply("m", 1, last, b, number, e, e + 1)
         for q in range(COUPLES):
             for e in range(2):
                 finish(1, q, e, e + 1)

import math
from contextlib import ExitStack

import concourse.mybir as mybir
from concourse.masks import make_identity

K, H, N, T, S, PAIRS = 1024, 1024, 768, 4096, 1024, 512
FLOPS = 2 * K * H * S + 2 * 2 * H * N * PAIRS

F32 = mybir.dt.float32
BF16 = mybir.dt.bfloat16
I32 = mybir.dt.int32
U32 = mybir.dt.uint32
U16 = mybir.dt.uint16
U8 = mybir.dt.uint8
FP8X4 = mybir.dt.float8_e4m3fn_x4
FP4X4 = mybir.dt.float4_e2m1fn_x4
ALU = mybir.AluOpType
ACT = mybir.ActivationFunctionType

P = 128
PACK = 4
PASS = P * PACK
PASSES = 2
BANK = 512
QUADS = 4
PER_COLUMN = 16
HALF = PAIRS // 2
COUPLES = N // (2 * P)
NARROW = 2 * P
ALIGN = 64
KIB = 1024


def tile_list_grasp_pair_wrench_kernel(
    tc, tab_words, tab_scales, offs, w1, b1, pos1, pos2, wm_words, wm_scales, ws, bs, out
):
    nc = tc.nc
    with ExitStack() as ctx:
        lists = ctx.enter_context(tc.tile_pool(name="lists", bufs=1))
        keep = ctx.enter_context(tc.tile_pool(name="keep", bufs=1))
        psum = ctx.enter_context(tc.psum_pool(name="psum", bufs=1))

        place = {"end": (0, 0, 0)}

        def sbuf(name, shape, dtype, over="", at=0, lead=0, trail=0):
            size = math.prod(shape[1:]) * (4 if dtype in (F32, I32, U32) else 2 if dtype == BF16 else 1)
            if over:
                first, low, high = place[over]
                first = first + at
                assert low <= first and first + size <= high
            else:
                low = place["end"][2]
                first = low + lead
                high = first + -(-size // ALIGN) * ALIGN + trail
                place["end"] = (high, high, high)
            place[name] = (first, low, high)
            return keep.tile(shape, dtype, name=name, bufs=1, align_bytes=ALIGN, offset=first)

        def bank(number, shape, name):
            return psum.tile(shape, F32, name=name, tag="bank%d" % number)

        offs_sb = lists.tile([P, S // PER_COLUMN], U16, name="offs_sb")
        pos1_sb = lists.tile([P, PAIRS // PER_COLUMN], U16, name="pos1_sb")
        pos2_sb = lists.tile([P, PAIRS // PER_COLUMN], U16, name="pos2_sb")

        scale_window = sbuf("scale_window", [P, T // 4], I32, trail=14 * KIB)
        v_scale = sbuf("v_scale", [P, PASSES, S], U8)
        scale_row = P - 32
        nc.vector.memset(scale_window[0:scale_row, :], 0)
        nc.vector.memset(v_scale[:].rearrange("p a s -> p (a s)").bitcast(I32), 0)

        nc.sync.dma_start(out=scale_window[scale_row:P, :], in_=tab_scales.bitcast(I32).rearrange("a g w -> g a w"))
        nc.sync.dma_start(offs_sb[:], offs)
        word_window = {}

        def load_words(a, over="", at=0):
            word_window[a] = sbuf("word_window%d" % a, [P, T], I32, over, at)
            nc.sync.dma_start(out=word_window[a][:], in_=tab_words[a].rearrange("p t x -> p (t x)").bitcast(I32))

        plain_raw = {}

        def load_plain(t, a, tiles=1, margin=0):
            raw = sbuf("plain_raw%d%d" % (t, a), [P, PACK, tiles * P], F32, lead=margin, trail=margin)
            nc.sync.dma_start(
                out=raw[:],
                in_=w1[PASS * a : PASS * (a + 1), P * t : P * (t + tiles)].rearrange("(p x) c -> p x c", x=PACK),
            )
            for i in range(tiles):
                plain_raw[t + i, a] = raw[:, :, P * i : P * (i + 1)]

        bias_rows = sbuf("bias_rows", [P, PASS], F32)
        identity = sbuf("identity", [P, P], F32)
        b1_row = P - PASSES
        nc.vector.memset(bias_rows[0:b1_row, :], 0.0)
        make_identity(nc, identity[:])
        load_words(0)
        load_plain(0, 0)
        nc.sync.dma_start(out=bias_rows[b1_row:P, :], in_=b1.rearrange("(b r) -> b r", b=PASSES))
        turned = [bank(6 + b, [P, PACK, P], "turned%d" % b) for b in range(PASSES)]
        for t in range(PACK):
            nc.tensor.transpose(turned[0][:, t, :], bias_rows[:, P * t : P * (t + 1)], identity[:])
        for t in range(PACK):
            nc.tensor.transpose(turned[1][:, t, :], bias_rows[:, t:PASS:PACK], identity[:])
        bias_of = {}
        for b in range(PASSES):
            columns = sbuf("bias_columns%d" % b, [P, PACK], F32)
            nc.scalar.copy(columns[:], turned[b][:, :, b1_row + b])
            for t in range(PACK):
                bias_of[b, t] = [columns[:, t : t + 1]] * 2
        bias_last = sbuf("bias_last1", [P, 1], F32, trail=KIB)
        nc.scalar.copy(bias_last[:], turned[1][:, PACK - 1, P - 1 : P])
        bias_of[1, PACK - 1] = [bias_of[1, PACK - 1][0], bias_last[:]]
        bs_sb = sbuf("bs_sb", [P, N // P], F32)

        dealt_raw = {}

        def load_dealt(a, piece, width, lead=0):
            dealt_raw[a, piece] = sbuf("dealt_raw%d%d" % (a, piece), [P, PACK, width], F32, lead=lead)
            c0 = PASS + width * piece
            nc.sync.dma_start(
                out=dealt_raw[a, piece][:],
                in_=w1[PASS * a : PASS * (a + 1), c0 : c0 + width].rearrange("(p x) c -> p x c", x=PACK),
            )

        ws_raw = []

        def load_ws(b):
            ws_raw.append(sbuf("ws_raw%d" % b, [P, PACK, N], F32))
            nc.sync.dma_start(
                out=ws_raw[b][:], in_=ws[PASS * b : PASS * (b + 1), :].rearrange("(p x) n -> p x n", x=PACK)
            )

        picked_scale = sbuf("picked_scale", [P, S], U8)
        nc.vector.tensor_copy(picked_scale[:], scale_window[:].bitcast(U8).indirect(offs_sb[:]))
        for quad in (0, 2, 1, 3):
            nc.sync.dma_start(
                out=v_scale[32 * quad : 32 * quad + 4, :, :].bitcast(I32),
                in_=picked_scale[scale_row + 8 * quad : scale_row + 8 * (quad + 1), :].bitcast(I32),
            )
        load_words(1, "scale_window", 2 * KIB)
        wm_scale = sbuf("wm_scale", [P, PASSES, N // 4], I32, "scale_window")
        nc.vector.memset(wm_scale[:], 0)
        load_plain(0, 1)
        load_plain(1, 0)
        load_plain(1, 1, margin=KIB)
        nc.sync.dma_start(pos1_sb[:], pos1)
        nc.sync.dma_start(pos2_sb[:], pos2)
        load_plain(2, 0, tiles=2)
        load_plain(2, 1)
        load_plain(3, 1)
        load_dealt(0, 0, PASS // 2)
        load_dealt(0, 1, PASS // 2, lead=KIB)
        load_dealt(1, 0, PASS)
        load_ws(0)
        wm_sb = sbuf("wm_sb", [P, PASSES, 2 * N], U8)

        def load_wm():
            nc.sync.dma_start(out=wm_sb[:].bitcast(I32), in_=wm_words.bitcast(I32).rearrange("b p w -> p b w"))
            for quad in range(QUADS):
                nc.sync.dma_start(
                    out=wm_scale[32 * quad : 32 * quad + 4, :, :],
                    in_=wm_scales[:, 4 * quad : 4 * quad + 4, :].bitcast(I32).rearrange("b row w -> row b w"),
                )
            with nc.allow_non_contiguous_dma(reason="one bias value for each partition and output tile"):
                nc.sync.dma_start(out=bs_sb[:], in_=bs.rearrange("(c p) -> p c", p=P))

        v_words = {}

        def gather_words(a, c0, c1, over=""):
            words = sbuf("v_words%d_%d" % (a, c0), [P, c1 - c0], U32, over)
            entries = slice(c0 // PER_COLUMN, c1 // PER_COLUMN)
            nc.vector.tensor_copy(words[:], word_window[a][:].bitcast(U32).indirect(offs_sb[:, entries]))
            v_words[a, c0] = words

        def words_of(a, c0, c1):
            runs = []
            for (b, first), words in v_words.items():
                low, high = max(c0, first), min(c1, first + words.shape[1])
                if b == a and low < high:
                    runs.append((low, high, words[:, low - first : high - first]))
            return runs

        def round_rows(engine, rounded, raw):
            if engine is nc.gpsimd:
                nc.gpsimd.tensor_scalar(rounded, raw.rearrange("p x c -> p c x"), 1.0, 0.0, ALU.mult, ALU.add)
            else:
                nc.scalar.copy(
                    rounded.rearrange("p (d u) x -> p d x u", u=4), raw.rearrange("p x (d u) -> p d x u", u=4)
                )

        def quantize(codes, scales, rounded):
            nc.vector.quantize_mx(out=codes.bitcast(FP8X4), scales=scales, in_=rounded)

        stationary = {}

        def quantize_w1(name, rounded, parts):
            codes = sbuf("code_" + name, [P, len(parts) * P], U32)
            scales = sbuf("scale_" + name, [P, len(parts) * P], U8)
            quantize(codes[:], scales[:], rounded)
            for i, part in enumerate(parts):
                stationary[part] = codes[:, P * i : P * (i + 1)], scales[:, P * i : P * (i + 1)]

        def round_pass(t, a, shares):
            rounded = sbuf("plain_bf%d%d" % (t, a), [P, P, PACK], BF16)
            for engine, c0, c1 in shares:
                round_rows(engine, rounded[:, c0:c1, :], plain_raw[t, a][:, :, c0:c1])
            return rounded[:].rearrange("p c x -> p (c x)")

        def round_plain(t, engines, over=""):
            rounded = sbuf("plain_bf%d" % t, [P, PASSES, P, PACK], BF16, over)
            for a in range(PASSES):
                round_rows(engines[a], rounded[:, a, :, :], plain_raw[t, a])
            return rounded[:].rearrange("p a c x -> p (a c x)")

        def deal(rounded, raw, t):
            nc.scalar.copy(
                rounded.rearrange("p t m x -> p m x t"),
                raw.rearrange("p x (m t) -> p m x t", t=PACK)[:, :, :, t : t + 2],
            )

        slots = [(1, t, a) for t, a in ((2, 0), (3, 0), (0, 0), (1, 0), (0, 1), (1, 1), (2, 1), (3, 1))]
        dealt_bf = sbuf("dealt_bf", [P, len(slots), P, PACK], BF16)

        def round_dealt_first(piece):
            for t in range(0, PACK, 2):
                slot = slots.index((1, t, 0))
                columns = slice(P // 2 * piece, P // 2 * (piece + 1))
                deal(dealt_bf[:, slot : slot + 2, columns, :], dealt_raw[0, piece][:], t)

        def round_dealt_last(t):
            slot = slots.index((1, t, 1))
            deal(dealt_bf[:, slot : slot + 2, :, :], dealt_raw[1, 0][:], t)

        def quantize_dealt(s0, s1):
            quantize_w1("d%d" % s0, dealt_bf[:, s0:s1, :, :].rearrange("p s m x -> p (s m x)"), slots[s0:s1])

        h, h_acc = {}, {}

        def multiply_h(b, t, a, parts):
            for number, c0, c1 in parts:
                if a == 0:
                    h_acc[b, t, c0] = bank(number, [P, c1 - c0], "h_acc%d%d_%d" % (b, t, c0))
                codes, scales = stationary[b, t, a]
                for low, high, words in words_of(a, c0, c1):
                    nc.tensor.matmul_mx(
                        out=h_acc[b, t, c0][:, low - c0 : high - c0],
                        lhsT=codes.bitcast(FP8X4),
                        lhsT_scale=scales,
                        rhs=words.bitcast(FP8X4),
                        rhs_scale=v_scale[:, a, low:high],
                        start=(a == 0),
                        stop=(a == PASSES - 1 and high == c1),
                    )

        def empty_h(b, t, parts, over="", at=0, on_vector=-1):
            h[b, t] = sbuf("h%d%d" % (b, t), [P, S], F32, over, at)
            for number, c0, c1 in parts:
                bias = bias_of[b, t][c0 // BANK]
                if c0 == on_vector:
                    nc.vector.tensor_scalar(h[b, t][:, c0:c1], h_acc[b, t, c0][:], bias, None, ALU.add)
                else:
                    nc.scalar.activation(h[b, t][:, c0:c1], h_acc[b, t, c0][:], ACT.Identity, bias=bias)

        def sides(first, second):
            return ((first, 0, BANK), (second, BANK, S))

        z_code, z_scale = {}, {}
        dealt_fingers = [sbuf("dealt_finger%d" % f, [P, PACK, PAIRS], F32) for f in range(2)]
        plain_fingers = {}

        def gather(picked, b, t, f):
            nc.vector.tensor_copy(picked, h[b, t][:].indirect((pos1_sb, pos2_sb)[f][:]))

        def gather_plain(t, f, over="", at=0, trail=0):
            plain_fingers[t, f] = sbuf("finger%d%d" % (t, f), [P, PAIRS], F32, over, at, trail=trail)
            gather(plain_fingers[t, f][:], 0, t, f)

        def gather_dealt(t):
            for f in range(2):
                gather(dealt_fingers[f][:, t, :], 1, t, f)

        def dealt_max(half, over=""):
            z_bf = sbuf("z_bf1_%d" % half, [P, HALF, PACK], BF16, over)
            j = slice(HALF * half, HALF * (half + 1))
            nc.vector.tensor_tensor(
                z_bf[:].rearrange("p (d u) t -> p d t u", u=2),
                dealt_fingers[0][:, :, j].rearrange("p t (d u) -> p d t u", u=2),
                dealt_fingers[1][:, :, j].rearrange("p t (d u) -> p d t u", u=2),
                ALU.max,
            )
            return z_bf

        z_moved = sbuf("z_moved", [P, PACK, PAIRS], BF16, lead=2 * KIB, trail=4 * KIB)

        def plain_max(t, over, at=0):
            z_plain = sbuf("z_plain%d" % t, [P, PAIRS], BF16, over, at)
            nc.vector.tensor_tensor(z_plain[:], plain_fingers[t, 0][:], plain_fingers[t, 1][:], ALU.max)
            for x in range(PACK):
                nc.sync.dma_start(out=z_moved[32 * t : 32 * (t + 1), x, :], in_=z_plain[x:P:PACK, :])

        def quantize_z(z_bf, b, half, over=""):
            z_code[b, half] = sbuf("z_code%d%d" % (b, half), [P, HALF], U32, over)
            z_scale[b, half] = sbuf("z_scale%d%d" % (b, half), [P, HALF], U8)
            quantize(z_code[b, half][:], z_scale[b, half][:], z_bf.rearrange("p j x -> p (j x)"))

        ws_q = {}

        def quantize_ws(b, n0, n1, rounded):
            codes = sbuf("ws_code%d_%d" % (b, n0), [P, n1 - n0], U32)
            scales = sbuf("ws_scale%d_%d" % (b, n0), [P, n1 - n0], U8)
            quantize(codes[:], scales[:], rounded.rearrange("p n x -> p (n x)"))
            for c in range(n0 // P, n1 // P):
                ws_q[b, c] = codes[:, P * c - n0 : P * (c + 1) - n0], scales[:, P * c - n0 : P * (c + 1) - n0]

        acc, gates = {}, {}

        def multiply(kind, half, q, b, number=None, e0=0, e1=2):
            if b == 0:
                sums = bank(number, [P, e1 - e0, HALF], "%s_acc%d%d%d" % (kind, half, q, e0))
                for e in range(e0, e1):
                    acc[kind, half, q, e] = sums[:, e - e0 : e1 - e0, :]
            for e in range(e0, e1):
                c = 2 * q + e
                if kind == "g":
                    codes, scales = ws_q[b, c][0].bitcast(FP8X4), ws_q[b, c][1]
                else:
                    codes = wm_sb[:, b, 2 * P * c : 2 * P * (c + 1)].bitcast(FP4X4)
                    scales = wm_scale[:, b, P // 4 * c : P // 4 * (c + 1)].bitcast(U8)
                nc.tensor.matmul_mx(
                    out=acc[kind, half, q, e][:, 0, :],
                    lhsT=codes,
                    lhsT_scale=scales,
                    rhs=z_code[b, half][:].bitcast(FP8X4),
                    rhs_scale=z_scale[b, half][:],
                    start=(b, e) == (0, e0),
                    stop=(b, e) == (1, e1 - 1),
                )

        def gate(half, q):
            gates[half, q] = sbuf("gate%d%d" % (half, q), [P, 2, HALF], F32, "h%d%d" % (half, q))
            for e in range(2):
                c = 2 * q + e
                nc.scalar.activation(
                    gates[half, q][:, e, :], acc["g", half, q, e][:, 0, :], ACT.Sigmoid, bias=bs_sb[:, c : c + 1]
                )

        def finish(half, q, e0=0, e1=2):
            result = gates[half, q][:, e0:e1, :]
            nc.vector.tensor_tensor(result, acc["m", half, q, e0][:, 0 : e1 - e0, :], result, ALU.mult)
            rows = slice(P * (2 * q + e0), P * (2 * q + e1))
            nc.sync.dma_start(
                out=out[rows, HALF * half : HALF * (half + 1)].rearrange("(e p) j -> p e j", p=P), in_=result
            )

        both = ((nc.scalar, 0, P // 2), (nc.gpsimd, P // 2, P))
        cut = BANK + BANK // 2
        first_parts = ((0, 0, BANK), (1, BANK, cut), (2, cut, S))
        gather_words(0, 0, S)
        quantize_w1("00", round_pass(0, 0, both), [(0, 0, 0)])
        multiply_h(0, 0, 0, first_parts)
        gather_words(1, 0, cut)
        quantize_w1("01", round_pass(0, 1, both), [(0, 0, 1)])
        gather_words(1, cut, S, "plain_raw01")
        multiply_h(0, 0, 1, first_parts)
        quantize_w1("1", round_plain(1, (nc.gpsimd, nc.scalar)), [(0, 1, 0), (0, 1, 1)])
        empty_h(0, 0, first_parts, "plain_raw11", -KIB, on_vector=cut)
        for a in range(PASSES):
            multiply_h(0, 1, a, sides(3, 4))
        empty_h(0, 1, sides(3, 4))
        rounded = round_plain(2, (nc.gpsimd, nc.gpsimd), "plain_bf1")
        gather_plain(0, 0)
        gather_plain(0, 1)
        quantize_w1("2", rounded, [(0, 2, 0), (0, 2, 1)])
        plain_max(0, "plain_raw21")
        load_ws(1)
        for a in range(PASSES):
            multiply_h(0, 2, a, sides(5, 6))
        round_dealt_first(0)
        empty_h(0, 2, sides(5, 6), "dealt_raw00")
        rounded = round_plain(3, (nc.gpsimd, nc.gpsimd), "finger01")
        gather_plain(1, 0, "plain_bf2")
        gather_plain(1, 1, "finger00")
        quantize_w1("3", rounded, [(0, 3, 0), (0, 3, 1)])
        plain_max(1, "plain_raw31")
        for a in range(PASSES):
            multiply_h(0, 3, a, sides(7, 0))
        round_dealt_first(1)
        gather_plain(2, 0, "plain_bf3")
        gather_plain(2, 1, "finger10")
        quantize_dealt(0, 3)
        plain_max(2, "dealt_raw01", 3 * KIB)
        round_dealt_last(0)
        quantize_dealt(3, 6)
        for t in range(2):
            for a in range(PASSES):
                multiply_h(1, t, a, sides(2 * t + 1, 2 * t + 2))
        empty_h(0, 3, sides(7, 0), "dealt_raw01", -KIB)
        round_dealt_last(2)
        gather_plain(3, 0)
        gather_plain(3, 1, trail=8 * KIB)
        quantize_dealt(6, 8)
        plain_max(3, "dealt_raw10")
        load_wm()

        joined = sbuf("joined", [P, N + PAIRS, PACK], BF16, "finger31")
        round_rows(nc.gpsimd, joined[:, 0:N, :], ws_raw[0][:])
        for t in range(2):
            empty_h(1, t, sides(2 * t + 1, 2 * t + 2))
        for t, banks in ((2, sides(7, 0)), (3, sides(1, 2))):
            for a in range(PASSES):
                multiply_h(1, t, a, banks)
        gather_dealt(0)
        gather_dealt(1)
        rest = N
        empty_h(1, 2, sides(7, 0))
        gather_dealt(2)
        woven = joined[:, rest:, :]
        round_rows(nc.scalar, woven, z_moved[:])
        codes = sbuf("joined_code", [P, rest + HALF], U32)
        scales = sbuf("joined_scale", [P, rest + HALF], U8)
        quantize(codes[:], scales[:], joined[:, 0 : rest + HALF, :].rearrange("p c x -> p (c x)"))
        for e in range(rest // P):
            ws_q[0, e] = codes[:, P * e : P * (e + 1)], scales[:, P * e : P * (e + 1)]
        z_code[0, 0], z_scale[0, 0] = codes[:, rest:], scales[:, rest:]
        empty_h(1, 3, sides(1, 2), "z_moved", -2 * KIB)
        gather_dealt(3)

        quantize_z(woven[:, HALF:PAIRS, :], 0, 1, "bias_last1")
        ws_last = sbuf("ws_last", [P, N, PACK], BF16, "z_moved", 2 * KIB)
        z_bf = dealt_max(0)
        round_rows(nc.scalar, ws_last[:, 0:NARROW, :], ws_raw[1][:, :, 0:NARROW])
        quantize_ws(1, 0, NARROW, ws_last[:, 0:NARROW, :])
        for q in range(COUPLES):
            multiply("g", 0, q, 0, q)
        for q in range(COUPLES):
            multiply("m", 0, q, 0, COUPLES + q)
        for q in range(COUPLES - 1):
            multiply("m", 1, q, 0, 2 * COUPLES + q)
        quantize_z(z_bf[:], 1, 0)
        round_rows(nc.scalar, ws_last[:, NARROW:N, :], ws_raw[1][:, :, NARROW:N])
        quantize_ws(1, NARROW, N, ws_last[:, NARROW:N, :])
        for q in range(COUPLES):
            multiply("g", 0, q, 1)
            gate(0, q)
            multiply("m", 0, q, 1)
        z_bf = dealt_max(1, "ws_raw1")
        finish(0, 0, 0, 1)
        last = COUPLES - 1
        for q in range(last):
            multiply("g", 1, q, 0, q)
        quantize_z(z_bf[:], 1, 1)
        finish(0, 0, 1, 2)
        for q in range(1, COUPLES):
            finish(0, q)
        multiply("g", 1, 0, 1)
        gate(1, 0)
        multiply("m", 1, 0, 1)
        multiply("g", 1, 1, 1)
        gate(1, 1)
        multiply("m", 1, 1, 1)
        multiply("g", 1, last, 0, last)
        multiply("g", 1, last, 1)
        gate(1, last)
        for e, number in enumerate((COUPLES, 0)):
            for b in range(PASSES):
                multiply("m", 1, last, b, number, e, e + 1)
        for q in range(COUPLES):
            for e in range(2):
                finish(1, q, e, e + 1)
